import numpy as np
import ml_dtypes


def mxq(x, axis, fmt="e4m3"):
    dtype, down = {"e4m3": (ml_dtypes.float8_e4m3fn, 7), "e5m2": (ml_dtypes.float8_e5m2, 14)}[fmt]
    v = np.moveaxis(np.asarray(x, np.float32).astype(ml_dtypes.bfloat16).astype(np.float64), axis, -1)
    blocks = v.reshape(v.shape[:-1] + (-1, 32))
    amax = np.abs(blocks).max(-1, keepdims=True)
    byte = np.maximum(np.where(amax > 0, np.frexp(amax)[1] - 1 + 127, 0) - down, 1)
    scale = np.exp2(byte - 127.0)
    codes = (blocks / scale).astype(np.float32).astype(dtype).astype(np.float64)
    return np.moveaxis((codes * scale).reshape(v.shape), -1, axis)


WIDE = False


def mx_kscale(k):
    if not WIDE:
        return np.ones(k)
    levels = np.array([10, -10, 5, -5, 0])
    if k % 512:
        return np.exp2(np.random.permutation(np.resize(levels, k // 32))).repeat(32)
    a = np.empty((k // 512, 16))
    for p in range(k // 512):
        a[p, :8] = np.random.permutation(np.resize(levels, 8))
        for g in range(8):
            far = levels[np.abs(levels - a[p, g]) >= 10]
            a[p, g + 8] = far[np.random.randint(len(far))]
    return np.exp2(a.ravel()).repeat(32)


BF16 = ml_dtypes.bfloat16


def bf(x):
    return np.asarray(x, np.float32).astype(BF16)


def f64(x):
    return np.asarray(x).astype(np.float64)


M, K, N, R = 2048, 1024, 1024, 1024
OMEGA1, OMEGA2 = 1.5, 2.0


def draw0():
    s, u = mx_kscale(K), mx_kscale(M)
    return {"x": bf(np.random.standard_normal((M, K)) * s),
            "w": bf(np.random.standard_normal((K, N)) / np.sqrt(K) / s[:, None]),
            "b": bf(0.3 * np.random.standard_normal(N)),
            "freq1": bf(OMEGA1 * (1 + 0.1 * np.random.standard_normal(N))),
            "amp": bf(np.exp(0.3 * np.random.standard_normal(M)) * u),
            "p": bf(np.random.standard_normal((R, M)) / np.sqrt(M) / u),
            "c": bf(0.3 * np.random.standard_normal(N)),
            "freq2": bf(OMEGA2 * (1 + 0.1 * np.random.standard_normal(N)))}


def core(x, w, b, freq1, amp, p, c, freq2):
    y = mxq(f64(x), 1, "e4m3") @ mxq(f64(w), 0, "e4m3")
    h = f64(amp)[:, None] * np.sin(f64(freq1) * (y + f64(b)))
    z = mxq(f64(p), 1, "e4m3") @ mxq(h, 0, "e4m3")
    return np.sin(f64(freq2) * (z + f64(c)))


def e4m3fn_bytes(y):
    return np.clip(np.asarray(y, np.float64), -448.0, 448.0).astype(np.float32).astype(ml_dtypes.float8_e4m3fn).view(np.uint8)


def e4m3fn_values(b):
    return np.asarray(b, np.uint8).view(ml_dtypes.float8_e4m3fn).astype(np.float64)


def setup_inputs():
    d = draw0()
    x0 = np.asarray(d['x']).astype(np.float64)
    s = (np.max(np.abs(x0), axis=(0,), keepdims=True) / 448.0).astype(np.float32)
    out = {}
    for k, v in d.items():
        if k == 'x':
            out['x_bytes'] = e4m3fn_bytes(x0 / s.astype(np.float64))
            out['x_scale'] = s
        else:
            out[k] = v
    return out


def reference(x_bytes, x_scale, w, b, freq1, amp, p, c, freq2):
    return core(e4m3fn_values(x_bytes) * x_scale.astype(np.float64), w, b, freq1, amp, p, c, freq2)

@@ -1,0 +1,282 @@
+from contextlib import ExitStack
+import math
+
+import concourse.mybir as mybir
+from concourse.masks import make_identity
+
+M, K, N, R = 2048, 1024, 1024, 1024
+FLOPS = 2 * M * K * N + 2 * R * M * N
+
+F32 = mybir.dt.float32
+BF16 = mybir.dt.bfloat16
+I32 = mybir.dt.int32
+U32 = mybir.dt.uint32
+U8 = mybir.dt.uint8
+FP8 = mybir.dt.float8_e4m3fn
+FP8X4 = mybir.dt.float8_e4m3fn_x4
+ACT = mybir.ActivationFunctionType
+OP = mybir.AluOpType
+
+P = 128
+PACK = 4
+TWO_PI = 2.0 * math.pi
+GROUP0 = 4
+
+
+def tile_siren_anchor_field_f4_kernel(tc, x_bytes, x_scale, w, b, freq1, amp, p, c, freq2, out):
+    nc = tc.nc
+    with ExitStack() as ctx:
+        keep = ctx.enter_context(tc.tile_pool(name="keep", bufs=1))
+        stage = ctx.enter_context(tc.tile_pool(name="stage", bufs=2))
+        psum = ctx.enter_context(tc.psum_pool(name="psum", bufs=2))
+
+        x_view = x_bytes.rearrange("(j q t) k -> j q t k", q=P, t=PACK)
+        xb = []
+        for j in range(4):
+            xb.append(keep.tile([P, PACK, K], U8, name=f"xb{j}", align_bytes=64))
+        nc.sync.dma_start(out=xb[0][:], in_=x_view[0])
+        xs_sc = keep.tile([P, K], F32, name="xs_sc")
+        nc.scalar.dma_start(out=xs_sc[:], in_=x_scale.rearrange("o k -> (o k)").partition_broadcast(P))
+        vrows = keep.tile([P, P], BF16, name="vrows")
+        nc.vector.memset(vrows[:], 0.0)
+        w_view = w.rearrange("(g q t) n -> g q t n", q=P, t=PACK)
+        wraw = []
+        for g in range(2):
+            wraw.append(keep.tile([P, PACK, N], BF16, name=f"wraw{g}", align_bytes=64))
+        nc.sync.dma_start(out=wraw[0][:], in_=w_view[0])
+        nc.sync.dma_start(out=wraw[1][:], in_=w_view[1])
+        for q, vec in enumerate((freq1, b, freq2, c)):
+            nc.sync.dma_start(out=vrows[8 * q : 8 * q + 8, :], in_=vec.rearrange("(i q) -> i q", q=P))
+        amp_sb = keep.tile([P, 4, PACK], BF16, name="amp_sb")
+        nc.sync.dma_start(out=amp_sb[:], in_=amp.rearrange("(j q t) -> q j t", q=P, t=PACK))
+        for j in range(1, 4):
+            nc.sync.dma_start(out=xb[j][:], in_=x_view[j])
+        praw = []
+        for rt in range(8):
+            praw.append(keep.tile([P, M], BF16, name=f"praw{rt}", align_bytes=64))
+            nc.sync.dma_start(out=praw[rt][:], in_=p[rt * P : (rt + 1) * P, :])
+
+        warm = keep.tile([P, 1], F32, name="warm")
+        nc.vector.memset(warm[:], 0.0)
+        nc.scalar.activation(out=warm[:], in_=warm[:], func=ACT.Sin)
+        ident_b = keep.tile([P, P], BF16, name="ident_b")
+        make_identity(nc, ident_b[:])
+        ident_f = keep.tile([P, P], F32, name="ident_f")
+        make_identity(nc, ident_f[:])
+
+        vt = psum.tile([P, P], BF16, name="vt", tag="tx", bufs=3)
+        nc.tensor.transpose(vt[:], vrows[:], ident_b[:])
+        f1 = keep.tile([P, 8], F32, name="f1")
+        fb1 = keep.tile([P, 8], F32, name="fb1")
+        b1 = keep.tile([P, 8], F32, name="b1")
+        f2 = keep.tile([P, 8], F32, name="f2")
+        b2 = keep.tile([P, 8], F32, name="b2")
+        vs = keep.tile([P, 32], F32, name="vs")
+        nc.vector.tensor_copy(out=vs[:], in_=vt[:, 0:32])
+        nc.vector.tensor_scalar(f1[:], vs[:, 0:8], 1.0 / TWO_PI, None, OP.mult)
+        nc.vector.tensor_tensor(fb1[:], vs[:, 0:8], vs[:, 8:16], OP.mult)
+        nc.vector.tensor_scalar(b1[:], fb1[:], 1.0 / TWO_PI, None, OP.mult)
+        nc.vector.tensor_scalar(f2[:], vs[:, 16:24], 1.0 / TWO_PI, None, OP.mult)
+        nc.vector.tensor_tensor(b2[:], f2[:], vs[:, 24:32], OP.mult)
+
+        xq = keep.tile([P, 4, 2, 512], U32, name="xq", align_bytes=64)
+        xqs = keep.tile([P, 4, 2, 512], U8, name="xqs", align_bytes=64)
+        wq = keep.tile([P, 2, N], U32, name="wq", align_bytes=64)
+        wqs = keep.tile([P, 2, N], U8, name="wqs", align_bytes=64)
+        pq = keep.tile([P, 4, R], U32, name="pq", align_bytes=64)
+        pqs = keep.tile([P, 4, R], U8, name="pqs", align_bytes=64)
+        hq = keep.tile([P, 4, N], U32, name="hq", align_bytes=64)
+        hqs = keep.tile([P, 4, N], U8, name="hqs", align_bytes=64)
+
+        def w_prep(q):
+            cols = slice(256 * q, 256 * q + 256)
+            for g in range(2):
+                wi = stage.tile([P, 256, PACK], BF16, name="wi", align_bytes=64, bufs=2)
+                nc.scalar.copy(out=wi[:], in_=wraw[g][:, :, cols].rearrange("q t n -> q n t"))
+                nc.vector.quantize_mx(
+                    out=wq[:, g, cols].bitcast(FP8X4),
+                    scales=wqs[:, g, cols],
+                    in_=wi[:].rearrange("q n t -> q (n t)"),
+                )
+
+        xs = {}
+        xi = {}
+
+        def x_mult(j, t):
+            if t == 0:
+                xs[j] = stage.tile([P, PACK, K], BF16, name="xs", align_bytes=64, bufs=2)
+            nc.vector.tensor_tensor(xs[j][:, t, :], xb[j][:, t, :].bitcast(FP8), xs_sc[:], OP.mult)
+
+        def x_turn(j, t):
+            if t == 0:
+                xi[j] = stage.tile([P, 2, 512, PACK], BF16, name="xi", align_bytes=64, bufs=2)
+            bank = psum.tile([P, 2, 2, P], F32, name="bank", tag="tx", bufs=3)
+            words = xs[j][:, t, :].bitcast(F32)
+            for g in range(2):
+                for u in range(2):
+                    nc.tensor.transpose(bank[:, g, u, :], words[:, 256 * g + u : 256 * (g + 1) : 2], ident_f[:])
+            dst = xi[j][:].bitcast(F32)[:, :, t * P : (t + 1) * P, :]
+            nc.scalar.copy(out=dst, in_=bank[:].rearrange("q g u r -> q g r u"))
+
+        def x_quant(j, g):
+            nc.vector.quantize_mx(
+                out=xq[:, j, g, :].bitcast(FP8X4),
+                scales=xqs[:, j, g, :],
+                in_=xi[j][:, g].rearrange("q m t -> q (m t)"),
+            )
+
+        pi = {}
+
+        def p_turn(half, jp, rr):
+            if rr == 0:
+                pi[half, jp] = stage.tile([P, 2, 512, PACK], BF16, name="pi", align_bytes=64, bufs=2)
+            bank = psum.tile([P, 2, 2, P], F32, name="bank", tag="tx", bufs=3)
+            words = praw[4 * half + rr][:].bitcast(F32)
+            for jj in range(2):
+                j = 2 * jp + jj
+                for u in range(2):
+                    nc.tensor.transpose(bank[:, jj, u, :], words[:, 256 * j + u : 256 * (j + 1) : 2], ident_f[:])
+            dst = pi[half, jp][:].bitcast(F32)[:, :, rr * P : (rr + 1) * P, :]
+            nc.scalar.copy(out=dst, in_=bank[:].rearrange("q g u r -> q g r u"))
+            if rr == 3:
+                for jj in range(2):
+                    j = 2 * jp + jj
+                    nc.vector.quantize_mx(
+                        out=pq[:, j, half * 512 : half * 512 + 512].bitcast(FP8X4),
+                        scales=pqs[:, j, half * 512 : half * 512 + 512],
+                        in_=pi[half, jp][:, jj].rearrange("q m t -> q (m t)"),
+                    )
+
+        st = {}
+
+        def u_mm(i, j):
+            y = psum.tile([P, 512], F32, name="y", tag="y", bufs=2)
+            ncols = slice(P * i, P * i + P)
+            for g in range(2):
+                nc.tensor.matmul_mx(
+                    out=y[:],
+                    lhsT=wq[:, g, ncols].bitcast(FP8X4),
+                    lhsT_scale=wqs[:, g, ncols],
+                    rhs=xq[:, j, g, :].bitcast(FP8X4),
+                    rhs_scale=xqs[:, j, g, :],
+                    start=(g == 0),
+                    stop=(g == 1),
+                )
+            turns = stage.tile([P, 512], F32, name="turns", bufs=2)
+            nc.scalar.activation(out=turns[:], in_=y[:], func=ACT.Identity, scale=f1[:, i : i + 1], bias=b1[:, i : i + 1])
+            k = stage.tile([P, 512], I32, name="k", bufs=3)
+            nc.gpsimd.tensor_scalar(k[:], turns[:], 1.0, 0.0, OP.mult, OP.add)
+            st[i, j] = (y, k)
+
+        def u_sin(i, j):
+            y, k = st[i, j]
+            r = stage.tile([P, 512], F32, name="r", bufs=2)
+            nc.vector.scalar_tensor_tensor(r[:], y[:], f1[:, i : i + 1], k[:], OP.mult, OP.subtract)
+            s = stage.tile([P, 512], F32, name="s", bufs=3)
+            nc.scalar.activation(out=s[:], in_=r[:], func=ACT.Sin, scale=TWO_PI, bias=fb1[:, i : i + 1])
+            st[i, j] = s
+
+        hi = {}
+
+        def u_turn(i, j):
+            s = st[i, j]
+            th = psum.tile([P, PACK, P], F32, name="th", tag="th", bufs=1)
+            for t in range(PACK):
+                nc.tensor.transpose(th[:, t, :], s[:, t * P : (t + 1) * P], ident_f[:])
+            hi[i, j] = stage.tile([P, P, PACK], BF16, name="hi", align_bytes=64, bufs=3)
+            nc.vector.tensor_tensor(
+                hi[i, j][:],
+                th[:].rearrange("q t n -> q n t"),
+                amp_sb[:, j, :].unsqueeze(1).to_broadcast([P, P, PACK]),
+                OP.mult,
+            )
+
+        def u_quant(i, j):
+            ncols = slice(P * i, P * i + P)
+            nc.vector.quantize_mx(
+                out=hq[:, j, ncols].bitcast(FP8X4),
+                scales=hqs[:, j, ncols],
+                in_=hi[i, j][:].rearrange("q n t -> q (n t)"),
+            )
+
+        zs = {}
+
+        def z_mm(i, half):
+            z = psum.tile([P, 512], F32, name="z", tag="z", bufs=2)
+            ncols = slice(P * i, P * i + P)
+            rcols = slice(512 * half, 512 * half + 512)
+            for j in range(4):
+                nc.tensor.matmul_mx(
+                    out=z[:],
+                    lhsT=hq[:, j, ncols].bitcast(FP8X4),
+                    lhsT_scale=hqs[:, j, ncols],
+                    rhs=pq[:, j, rcols].bitcast(FP8X4),
+                    rhs_scale=pqs[:, j, rcols],
+                    start=(j == 0),
+                    stop=(j == 3),
+                )
+            zs[i, half] = z
+
+        def z_red(i, half):
+            turns2 = stage.tile([P, 512], F32, name="turns2", bufs=2)
+            nc.scalar.activation(out=turns2[:], in_=zs[i, half][:], func=ACT.Identity, scale=f2[:, i : i + 1], bias=b2[:, i : i + 1])
+            k2 = stage.tile([P, 512], I32, name="k2", bufs=2)
+            nc.vector.tensor_copy(out=k2[:], in_=turns2[:])
+            r2 = stage.tile([P, 512], F32, name="r2", bufs=2)
+            nc.vector.tensor_tensor(r2[:], turns2[:], k2[:], OP.subtract)
+            zs[i, half] = r2
+
+        def z_out(i, half):
+            r2 = zs[i, half]
+            ob = psum.tile([P, PACK, P], F32, name="ob", tag="tx", bufs=3)
+            for q in range(4):
+                nc.tensor.transpose(ob[:, q, :], r2[:, q * P : (q + 1) * P], ident_f[:])
+            o = stage.tile([P, PACK, P], F32, name="o", bufs=3)
+            nc.scalar.activation(out=o[:], in_=ob[:], func=ACT.Sin, scale=TWO_PI)
+            nc.sync.dma_start(
+                out=out[512 * half : 512 * half + 512, P * i : P * i + P].rearrange("(a q) n -> q a n", q=P),
+                in_=o[:],
+            )
+
+        units = [(i, j) for j in range(4) for i in range(GROUP0)] + [(i, j) for i in range(GROUP0, 8) for j in range(4)]
+        z_tasks = [(i, h) for i in range(8) for h in range(2)]
+        p_tasks = [(h, jp, rr) for h in range(2) for jp in range(2) for rr in range(4)]
+        at = {u: s for s, u in enumerate(units)}
+
+        for q in range(4):
+            w_prep(q)
+        for t in range(4):
+            x_mult(0, t)
+            x_turn(0, t)
+        x_quant(0, 0)
+        x_quant(0, 1)
+
+        z_next = 0
+        z_log = {}
+        s = 0
+        while s < len(units) + 4 or z_next < len(z_tasks) or (s - 1) in z_log or (s - 2) in z_log:
+            if 0 <= s - 1 < 32:
+                u_sin(*units[s - 1])
+            if 0 <= s - 2 < 32:
+                u_turn(*units[s - 2])
+            if s - 2 in z_log:
+                z_out(*z_log[s - 2])
+            if s < 16 and s // 4 + 1 < 4:
+                x_mult(s // 4 + 1, s % 4)
+                x_turn(s // 4 + 1, s % 4)
+                if s % 4 == 3:
+                    x_quant(s // 4 + 1, 0)
+                    x_quant(s // 4 + 1, 1)
+            if 2 <= s < 18:
+                p_turn(*p_tasks[s - 2])
+            if 0 <= s - 3 < 32:
+                u_quant(*units[s - 3])
+            if s - 1 in z_log:
+                z_red(*z_log[s - 1])
+            if s < 32:
+                u_mm(*units[s])
+            if z_next < 16 and s >= 18 and at[z_tasks[z_next][0], 3] + 4 <= s:
+                z_log[s] = z_tasks[z_next]
+                z_mm(*z_log[s])
+                z_next += 1
+            s += 1

@@ -28,255 +28,313 @@ def tile_siren_anchor_field_f4_kernel(tc, x_bytes, x_scale, w, b, freq1, amp, p,
     with ExitStack() as ctx:
         keep = ctx.enter_context(tc.tile_pool(name="keep", bufs=1))
         stage = ctx.enter_context(tc.tile_pool(name="stage", bufs=2))
-        psum = ctx.enter_context(tc.psum_pool(name="psum", bufs=2))
+        psum = ctx.enter_context(tc.psum_pool(name="psum", bufs=1))
+        ctx.enter_context(tc.manual_schedule())
 
+        xs_col = keep.tile([P, 2, PACK], F32, name="xs_col")
+        nc.sync.dma_start(out=xs_col[:], in_=x_scale.rearrange("o (g q t) -> q (o g) t", q=P, t=PACK))
         x_view = x_bytes.rearrange("(j q t) k -> j q t k", q=P, t=PACK)
-        xb = []
-        for j in range(4):
-            xb.append(keep.tile([P, PACK, K], U8, name=f"xb{j}", align_bytes=64))
-        nc.sync.dma_start(out=xb[0][:], in_=x_view[0])
-        xs_sc = keep.tile([P, K], F32, name="xs_sc")
-        nc.scalar.dma_start(out=xs_sc[:], in_=x_scale.rearrange("o k -> (o k)").partition_broadcast(P))
-        vrows = keep.tile([P, P], BF16, name="vrows")
-        nc.vector.memset(vrows[:], 0.0)
         w_view = w.rearrange("(g q t) n -> g q t n", q=P, t=PACK)
-        wraw = []
-        for g in range(2):
-            wraw.append(keep.tile([P, PACK, N], BF16, name=f"wraw{g}", align_bytes=64))
-        nc.sync.dma_start(out=wraw[0][:], in_=w_view[0])
-        nc.sync.dma_start(out=wraw[1][:], in_=w_view[1])
-        for q, vec in enumerate((freq1, b, freq2, c)):
-            nc.sync.dma_start(out=vrows[8 * q : 8 * q + 8, :], in_=vec.rearrange("(i q) -> i q", q=P))
+        xb, wraw, praw = {}, {}, {}
+
+        def load_x(j):
+            for hf in range(2):
+                xb[j, hf] = keep.tile([P, 2, K], U8, name=f"xb{j}_{hf}", align_bytes=64)
+                nc.sync.dma_start(out=xb[j, hf][:], in_=x_view[j][:, 2 * hf : 2 * hf + 2, :])
+
+        def load_w(q):
+            for g in range(2):
+                wraw[q, g] = keep.tile([P, PACK, 256], BF16, name=f"wraw{q}_{g}", align_bytes=64)
+                nc.sync.dma_start(out=wraw[q, g][:], in_=w_view[g][:, :, 256 * q : 256 * q + 256])
+
+        def load_p(half):
+            for rt in range(4 * half, 4 * half + 4):
+                praw[rt] = keep.tile([P, M], BF16, name=f"praw{rt}", align_bytes=64)
+                nc.sync.dma_start(out=praw[rt][:], in_=p[rt * P : (rt + 1) * P, :])
+
+        load_x(0)
+        load_w(0)
+        load_x(1)
+        load_w(1)
+        load_p(0)
+        load_x(2)
+        load_x(3)
+        load_p(1)
+        load_w(2)
+        load_w(3)
+
+        ident = keep.tile([P, P], F32, name="ident")
+        make_identity(nc, ident[:])
+        vrows = keep.tile([P, 2, P], BF16, name="vrows")
+        nc.gpsimd.memset(vrows[:], 0.0)
+        for layer, (fr, bias) in enumerate(((freq1, b), (freq2, c))):
+            nc.gpsimd.dma_start(out=vrows[8 * layer : 8 * layer + 8, 0, :], in_=fr.rearrange("(i q) -> i q", q=P))
+            nc.gpsimd.dma_start(out=vrows[8 * layer : 8 * layer + 8, 1, :], in_=bias.rearrange("(i q) -> i q", q=P))
         amp_sb = keep.tile([P, 4, PACK], BF16, name="amp_sb")
-        nc.sync.dma_start(out=amp_sb[:], in_=amp.rearrange("(j q t) -> q j t", q=P, t=PACK))
-        for j in range(1, 4):
-            nc.sync.dma_start(out=xb[j][:], in_=x_view[j])
-        praw = []
-        for rt in range(8):
-            praw.append(keep.tile([P, M], BF16, name=f"praw{rt}", align_bytes=64))
-            nc.sync.dma_start(out=praw[rt][:], in_=p[rt * P : (rt + 1) * P, :])
+        nc.gpsimd.dma_start(out=amp_sb[:], in_=amp.rearrange("(j q t) -> q j t", q=P, t=PACK))
 
         warm = keep.tile([P, 1], F32, name="warm")
         nc.vector.memset(warm[:], 0.0)
         nc.scalar.activation(out=warm[:], in_=warm[:], func=ACT.Sin)
-        ident_b = keep.tile([P, P], BF16, name="ident_b")
-        make_identity(nc, ident_b[:])
-        ident_f = keep.tile([P, P], F32, name="ident_f")
-        make_identity(nc, ident_f[:])
 
-        vt = psum.tile([P, P], BF16, name="vt", tag="tx", bufs=3)
-        nc.tensor.transpose(vt[:], vrows[:], ident_b[:])
-        f1 = keep.tile([P, 8], F32, name="f1")
-        fb1 = keep.tile([P, 8], F32, name="fb1")
-        b1 = keep.tile([P, 8], F32, name="b1")
-        f2 = keep.tile([P, 8], F32, name="f2")
-        b2 = keep.tile([P, 8], F32, name="b2")
-        vs = keep.tile([P, 32], F32, name="vs")
-        nc.vector.tensor_copy(out=vs[:], in_=vt[:, 0:32])
-        nc.vector.tensor_scalar(f1[:], vs[:, 0:8], 1.0 / TWO_PI, None, OP.mult)
-        nc.vector.tensor_tensor(fb1[:], vs[:, 0:8], vs[:, 8:16], OP.mult)
-        nc.vector.tensor_scalar(b1[:], fb1[:], 1.0 / TWO_PI, None, OP.mult)
-        nc.vector.tensor_scalar(f2[:], vs[:, 16:24], 1.0 / TWO_PI, None, OP.mult)
-        nc.vector.tensor_tensor(b2[:], f2[:], vs[:, 24:32], OP.mult)
+        xs_sc = keep.tile([P, 2, P, PACK], F32, name="xs_sc")
+        for g in range(2):
+            bank = psum.tile([P, PACK, P], F32, name="bank", tag="tx", bufs=3)
+            for t in range(PACK):
+                nc.tensor.transpose(bank[:, t, :], xs_col[:, g, t : t + 1].to_broadcast([P, P]), ident[:])
+            nc.scalar.copy(out=xs_sc[:, g], in_=bank[:].rearrange("p t q -> p q t"))
 
-        xq = keep.tile([P, 4, 2, 512], U32, name="xq", align_bytes=64)
-        xqs = keep.tile([P, 4, 2, 512], U8, name="xqs", align_bytes=64)
-        wq = keep.tile([P, 2, N], U32, name="wq", align_bytes=64)
-        wqs = keep.tile([P, 2, N], U8, name="wqs", align_bytes=64)
-        pq = keep.tile([P, 4, R], U32, name="pq", align_bytes=64)
-        pqs = keep.tile([P, 4, R], U8, name="pqs", align_bytes=64)
-        hq = keep.tile([P, 4, N], U32, name="hq", align_bytes=64)
-        hqs = keep.tile([P, 4, N], U8, name="hqs", align_bytes=64)
+        turn = keep.tile([P, 2, 16], F32, name="turn")
+        phase1 = keep.tile([P, 8], F32, name="phase1")
 
-        def w_prep(q):
-            cols = slice(256 * q, 256 * q + 256)
-            for g in range(2):
-                wi = stage.tile([P, 256, PACK], BF16, name="wi", align_bytes=64, bufs=2)
-                nc.scalar.copy(out=wi[:], in_=wraw[g][:, :, cols].rearrange("q t n -> q n t"))
-                nc.vector.quantize_mx(
-                    out=wq[:, g, cols].bitcast(FP8X4),
-                    scales=wqs[:, g, cols],
-                    in_=wi[:].rearrange("q n t -> q (n t)"),
-                )
+        def channel_constants():
+            vf = keep.tile([P, 2, P], F32, name="vf")
+            nc.gpsimd.tensor_scalar(vf[:, 0, :], vrows[:, 0, :], 1.0, 0.0, OP.mult, OP.add)
+            nc.gpsimd.tensor_tensor(vf[:, 1, :], vrows[:, 0, :], vrows[:, 1, :], OP.mult)
+            vt = psum.tile([P, 2, P], F32, name="vt", tag="tx", bufs=3)
+            for a in range(2):
+                nc.tensor.transpose(vt[:, a, :], vf[:, a, :], ident[:])
+            nc.scalar.activation(out=turn[:], in_=vt[:, :, 0:16], func=ACT.Copy, scale=1.0 / TWO_PI)
+            nc.scalar.copy(out=phase1[:], in_=vt[:, 1, 0:8])
 
-        xs = {}
-        xi = {}
+        def planes(name, count, width):
+            codes = [keep.tile([P, width], U32, name=f"{name}c{a}", align_bytes=64) for a in range(count)]
+            scales = [keep.tile([P, width], U8, name=f"{name}s{a}", align_bytes=64) for a in range(count)]
+            return codes, scales
 
-        def x_mult(j, t):
-            if t == 0:
-                xs[j] = stage.tile([P, PACK, K], BF16, name="xs", align_bytes=64, bufs=2)
-            nc.vector.tensor_tensor(xs[j][:, t, :], xb[j][:, t, :].bitcast(FP8), xs_sc[:], OP.mult)
+        xq, xqs = planes("xq", 8, 512)
+        wq, wqs = planes("wq", 8, 256)
+        pq, pqs = planes("pq", 8, 512)
+        hq, hqs = planes("hq", 32, P)
 
-        def x_turn(j, t):
-            if t == 0:
-                xi[j] = stage.tile([P, 2, 512, PACK], BF16, name="xi", align_bytes=64, bufs=2)
-            bank = psum.tile([P, 2, 2, P], F32, name="bank", tag="tx", bufs=3)
-            words = xs[j][:, t, :].bitcast(F32)
-            for g in range(2):
-                for u in range(2):
-                    nc.tensor.transpose(bank[:, g, u, :], words[:, 256 * g + u : 256 * (g + 1) : 2], ident_f[:])
-            dst = xi[j][:].bitcast(F32)[:, :, t * P : (t + 1) * P, :]
-            nc.scalar.copy(out=dst, in_=bank[:].rearrange("q g u r -> q g r u"))
+        def quantize(codes, scales, src):
+            nc.vector.quantize_mx(out=codes[:].bitcast(FP8X4), scales=scales[:], in_=src)
 
-        def x_quant(j, g):
-            nc.vector.quantize_mx(
-                out=xq[:, j, g, :].bitcast(FP8X4),
-                scales=xqs[:, j, g, :],
-                in_=xi[j][:, g].rearrange("q m t -> q (m t)"),
+        wi, xs, xi, pi, banks = {}, {}, {}, {}, {}
+
+        def w_weave(n):
+            q, g = divmod(n, 2)
+            wi[n] = stage.tile([P, 256, PACK], BF16, name="wi", align_bytes=64, bufs=2)
+            nc.scalar.copy(
+                out=wi[n][:].rearrange("p (a i) t -> p a t i", i=4),
+                in_=wraw[q, g][:].rearrange("p t (a i) -> p a t i", i=4),
             )
 
-        pi = {}
+        def w_quant(n):
+            quantize(wq[n], wqs[n], wi[n][:].rearrange("p n t -> p (n t)"))
 
-        def p_turn(half, jp, rr):
-            if rr == 0:
-                pi[half, jp] = stage.tile([P, 2, 512, PACK], BF16, name="pi", align_bytes=64, bufs=2)
-            bank = psum.tile([P, 2, 2, P], F32, name="bank", tag="tx", bufs=3)
-            words = praw[4 * half + rr][:].bitcast(F32)
-            for jj in range(2):
-                j = 2 * jp + jj
+        def x_mult(n):
+            j, t = divmod(n, 4)
+            xs[n] = stage.tile([P, K], BF16, name="xs", align_bytes=64, bufs=3)
+            nc.vector.tensor_tensor(
+                xs[n][:], xb[j, t // 2][:, t % 2, :].bitcast(FP8), xs_sc[:].rearrange("p g q t -> p (g q t)"), OP.mult
+            )
+
+        def turn_words(key, words):
+            banks[key] = psum.tile([P, 2, 2, P], F32, name="bank", tag="tx", bufs=3)
+            for g in range(2):
                 for u in range(2):
-                    nc.tensor.transpose(bank[:, jj, u, :], words[:, 256 * j + u : 256 * (j + 1) : 2], ident_f[:])
-            dst = pi[half, jp][:].bitcast(F32)[:, :, rr * P : (rr + 1) * P, :]
-            nc.scalar.copy(out=dst, in_=bank[:].rearrange("q g u r -> q g r u"))
-            if rr == 3:
-                for jj in range(2):
-                    j = 2 * jp + jj
-                    nc.vector.quantize_mx(
-                        out=pq[:, j, half * 512 : half * 512 + 512].bitcast(FP8X4),
-                        scales=pqs[:, j, half * 512 : half * 512 + 512],
-                        in_=pi[half, jp][:, jj].rearrange("q m t -> q (m t)"),
-                    )
+                    nc.tensor.transpose(banks[key][:, g, u, :], words[:, 256 * g + u : 256 * (g + 1) : 2], ident[:])
 
-        st = {}
+        def copy_words(key, woven, slot):
+            dst = woven[:].bitcast(F32)[:, :, slot * P : (slot + 1) * P, :]
+            nc.scalar.copy(out=dst, in_=banks[key][:].rearrange("q g u r -> q g r u"))
 
-        def u_mm(i, j):
-            y = psum.tile([P, 512], F32, name="y", tag="y", bufs=2)
-            ncols = slice(P * i, P * i + P)
+        def x_turn(n):
+            turn_words(("x", n), xs[n][:].bitcast(F32))
+
+        def x_copy(n):
+            j, t = divmod(n, 4)
+            if t == 0:
+                xi[j] = stage.tile([P, 2, 512, PACK], BF16, name="xi", tag="woven", align_bytes=64, bufs=3)
+            copy_words(("x", n), xi[j], t)
+
+        def x_quant(j):
+            for g in range(2):
+                quantize(xq[2 * j + g], xqs[2 * j + g], xi[j][:, g].rearrange("q m t -> q (m t)"))
+
+        def p_turn(n):
+            half, jp, rr = n // 8, n // 4 % 2, n % 4
+            turn_words(("p", n), praw[4 * half + rr][:].bitcast(F32)[:, 512 * jp : 512 * jp + 512])
+
+        def p_copy(n):
+            if n % 4 == 0:
+                pi[n // 4] = stage.tile([P, 2, 512, PACK], BF16, name="pi", tag="woven", align_bytes=64, bufs=3)
+            copy_words(("p", n), pi[n // 4], n % 4)
+
+        def p_quant(a, jj):
+            quantize(pq[2 * a + jj], pqs[2 * a + jj], pi[a][:, jj].rearrange("q m t -> q (m t)"))
+
+        units = [(i, j) for j in range(4) for i in range(GROUP0)] + [(i, j) for i in range(GROUP0, 8) for j in range(4)]
+        ys, us, ks, rs, ss, ths, his = {}, {}, {}, {}, {}, {}, {}
+
+        def y_mm(s):
+            i, j = units[s]
+            ys[s] = psum.tile([P, 512], F32, name="y", tag="y", bufs=3)
+            cols = slice(P * (i % 2), P * (i % 2) + P)
             for g in range(2):
                 nc.tensor.matmul_mx(
-                    out=y[:],
-                    lhsT=wq[:, g, ncols].bitcast(FP8X4),
-                    lhsT_scale=wqs[:, g, ncols],
-                    rhs=xq[:, j, g, :].bitcast(FP8X4),
-                    rhs_scale=xqs[:, j, g, :],
+                    out=ys[s][:],
+                    lhsT=wq[2 * (i // 2) + g][:, cols].bitcast(FP8X4),
+                    lhsT_scale=wqs[2 * (i // 2) + g][:, cols],
+                    rhs=xq[2 * j + g][:].bitcast(FP8X4),
+                    rhs_scale=xqs[2 * j + g][:],
                     start=(g == 0),
                     stop=(g == 1),
                 )
-            turns = stage.tile([P, 512], F32, name="turns", bufs=2)
-            nc.scalar.activation(out=turns[:], in_=y[:], func=ACT.Identity, scale=f1[:, i : i + 1], bias=b1[:, i : i + 1])
-            k = stage.tile([P, 512], I32, name="k", bufs=3)
-            nc.gpsimd.tensor_scalar(k[:], turns[:], 1.0, 0.0, OP.mult, OP.add)
-            st[i, j] = (y, k)
 
-        def u_sin(i, j):
-            y, k = st[i, j]
-            r = stage.tile([P, 512], F32, name="r", bufs=2)
-            nc.vector.scalar_tensor_tensor(r[:], y[:], f1[:, i : i + 1], k[:], OP.mult, OP.subtract)
-            s = stage.tile([P, 512], F32, name="s", bufs=3)
-            nc.scalar.activation(out=s[:], in_=r[:], func=ACT.Sin, scale=TWO_PI, bias=fb1[:, i : i + 1])
-            st[i, j] = s
+        def y_turns(s):
+            i = units[s][0]
+            us[s] = stage.tile([P, 512], F32, name="u", bufs=2)
+            nc.scalar.activation(
+                out=us[s][:], in_=ys[s][:], func=ACT.Identity, scale=turn[:, 0, i : i + 1], bias=turn[:, 1, i : i + 1]
+            )
 
-        hi = {}
+        def y_round(s):
+            ks[s] = stage.tile([P, 512], I32, name="k", tag=f"kh{s % 2}", align_bytes=64, bufs=1)
+            nc.gpsimd.tensor_scalar(ks[s][:], us[s][:], 1.0, 0.0, OP.mult, OP.add)
 
-        def u_turn(i, j):
-            s = st[i, j]
-            th = psum.tile([P, PACK, P], F32, name="th", tag="th", bufs=1)
+        def y_rest(s):
+            i = units[s][0]
+            rs[s] = stage.tile([P, 512], F32, name="r", bufs=2)
+            nc.vector.scalar_tensor_tensor(rs[s][:], ys[s][:], turn[:, 0, i : i + 1], ks[s][:], OP.mult, OP.subtract)
+
+        def y_sin(s):
+            i = units[s][0]
+            ss[s] = stage.tile([P, 512], F32, name="s", bufs=3)
+            nc.scalar.activation(out=ss[s][:], in_=rs[s][:], func=ACT.Sin, scale=TWO_PI, bias=phase1[:, i : i + 1])
+
+        def h_turn(s):
+            ths[s] = psum.tile([P, PACK, P], F32, name="th", tag="th", bufs=2)
             for t in range(PACK):
-                nc.tensor.transpose(th[:, t, :], s[:, t * P : (t + 1) * P], ident_f[:])
-            hi[i, j] = stage.tile([P, P, PACK], BF16, name="hi", align_bytes=64, bufs=3)
+                nc.tensor.transpose(ths[s][:, t, :], ss[s][:, t * P : (t + 1) * P], ident[:])
+
+        def h_amp(s):
+            j = units[s][1]
+            his[s] = stage.tile([P, P, PACK], BF16, name="hi", tag=f"kh{s % 2}", align_bytes=64, bufs=1)
             nc.vector.tensor_tensor(
-                hi[i, j][:],
-                th[:].rearrange("q t n -> q n t"),
+                his[s][:],
+                ths[s][:].rearrange("q t n -> q n t"),
                 amp_sb[:, j, :].unsqueeze(1).to_broadcast([P, P, PACK]),
                 OP.mult,
             )
 
-        def u_quant(i, j):
-            ncols = slice(P * i, P * i + P)
-            nc.vector.quantize_mx(
-                out=hq[:, j, ncols].bitcast(FP8X4),
-                scales=hqs[:, j, ncols],
-                in_=hi[i, j][:].rearrange("q n t -> q (n t)"),
-            )
+        def h_quant(s):
+            i, j = units[s]
+            quantize(hq[4 * i + j], hqs[4 * i + j], his[s][:].rearrange("q n t -> q (n t)"))
 
-        zs = {}
+        z_tasks = [(0, 0, 512), (1, 0, 512), (0, 512, 512), (1, 512, 512)]
+        z_tasks.extend((i, r0, 512) for i in range(2, 7) for r0 in (0, 512))
+        z_tasks.extend((7, r0, 256) for r0 in range(0, R, 256))
+        zs, u2s, k2s, r2s, obs = {}, {}, {}, {}, {}
 
-        def z_mm(i, half):
-            z = psum.tile([P, 512], F32, name="z", tag="z", bufs=2)
-            ncols = slice(P * i, P * i + P)
-            rcols = slice(512 * half, 512 * half + 512)
-            for j in range(4):
+        def z_passes(n, dst, chunks):
+            i, r0, width = z_tasks[n]
+            half, cols = r0 // 512, slice(r0 % 512, r0 % 512 + width)
+            for j in chunks:
                 nc.tensor.matmul_mx(
-                    out=z[:],
-                    lhsT=hq[:, j, ncols].bitcast(FP8X4),
-                    lhsT_scale=hqs[:, j, ncols],
-                    rhs=pq[:, j, rcols].bitcast(FP8X4),
-                    rhs_scale=pqs[:, j, rcols],
+                    out=dst,
+                    lhsT=hq[4 * i + j][:].bitcast(FP8X4),
+                    lhsT_scale=hqs[4 * i + j][:],
+                    rhs=pq[4 * half + j][:, cols].bitcast(FP8X4),
+                    rhs_scale=pqs[4 * half + j][:, cols],
                     start=(j == 0),
                     stop=(j == 3),
                 )
-            zs[i, half] = z
 
-        def z_red(i, half):
-            turns2 = stage.tile([P, 512], F32, name="turns2", bufs=2)
-            nc.scalar.activation(out=turns2[:], in_=zs[i, half][:], func=ACT.Identity, scale=f2[:, i : i + 1], bias=b2[:, i : i + 1])
-            k2 = stage.tile([P, 512], I32, name="k2", bufs=2)
-            nc.vector.tensor_copy(out=k2[:], in_=turns2[:])
-            r2 = stage.tile([P, 512], F32, name="r2", bufs=2)
-            nc.vector.tensor_tensor(r2[:], turns2[:], k2[:], OP.subtract)
-            zs[i, half] = r2
+        def z_mm(n):
+            zs[n] = psum.tile([P, z_tasks[n][2]], F32, name="z", tag="tx", bufs=3)
+            z_passes(n, zs[n][:], range(4))
 
-        def z_out(i, half):
-            r2 = zs[i, half]
-            ob = psum.tile([P, PACK, P], F32, name="ob", tag="tx", bufs=3)
-            for q in range(4):
-                nc.tensor.transpose(ob[:, q, :], r2[:, q * P : (q + 1) * P], ident_f[:])
-            o = stage.tile([P, PACK, P], F32, name="o", bufs=3)
-            nc.scalar.activation(out=o[:], in_=ob[:], func=ACT.Sin, scale=TWO_PI)
+        def z_turns(n):
+            i = 8 + z_tasks[n][0]
+            u2s[n] = stage.tile([P, z_tasks[n][2]], F32, name="u2", bufs=4)
+            nc.scalar.activation(
+                out=u2s[n][:], in_=zs[n][:], func=ACT.Identity, scale=turn[:, 0, i : i + 1], bias=turn[:, 1, i : i + 1]
+            )
+
+        def z_round(n):
+            k2s[n] = stage.tile([P, z_tasks[n][2]], I32, name="k2", bufs=3)
+            nc.vector.tensor_copy(out=k2s[n][:], in_=u2s[n][:])
+
+        def z_rest(n):
+            r2s[n] = stage.tile([P, z_tasks[n][2]], F32, name="r2", bufs=3)
+            nc.vector.tensor_tensor(r2s[n][:], u2s[n][:], k2s[n][:], OP.subtract)
+
+        def z_turn(n):
+            blocks = z_tasks[n][2] // P
+            obs[n] = psum.tile([P, blocks, P], F32, name="ob", tag="tx", bufs=3)
+            for a in range(blocks):
+                nc.tensor.transpose(obs[n][:, a, :], r2s[n][:, a * P : (a + 1) * P], ident[:])
+
+        def z_out(n):
+            i, r0, width = z_tasks[n]
+            o = stage.tile([P, width // P, P], F32, name="o", bufs=4)
+            nc.scalar.activation(out=o[:], in_=obs[n][:], func=ACT.Sin, scale=TWO_PI)
             nc.sync.dma_start(
-                out=out[512 * half : 512 * half + 512, P * i : P * i + P].rearrange("(a q) n -> q a n", q=P),
+                out=out[r0 : r0 + width, P * i : P * i + P].rearrange("(a q) n -> q a n", q=P),
                 in_=o[:],
             )
 
-        units = [(i, j) for j in range(4) for i in range(GROUP0)] + [(i, j) for i in range(GROUP0, 8) for j in range(4)]
-        z_tasks = [(i, h) for i in range(8) for h in range(2)]
-        p_tasks = [(h, jp, rr) for h in range(2) for jp in range(2) for rr in range(4)]
-        at = {u: s for s, u in enumerate(units)}
+        def at(fn, n, count):
+            if n is not None and 0 <= n < count:
+                fn(n)
 
-        for q in range(4):
-            w_prep(q)
-        for t in range(4):
-            x_mult(0, t)
-            x_turn(0, t)
-        x_quant(0, 0)
-        x_quant(0, 1)
-
-        z_next = 0
-        z_log = {}
-        s = 0
-        while s < len(units) + 4 or z_next < len(z_tasks) or (s - 1) in z_log or (s - 2) in z_log:
-            if 0 <= s - 1 < 32:
-                u_sin(*units[s - 1])
-            if 0 <= s - 2 < 32:
-                u_turn(*units[s - 2])
-            if s - 2 in z_log:
-                z_out(*z_log[s - 2])
-            if s < 16 and s // 4 + 1 < 4:
-                x_mult(s // 4 + 1, s % 4)
-                x_turn(s // 4 + 1, s % 4)
-                if s % 4 == 3:
-                    x_quant(s // 4 + 1, 0)
-                    x_quant(s // 4 + 1, 1)
-            if 2 <= s < 18:
-                p_turn(*p_tasks[s - 2])
-            if 0 <= s - 3 < 32:
-                u_quant(*units[s - 3])
-            if s - 1 in z_log:
-                z_red(*z_log[s - 1])
-            if s < 32:
-                u_mm(*units[s])
-            if z_next < 16 and s >= 18 and at[z_tasks[z_next][0], 3] + 4 <= s:
-                z_log[s] = z_tasks[z_next]
-                z_mm(*z_log[s])
-                z_next += 1
-            s += 1
+        x_mult(0)
+        w_weave(0)
+        x_turn(0)
+        x_mult(1)
+        x_copy(0)
+        x_turn(1)
+        x_mult(2)
+        w_weave(1)
+        x_copy(1)
+        x_turn(2)
+        x_mult(3)
+        x_copy(2)
+        x_turn(3)
+        w_quant(0)
+        w_quant(1)
+        x_mult(4)
+        x_copy(3)
+        channel_constants()
+        x_turn(4)
+        x_mult(5)
+        w_weave(2)
+        x_copy(4)
+        x_quant(0)
+        z_step = {(18 + n + n // 2 if n < 10 else 22 + n): n for n in range(14)}
+        w_step = {-2: 2, 0: 3, 9: 4, 10: 5, 11: 6, 12: 7}
+        for s in range(0, 36):
+            at(y_mm, s, 32)
+            at(z_mm, z_step.get(s), 14)
+            at(h_turn, s - 3, 32)
+            at(z_turn, z_step.get(s - 3), 14)
+            at(x_turn, s + 5, 16)
+            at(p_turn, s - 0, 16)
+            at(z_round, z_step.get(s - 1), 14)
+            at(z_rest, z_step.get(s - 2), 14)
+            at(x_mult, s + 6, 16)
+            at(w_quant, w_step.get(s - (1 if s == 1 else 2)) if s != 2 else None, 8)
+            if (s + 1) % 4 == 0:
+                at(x_quant, (s + 1) // 4, 4)
+            if 5 <= s - 0 < 21 and (s - 0 - 1) % 4 < 2:
+                p_quant((s - 0 - 1) // 4 - 1, (s - 0 - 1) % 4)
+            at(h_quant, s - 4, 32)
+            at(y_sin, s - 2, 32)
+            at(y_turns, s, 32)
+            at(y_round, s, 32)
+            at(y_rest, s - 1, 32)
+            at(h_amp, s - 3, 32)
+            at(z_turns, z_step.get(s), 14)
+            at(x_copy, s + 5, 16)
+            at(p_copy, s - 0, 16)
+            at(w_weave, w_step.get(s) if s >= 0 else None, 8)
+            at(z_out, z_step.get(s - 3), 14)
+        for s in range(36, 44):
+            at(z_mm, s - 22, 18)
+            at(z_turn, s - 25, 18)
+            at(z_turns, s - 22, 18)
+            at(z_round, s - 23, 18)
+            at(z_rest, s - 24, 18)
+            at(z_out, s - 25, 18)

@@ -58,10 +58,10 @@ def tile_siren_anchor_field_f4_kernel(tc, x_bytes, x_scale, w, b, freq1, amp, p,
         load_w(1)
         load_p(0)
         load_x(2)
-        load_x(3)
-        load_p(1)
         load_w(2)
+        load_x(3)
         load_w(3)
+        load_p(1)
 
         ident = keep.tile([P, P], F32, name="ident")
         make_identity(nc, ident[:])
@@ -103,7 +103,7 @@ def tile_siren_anchor_field_f4_kernel(tc, x_bytes, x_scale, w, b, freq1, amp, p,
             return codes, scales
 
         xq, xqs = planes("xq", 8, 512)
-        wq, wqs = planes("wq", 8, 256)
+        wq, wqs = planes("wq", 16, P)
         pq, pqs = planes("pq", 8, 512)
         hq, hqs = planes("hq", 32, P)
 
@@ -113,11 +113,11 @@ def tile_siren_anchor_field_f4_kernel(tc, x_bytes, x_scale, w, b, freq1, amp, p,
         wi, xs, xi, pi, banks = {}, {}, {}, {}, {}
 
         def w_weave(n):
-            q, g = divmod(n, 2)
-            wi[n] = stage.tile([P, 256, PACK], BF16, name="wi", align_bytes=64, bufs=2)
+            i, g = divmod(n, 2)
+            wi[n] = stage.tile([P, P, PACK], BF16, name="wi", align_bytes=64, bufs=4)
             nc.scalar.copy(
-                out=wi[n][:].rearrange("p (a i) t -> p a t i", i=4),
-                in_=wraw[q, g][:].rearrange("p t (a i) -> p a t i", i=4),
+                out=wi[n][:].rearrange("p (a e) t -> p a t e", e=4),
+                in_=wraw[i // 2, g][:, :, P * (i % 2) : P * (i % 2) + P].rearrange("p t (a e) -> p a t e", e=4),
             )
 
         def w_quant(n):
@@ -149,9 +149,8 @@ def tile_siren_anchor_field_f4_kernel(tc, x_bytes, x_scale, w, b, freq1, amp, p,
                 xi[j] = stage.tile([P, 2, 512, PACK], BF16, name="xi", tag="woven", align_bytes=64, bufs=3)
             copy_words(("x", n), xi[j], t)
 
-        def x_quant(j):
-            for g in range(2):
-                quantize(xq[2 * j + g], xqs[2 * j + g], xi[j][:, g].rearrange("q m t -> q (m t)"))
+        def x_quant(n):
+            quantize(xq[n], xqs[n], xi[n // 2][:, n % 2].rearrange("q m t -> q (m t)"))
 
         def p_turn(n):
             half, jp, rr = n // 8, n // 4 % 2, n % 4
@@ -171,12 +170,11 @@ def tile_siren_anchor_field_f4_kernel(tc, x_bytes, x_scale, w, b, freq1, amp, p,
         def y_mm(s):
             i, j = units[s]
             ys[s] = psum.tile([P, 512], F32, name="y", tag="y", bufs=3)
-            cols = slice(P * (i % 2), P * (i % 2) + P)
             for g in range(2):
                 nc.tensor.matmul_mx(
                     out=ys[s][:],
-                    lhsT=wq[2 * (i // 2) + g][:, cols].bitcast(FP8X4),
-                    lhsT_scale=wqs[2 * (i // 2) + g][:, cols],
+                    lhsT=wq[2 * i + g][:].bitcast(FP8X4),
+                    lhsT_scale=wqs[2 * i + g][:],
                     rhs=xq[2 * j + g][:].bitcast(FP8X4),
                     rhs_scale=xqs[2 * j + g][:],
                     start=(g == 0),
@@ -228,23 +226,33 @@ def tile_siren_anchor_field_f4_kernel(tc, x_bytes, x_scale, w, b, freq1, amp, p,
         z_tasks.extend((7, r0, 256) for r0 in range(0, R, 256))
         zs, u2s, k2s, r2s, obs = {}, {}, {}, {}, {}
 
-        def z_passes(n, dst, chunks):
-            i, r0, width = z_tasks[n]
-            half, cols = r0 // 512, slice(r0 % 512, r0 % 512 + width)
+        def z_passes(i, half, dst, chunks):
             for j in chunks:
                 nc.tensor.matmul_mx(
-                    out=dst,
+                    out=dst[:],
                     lhsT=hq[4 * i + j][:].bitcast(FP8X4),
                     lhsT_scale=hqs[4 * i + j][:],
-                    rhs=pq[4 * half + j][:, cols].bitcast(FP8X4),
-                    rhs_scale=pqs[4 * half + j][:, cols],
+                    rhs=pq[4 * half + j][:].bitcast(FP8X4),
+                    rhs_scale=pqs[4 * half + j][:],
                     start=(j == 0),
                     stop=(j == 3),
                 )
 
         def z_mm(n):
-            zs[n] = psum.tile([P, z_tasks[n][2]], F32, name="z", tag="tx", bufs=3)
-            z_passes(n, zs[n][:], range(4))
+            i, r0, width = z_tasks[n]
+            zs[n] = psum.tile([P, width], F32, name="z", tag="tx", bufs=3)
+            z_passes(i, r0 // 512, zs[n], range(4))
+
+        last = {}
+
+        def last_open(half):
+            last[half] = psum.tile([P, 512], F32, name="z", tag="y", bufs=3)
+            z_passes(7, half, last[half], range(3))
+
+        def last_close(half):
+            z_passes(7, half, last[half], range(3, 4))
+            for a in range(2):
+                zs[14 + 2 * half + a] = last[half][:, 256 * a : 256 * a + 256]
 
         def z_turns(n):
             i = 8 + z_tasks[n][0]
@@ -269,7 +277,7 @@ def tile_siren_anchor_field_f4_kernel(tc, x_bytes, x_scale, w, b, freq1, amp, p,
 
         def z_out(n):
             i, r0, width = z_tasks[n]
-            o = stage.tile([P, width // P, P], F32, name="o", bufs=4)
+            o = stage.tile([P, width // P, P], F32, name="o", bufs=6)
             nc.scalar.activation(out=o[:], in_=obs[n][:], func=ACT.Sin, scale=TWO_PI)
             nc.sync.dma_start(
                 out=out[r0 : r0 + width, P * i : P * i + P].rearrange("(a q) n -> q a n", q=P),
@@ -282,59 +290,119 @@ def tile_siren_anchor_field_f4_kernel(tc, x_bytes, x_scale, w, b, freq1, amp, p,
 
         x_mult(0)
         w_weave(0)
+        w_weave(1)
         x_turn(0)
         x_mult(1)
         x_copy(0)
         x_turn(1)
         x_mult(2)
-        w_weave(1)
+        w_weave(2)
         x_copy(1)
         x_turn(2)
         x_mult(3)
+        w_weave(3)
         x_copy(2)
         x_turn(3)
-        w_quant(0)
-        w_quant(1)
+        for n in range(4):
+            w_quant(n)
         x_mult(4)
+        w_weave(4)
         x_copy(3)
         channel_constants()
         x_turn(4)
         x_mult(5)
-        w_weave(2)
+        w_weave(5)
         x_copy(4)
         x_quant(0)
-        z_step = {(18 + n + n // 2 if n < 10 else 22 + n): n for n in range(14)}
-        w_step = {-2: 2, 0: 3, 9: 4, 10: 5, 11: 6, 12: 7}
-        for s in range(0, 36):
+        x_quant(1)
+        x_turn(5)
+        w_quant(4)
+        w_quant(5)
+        x_mult(6)
+        w_weave(6)
+        x_copy(5)
+        z_step = {17 + n + n // 3: n for n in range(12)}
+        for s in range(0, 32):
             at(y_mm, s, 32)
             at(z_mm, z_step.get(s), 14)
             at(h_turn, s - 3, 32)
             at(z_turn, z_step.get(s - 3), 14)
-            at(x_turn, s + 5, 16)
+            at(x_turn, s + 6, 16)
             at(p_turn, s - 0, 16)
             at(z_round, z_step.get(s - 1), 14)
+            if s % 4 >= 2:
+                at(x_quant, 2 * (s // 4) + s % 4, 8)
             at(z_rest, z_step.get(s - 2), 14)
-            at(x_mult, s + 6, 16)
-            at(w_quant, w_step.get(s - (1 if s == 1 else 2)) if s != 2 else None, 8)
-            if (s + 1) % 4 == 0:
-                at(x_quant, (s + 1) // 4, 4)
+            at(x_mult, s + 7, 16)
+            at(w_quant, s + 6, 16)
             if 5 <= s - 0 < 21 and (s - 0 - 1) % 4 < 2:
                 p_quant((s - 0 - 1) // 4 - 1, (s - 0 - 1) % 4)
             at(h_quant, s - 4, 32)
-            at(y_sin, s - 2, 32)
             at(y_turns, s, 32)
             at(y_round, s, 32)
             at(y_rest, s - 1, 32)
             at(h_amp, s - 3, 32)
+            at(y_sin, s - 2, 32)
+            at(w_weave, s + 7, 16)
             at(z_turns, z_step.get(s), 14)
-            at(x_copy, s + 5, 16)
+            at(x_copy, s + 6, 16)
             at(p_copy, s - 0, 16)
-            at(w_weave, w_step.get(s) if s >= 0 else None, 8)
             at(z_out, z_step.get(s - 3), 14)
-        for s in range(36, 44):
-            at(z_mm, s - 22, 18)
-            at(z_turn, s - 25, 18)
-            at(z_turns, s - 22, 18)
-            at(z_round, s - 23, 18)
-            at(z_rest, s - 24, 18)
-            at(z_out, s - 25, 18)
+        h_turn(29)
+        z_turn(9)
+        z_mm(12)
+        y_sin(30)
+        y_rest(31)
+        h_amp(29)
+        h_quant(28)
+        z_round(11)
+        z_rest(10)
+        z_out(9)
+        y_sin(31)
+        z_turns(12)
+        h_turn(30)
+        z_turn(10)
+        h_quant(29)
+        h_amp(30)
+        h_turn(31)
+        z_mm(13)
+        z_rest(11)
+        h_quant(30)
+        h_amp(31)
+        z_round(12)
+        h_quant(31)
+        z_out(10)
+        z_turns(13)
+        last_open(0)
+        last_close(0)
+        last_open(1)
+        last_close(1)
+        z_rest(12)
+        z_round(13)
+        z_turn(11)
+        z_turn(12)
+        z_turns(14)
+        z_turns(15)
+        z_out(11)
+        z_turns(16)
+        z_turns(17)
+        z_out(12)
+        z_rest(13)
+        z_round(14)
+        z_round(15)
+        z_rest(14)
+        z_turn(13)
+        z_out(13)
+        z_rest(15)
+        z_turn(14)
+        z_out(14)
+        z_round(16)
+        z_round(17)
+        z_rest(16)
+        z_turn(15)
+        z_out(15)
+        z_rest(17)
+        z_turn(16)
+        z_out(16)
+        z_turn(17)
+        z_out(17)

@@ -20,7 +20,6 @@ OP = mybir.AluOpType
 P = 128
 PACK = 4
 TWO_PI = 2.0 * math.pi
-GROUP0 = 4
 
 
 def tile_siren_anchor_field_f4_kernel(tc, x_bytes, x_scale, w, b, freq1, amp, p, c, freq2, out):
@@ -82,7 +81,7 @@ def tile_siren_anchor_field_f4_kernel(tc, x_bytes, x_scale, w, b, freq1, amp, p,
             bank = psum.tile([P, PACK, P], F32, name="bank", tag="tx", bufs=3)
             for t in range(PACK):
                 nc.tensor.transpose(bank[:, t, :], xs_col[:, g, t : t + 1].to_broadcast([P, P]), ident[:])
-            nc.scalar.copy(out=xs_sc[:, g], in_=bank[:].rearrange("p t q -> p q t"))
+            (nc.scalar.copy, nc.vector.tensor_copy)[g](out=xs_sc[:, g], in_=bank[:].rearrange("p t q -> p q t"))
 
         turn = keep.tile([P, 2, 16], F32, name="turn")
         phase1 = keep.tile([P, 8], F32, name="phase1")
@@ -161,10 +160,10 @@ def tile_siren_anchor_field_f4_kernel(tc, x_bytes, x_scale, w, b, freq1, amp, p,
                 pi[n // 4] = stage.tile([P, 2, 512, PACK], BF16, name="pi", tag="woven", align_bytes=64, bufs=3)
             copy_words(("p", n), pi[n // 4], n % 4)
 
-        def p_quant(a, jj):
-            quantize(pq[2 * a + jj], pqs[2 * a + jj], pi[a][:, jj].rearrange("q m t -> q (m t)"))
+        def p_quant(n):
+            quantize(pq[n], pqs[n], pi[n // 2][:, n % 2].rearrange("q m t -> q (m t)"))
 
-        units = [(i, j) for j in range(4) for i in range(GROUP0)] + [(i, j) for i in range(GROUP0, 8) for j in range(4)]
+        units = [(i, j) for j in range(4) for i in range(4)] + [(i, j) for i in range(4, 8) for j in range(4)]
         ys, us, ks, rs, ss, ths, his = {}, {}, {}, {}, {}, {}, {}
 
         def y_mm(s):
@@ -191,6 +190,11 @@ def tile_siren_anchor_field_f4_kernel(tc, x_bytes, x_scale, w, b, freq1, amp, p,
         def y_round(s):
             ks[s] = stage.tile([P, 512], I32, name="k", tag=f"kh{s % 2}", align_bytes=64, bufs=1)
             nc.gpsimd.tensor_scalar(ks[s][:], us[s][:], 1.0, 0.0, OP.mult, OP.add)
+
+        def y_round_direct(s):
+            i = units[s][0]
+            ks[s] = stage.tile([P, 512], I32, name="k", tag=f"kh{s % 2}", align_bytes=64, bufs=1)
+            nc.vector.tensor_scalar(ks[s][:], ys[s][:], turn[:, 0, i : i + 1], turn[:, 1, i : i + 1], OP.mult, OP.add)
 
         def y_rest(s):
             i = units[s][0]
@@ -321,32 +325,47 @@ def tile_siren_anchor_field_f4_kernel(tc, x_bytes, x_scale, w, b, freq1, amp, p,
         x_mult(6)
         w_weave(6)
         x_copy(5)
-        z_step = {17 + n + n // 3: n for n in range(12)}
+        z_step = {step: n for n, step in enumerate([17 + n + n // 3 for n in range(12)])}
+        x_at = {s: (s + 6,) for s in range(10)}
+        xq_at = {2: (2,), 3: (3,), 6: (4,), 7: (5,), 10: (6,), 11: (7,)}
+        p_at = {s: (s,) for s in range(16)}
+        pq_at = {5: (0,), 6: (1,), 9: (2,), 10: (3,), 13: (4,), 14: (5,), 17: (6,), 18: (7,)}
+        w_at = {s: (s + 7,) for s in range(-1, 9)}
         for s in range(0, 32):
-            at(y_mm, s, 32)
+            y_mm(s)
             at(z_mm, z_step.get(s), 14)
             at(h_turn, s - 3, 32)
             at(z_turn, z_step.get(s - 3), 14)
-            at(x_turn, s + 6, 16)
-            at(p_turn, s - 0, 16)
-            at(z_round, z_step.get(s - 1), 14)
-            if s % 4 >= 2:
-                at(x_quant, 2 * (s // 4) + s % 4, 8)
-            at(z_rest, z_step.get(s - 2), 14)
-            at(x_mult, s + 7, 16)
-            at(w_quant, s + 6, 16)
-            if 5 <= s - 0 < 21 and (s - 0 - 1) % 4 < 2:
-                p_quant((s - 0 - 1) // 4 - 1, (s - 0 - 1) % 4)
+            turned = [(x_turn, x_copy, n) for n in x_at.get(s, ())] + [(p_turn, p_copy, n) for n in p_at.get(s, ())]
+            for turn_fn, copy_fn, n in turned[:3]:
+                turn_fn(n)
+            two_port = []
+            if s - 1 in z_step:
+                two_port.append((z_round, z_step[s - 1]))
+            two_port.extend((w_quant, n) for n in w_at.get(s - 1, ()))
+            two_port.extend((x_quant, n) for n in xq_at.get(s, ()))
+            two_port.extend((p_quant, n) for n in pq_at.get(s, ()))
+            if s - 2 in z_step:
+                two_port.append((z_rest, z_step[s - 2]))
+            two_port.extend((x_mult, n) for n in x_at.get(s + 1, ()))
+            for fn, n in two_port[:-1]:
+                fn(n)
             at(h_quant, s - 4, 32)
-            at(y_turns, s, 32)
-            at(y_round, s, 32)
+            for fn, n in two_port[-1:]:
+                fn(n)
+            y_turns(s)
+            y_round(s)
+            at(y_sin, s - 2, 32)
             at(y_rest, s - 1, 32)
             at(h_amp, s - 3, 32)
-            at(y_sin, s - 2, 32)
-            at(w_weave, s + 7, 16)
+            for n in w_at.get(s, ()):
+                w_weave(n)
             at(z_turns, z_step.get(s), 14)
-            at(x_copy, s + 6, 16)
-            at(p_copy, s - 0, 16)
+            for turn_fn, copy_fn, n in turned[:3]:
+                copy_fn(n)
+            for turn_fn, copy_fn, n in turned[3:]:
+                turn_fn(n)
+                copy_fn(n)
             at(z_out, z_step.get(s - 3), 14)
         h_turn(29)
         z_turn(9)
@@ -354,23 +373,23 @@ def tile_siren_anchor_field_f4_kernel(tc, x_bytes, x_scale, w, b, freq1, amp, p,
         y_sin(30)
         y_rest(31)
         h_amp(29)
-        h_quant(28)
         z_round(11)
+        h_quant(28)
         z_rest(10)
-        z_out(9)
         y_sin(31)
+        z_out(9)
         z_turns(12)
         h_turn(30)
-        z_turn(10)
-        h_quant(29)
-        h_amp(30)
         h_turn(31)
+        z_turn(10)
         z_mm(13)
-        z_rest(11)
-        h_quant(30)
+        h_amp(30)
+        h_quant(29)
         h_amp(31)
-        z_round(12)
+        h_quant(30)
+        z_rest(11)
         h_quant(31)
+        z_round(12)
         z_out(10)
         z_turns(13)
         last_open(0)
@@ -383,9 +402,9 @@ def tile_siren_anchor_field_f4_kernel(tc, x_bytes, x_scale, w, b, freq1, amp, p,
         z_turn(12)
         z_turns(14)
         z_turns(15)
-        z_out(11)
         z_turns(16)
         z_turns(17)
+        z_out(11)
         z_out(12)
         z_rest(13)
         z_round(14)

@@ -64,6 +64,8 @@ def tile_siren_anchor_field_f4_kernel(tc, x_bytes, x_scale, w, b, freq1, amp, p,
 
         ident = keep.tile([P, P], F32, name="ident")
         make_identity(nc, ident[:])
+        ident_b = keep.tile([P, P], BF16, name="ident_b")
+        nc.vector.tensor_copy(out=ident_b[:], in_=ident[:])
         vrows = keep.tile([P, 2, P], BF16, name="vrows")
         nc.gpsimd.memset(vrows[:], 0.0)
         for layer, (fr, bias) in enumerate(((freq1, b), (freq2, c))):
@@ -87,14 +89,14 @@ def tile_siren_anchor_field_f4_kernel(tc, x_bytes, x_scale, w, b, freq1, amp, p,
         phase1 = keep.tile([P, 8], F32, name="phase1")
 
         def channel_constants():
-            vf = keep.tile([P, 2, P], F32, name="vf")
-            nc.gpsimd.tensor_scalar(vf[:, 0, :], vrows[:, 0, :], 1.0, 0.0, OP.mult, OP.add)
-            nc.gpsimd.tensor_tensor(vf[:, 1, :], vrows[:, 0, :], vrows[:, 1, :], OP.mult)
-            vt = psum.tile([P, 2, P], F32, name="vt", tag="tx", bufs=3)
+            vt = psum.tile([P, 2, P], BF16, name="vt", tag="tx", bufs=3)
             for a in range(2):
-                nc.tensor.transpose(vt[:, a, :], vf[:, a, :], ident[:])
-            nc.scalar.activation(out=turn[:], in_=vt[:, :, 0:16], func=ACT.Copy, scale=1.0 / TWO_PI)
-            nc.scalar.copy(out=phase1[:], in_=vt[:, 1, 0:8])
+                nc.tensor.transpose(vt[:, a, :], vrows[:, a, :], ident_b[:])
+            nc.scalar.activation(out=turn[:, 0, :], in_=vt[:, 0, 0:16], func=ACT.Copy, scale=1.0 / TWO_PI)
+            nc.vector.tensor_tensor(turn[:, 1, :], vt[:, 1, 0:16], turn[:, 0, :], OP.mult)
+
+        def phase_constants():
+            nc.scalar.activation(out=phase1[:], in_=turn[:, 1, 0:8], func=ACT.Copy, scale=TWO_PI)
 
         def planes(name, count, width):
             codes = [keep.tile([P, width], U32, name=f"{name}c{a}", align_bytes=64) for a in range(count)]
@@ -113,7 +115,10 @@ def tile_siren_anchor_field_f4_kernel(tc, x_bytes, x_scale, w, b, freq1, amp, p,
 
         def w_weave(n):
             i, g = divmod(n, 2)
-            wi[n] = stage.tile([P, P, PACK], BF16, name="wi", align_bytes=64, bufs=4)
+            if 6 <= n < 10:
+                wi[n] = stage.tile([P, P, PACK], BF16, name="wi", tag=f"kh{(n - 7) % 3}", align_bytes=64, bufs=1)
+            else:
+                wi[n] = stage.tile([P, P, PACK], BF16, name="wi", align_bytes=64, bufs=4)
             nc.scalar.copy(
                 out=wi[n][:].rearrange("p (a e) t -> p a t e", e=4),
                 in_=wraw[i // 2, g][:, :, P * (i % 2) : P * (i % 2) + P].rearrange("p t (a e) -> p a t e", e=4),
@@ -182,23 +187,23 @@ def tile_siren_anchor_field_f4_kernel(tc, x_bytes, x_scale, w, b, freq1, amp, p,
 
         def y_turns(s):
             i = units[s][0]
-            us[s] = stage.tile([P, 512], F32, name="u", bufs=2)
+            us[s] = stage.tile([P, 512], F32, name="u", bufs=3)
             nc.scalar.activation(
                 out=us[s][:], in_=ys[s][:], func=ACT.Identity, scale=turn[:, 0, i : i + 1], bias=turn[:, 1, i : i + 1]
             )
 
         def y_round(s):
-            ks[s] = stage.tile([P, 512], I32, name="k", tag=f"kh{s % 2}", align_bytes=64, bufs=1)
+            ks[s] = stage.tile([P, 512], I32, name="k", tag=f"kh{(s - 1) % 3}", align_bytes=64, bufs=1)
             nc.gpsimd.tensor_scalar(ks[s][:], us[s][:], 1.0, 0.0, OP.mult, OP.add)
 
         def y_round_direct(s):
             i = units[s][0]
-            ks[s] = stage.tile([P, 512], I32, name="k", tag=f"kh{s % 2}", align_bytes=64, bufs=1)
+            ks[s] = stage.tile([P, 512], I32, name="k", tag=f"kh{(s - 1) % 3}", align_bytes=64, bufs=1)
             nc.vector.tensor_scalar(ks[s][:], ys[s][:], turn[:, 0, i : i + 1], turn[:, 1, i : i + 1], OP.mult, OP.add)
 
         def y_rest(s):
             i = units[s][0]
-            rs[s] = stage.tile([P, 512], F32, name="r", bufs=2)
+            rs[s] = stage.tile([P, 512], F32, name="r", bufs=3)
             nc.vector.scalar_tensor_tensor(rs[s][:], ys[s][:], turn[:, 0, i : i + 1], ks[s][:], OP.mult, OP.subtract)
 
         def y_sin(s):
@@ -213,7 +218,7 @@ def tile_siren_anchor_field_f4_kernel(tc, x_bytes, x_scale, w, b, freq1, amp, p,
 
         def h_amp(s):
             j = units[s][1]
-            his[s] = stage.tile([P, P, PACK], BF16, name="hi", tag=f"kh{s % 2}", align_bytes=64, bufs=1)
+            his[s] = stage.tile([P, P, PACK], BF16, name="hi", tag=f"kh{s % 3}", align_bytes=64, bufs=1)
             nc.vector.tensor_tensor(
                 his[s][:],
                 ths[s][:].rearrange("q t n -> q n t"),
@@ -296,40 +301,41 @@ def tile_siren_anchor_field_f4_kernel(tc, x_bytes, x_scale, w, b, freq1, amp, p,
         w_weave(0)
         w_weave(1)
         x_turn(0)
-        x_mult(1)
         x_copy(0)
-        x_turn(1)
-        x_mult(2)
+        x_mult(1)
         w_weave(2)
+        x_turn(1)
         x_copy(1)
-        x_turn(2)
-        x_mult(3)
+        x_mult(2)
         w_weave(3)
+        x_turn(2)
         x_copy(2)
-        x_turn(3)
-        for n in range(4):
-            w_quant(n)
-        x_mult(4)
+        x_mult(3)
         w_weave(4)
+        x_turn(3)
         x_copy(3)
-        channel_constants()
-        x_turn(4)
-        x_mult(5)
+        w_quant(0)
+        w_quant(1)
+        w_quant(2)
+        w_quant(3)
+        x_mult(4)
         w_weave(5)
+        x_turn(4)
         x_copy(4)
+        x_mult(5)
         x_quant(0)
         x_quant(1)
-        x_turn(5)
+        channel_constants()
         w_quant(4)
         w_quant(5)
-        x_mult(6)
         w_weave(6)
-        x_copy(5)
+        phase_constants()
+        x_mult(6)
         z_step = {step: n for n, step in enumerate([17 + n + n // 3 for n in range(12)])}
-        x_at = {s: (s + 6,) for s in range(10)}
+        x_at = {0: (5, 6), **{s: (s + 6,) for s in range(1, 10)}}
         xq_at = {2: (2,), 3: (3,), 6: (4,), 7: (5,), 10: (6,), 11: (7,)}
         p_at = {s: (s,) for s in range(16)}
-        pq_at = {5: (0,), 6: (1,), 9: (2,), 10: (3,), 13: (4,), 14: (5,), 17: (6,), 18: (7,)}
+        pq_at = {5: (0,), 7: (1,), 9: (2,), 11: (3,), 13: (4,), 14: (5,), 17: (6,), 18: (7,)}
         w_at = {s: (s + 7,) for s in range(-1, 9)}
         for s in range(0, 32):
             y_mm(s)
@@ -342,7 +348,8 @@ def tile_siren_anchor_field_f4_kernel(tc, x_bytes, x_scale, w, b, freq1, amp, p,
             two_port = []
             if s - 1 in z_step:
                 two_port.append((z_round, z_step[s - 1]))
-            two_port.extend((w_quant, n) for n in w_at.get(s - 1, ()))
+            if s >= 4:
+                two_port.extend((w_quant, n) for n in w_at.get(s - 1, ()))
             two_port.extend((x_quant, n) for n in xq_at.get(s, ()))
             two_port.extend((p_quant, n) for n in pq_at.get(s, ()))
             if s - 2 in z_step:
@@ -350,14 +357,17 @@ def tile_siren_anchor_field_f4_kernel(tc, x_bytes, x_scale, w, b, freq1, amp, p,
             two_port.extend((x_mult, n) for n in x_at.get(s + 1, ()))
             for fn, n in two_port[:-1]:
                 fn(n)
-            at(h_quant, s - 4, 32)
+            if s >= 4:
+                h_quant(s - 4)
+            else:
+                w_quant(s + 6)
             for fn, n in two_port[-1:]:
                 fn(n)
             y_turns(s)
             y_round(s)
             at(y_sin, s - 2, 32)
-            at(y_rest, s - 1, 32)
             at(h_amp, s - 3, 32)
+            at(y_rest, s - 1, 32)
             for n in w_at.get(s, ()):
                 w_weave(n)
             at(z_turns, z_step.get(s), 14)

@@ -36,31 +36,39 @@ def tile_siren_anchor_field_f4_kernel(tc, x_bytes, x_scale, w, b, freq1, amp, p,
         w_view = w.rearrange("(g q t) n -> g q t n", q=P, t=PACK)
         xb, wraw, praw = {}, {}, {}
 
-        def load_x(j):
-            for hf in range(2):
-                xb[j, hf] = keep.tile([P, 2, K], U8, name=f"xb{j}_{hf}", align_bytes=64)
-                nc.sync.dma_start(out=xb[j, hf][:], in_=x_view[j][:, 2 * hf : 2 * hf + 2, :])
+        def load_x(j, hf):
+            xb[j, hf] = keep.tile([P, 2, K], U8, name=f"xb{j}_{hf}", align_bytes=64)
+            nc.sync.dma_start(out=xb[j, hf][:], in_=x_view[j][:, 2 * hf : 2 * hf + 2, :])
 
         def load_w(q):
             for g in range(2):
                 wraw[q, g] = keep.tile([P, PACK, 256], BF16, name=f"wraw{q}_{g}", align_bytes=64)
                 nc.sync.dma_start(out=wraw[q, g][:], in_=w_view[g][:, :, 256 * q : 256 * q + 256])
 
-        def load_p(half):
-            for rt in range(4 * half, 4 * half + 4):
-                praw[rt] = keep.tile([P, M], BF16, name=f"praw{rt}", align_bytes=64)
-                nc.sync.dma_start(out=praw[rt][:], in_=p[rt * P : (rt + 1) * P, :])
+        def load_p(rt):
+            praw[rt] = keep.tile([P, M], BF16, name=f"praw{rt}", align_bytes=64)
+            nc.sync.dma_start(out=praw[rt][:], in_=p[rt * P : (rt + 1) * P, :])
 
-        load_x(0)
+        load_x(0, 0)
         load_w(0)
-        load_x(1)
+        load_x(0, 1)
         load_w(1)
+        load_x(1, 0)
+        load_x(1, 1)
         load_p(0)
-        load_x(2)
-        load_w(2)
-        load_x(3)
-        load_w(3)
         load_p(1)
+        load_p(2)
+        load_p(3)
+        load_x(2, 0)
+        load_x(2, 1)
+        load_w(2)
+        load_x(3, 0)
+        load_x(3, 1)
+        load_p(4)
+        load_p(5)
+        load_p(6)
+        load_p(7)
+        load_w(3)
 
         ident = keep.tile([P, P], F32, name="ident")
         make_identity(nc, ident[:])
@@ -88,11 +96,14 @@ def tile_siren_anchor_field_f4_kernel(tc, x_bytes, x_scale, w, b, freq1, amp, p,
         turn = keep.tile([P, 2, 16], F32, name="turn")
         phase1 = keep.tile([P, 8], F32, name="phase1")
 
-        def channel_constants():
-            vt = psum.tile([P, 2, P], BF16, name="vt", tag="tx", bufs=3)
+        vt = psum.tile([P, 2, P], BF16, name="vt", tag="th", bufs=2)
+
+        def channel_constants_a():
             for a in range(2):
                 nc.tensor.transpose(vt[:, a, :], vrows[:, a, :], ident_b[:])
             nc.scalar.activation(out=turn[:, 0, :], in_=vt[:, 0, 0:16], func=ACT.Copy, scale=1.0 / TWO_PI)
+
+        def channel_constants_b():
             nc.vector.tensor_tensor(turn[:, 1, :], vt[:, 1, 0:16], turn[:, 0, :], OP.mult)
 
         def phase_constants():
@@ -150,23 +161,39 @@ def tile_siren_anchor_field_f4_kernel(tc, x_bytes, x_scale, w, b, freq1, amp, p,
         def x_copy(n):
             j, t = divmod(n, 4)
             if t == 0:
-                xi[j] = stage.tile([P, 2, 512, PACK], BF16, name="xi", tag="woven", align_bytes=64, bufs=3)
+                xi[j] = stage.tile([P, 2, 512, PACK], BF16, name="xi", align_bytes=64, bufs=2)
             copy_words(("x", n), xi[j], t)
 
         def x_quant(n):
             quantize(xq[n], xqs[n], xi[n // 2][:, n % 2].rearrange("q m t -> q (m t)"))
 
         def p_turn(n):
-            half, jp, rr = n // 8, n // 4 % 2, n % 4
-            turn_words(("p", n), praw[4 * half + rr][:].bitcast(F32)[:, 512 * jp : 512 * jp + 512])
+            half, j, pair = n // 8, n // 2 % 4, n % 2
+            banks["p", n] = psum.tile([P, 2, 2, P], F32, name="bank", tag="tx", bufs=3)
+            for a in range(2):
+                words = praw[4 * half + 2 * pair + a][:].bitcast(F32)
+                for u in range(2):
+                    nc.tensor.transpose(banks["p", n][:, a, u, :], words[:, 256 * j + u : 256 * (j + 1) : 2], ident[:])
 
         def p_copy(n):
-            if n % 4 == 0:
-                pi[n // 4] = stage.tile([P, 2, 512, PACK], BF16, name="pi", tag="woven", align_bytes=64, bufs=3)
-            copy_words(("p", n), pi[n // 4], n % 4)
+            m, pair = divmod(n, 2)
+            if m < 4:
+                pi[n] = stage.tile([P, 1024], BF16, name="pi", tag="o", align_bytes=64, bufs=8)[:]
+            else:
+                if pair == 0:
+                    pi[m, "both"] = keep.tile([P, M], BF16, name=f"praw{m - 4}", align_bytes=64)
+                pi[n] = pi[m, "both"][:, 1024 * pair : 1024 * pair + 1024]
+            nc.scalar.copy(
+                out=pi[n].bitcast(F32).rearrange("q (a r u) -> q a r u", a=2, u=2),
+                in_=banks["p", n][:].rearrange("q a u r -> q a r u"),
+            )
 
         def p_quant(n):
-            quantize(pq[n], pqs[n], pi[n // 2][:, n % 2].rearrange("q m t -> q (m t)"))
+            if n >= 8:
+                quantize(pq[n - 4], pqs[n - 4], pi[n - 4, "both"][:])
+            else:
+                cols = slice(256 * (n % 2), 256 * (n % 2) + 256)
+                nc.vector.quantize_mx(out=pq[n // 2][:, cols].bitcast(FP8X4), scales=pqs[n // 2][:, cols], in_=pi[n])
 
         units = [(i, j) for j in range(4) for i in range(4)] + [(i, j) for i in range(4, 8) for j in range(4)]
         ys, us, ks, rs, ss, ths, his = {}, {}, {}, {}, {}, {}, {}
@@ -230,8 +257,8 @@ def tile_siren_anchor_field_f4_kernel(tc, x_bytes, x_scale, w, b, freq1, amp, p,
             i, j = units[s]
             quantize(hq[4 * i + j], hqs[4 * i + j], his[s][:].rearrange("q n t -> q (n t)"))
 
-        z_tasks = [(0, 0, 512), (1, 0, 512), (0, 512, 512), (1, 512, 512)]
-        z_tasks.extend((i, r0, 512) for i in range(2, 7) for r0 in (0, 512))
+        z_tasks = [(i, r0, 512) for r0 in (0, 512) for i in range(4)]
+        z_tasks.extend((i, r0, 512) for i in range(4, 7) for r0 in (0, 512))
         z_tasks.extend((7, r0, 256) for r0 in range(0, R, 256))
         zs, u2s, k2s, r2s, obs = {}, {}, {}, {}, {}
 
@@ -254,12 +281,10 @@ def tile_siren_anchor_field_f4_kernel(tc, x_bytes, x_scale, w, b, freq1, amp, p,
 
         last = {}
 
-        def last_open(half):
-            last[half] = psum.tile([P, 512], F32, name="z", tag="y", bufs=3)
-            z_passes(7, half, last[half], range(3))
-
-        def last_close(half):
-            z_passes(7, half, last[half], range(3, 4))
+        def last_pass(half, j):
+            if j == 0:
+                last[half] = psum.tile([P, 512], F32, name="z", tag="y", bufs=3)
+            z_passes(7, half, last[half], range(j, j + 1))
             for a in range(2):
                 zs[14 + 2 * half + a] = last[half][:, 256 * a : 256 * a + 256]
 
@@ -280,13 +305,16 @@ def tile_siren_anchor_field_f4_kernel(tc, x_bytes, x_scale, w, b, freq1, amp, p,
 
         def z_turn(n):
             blocks = z_tasks[n][2] // P
-            obs[n] = psum.tile([P, blocks, P], F32, name="ob", tag="tx", bufs=3)
+            if n in (14, 15):
+                obs[n] = psum.tile([P, blocks, P], F32, name="ob", tag="th", bufs=2)
+            else:
+                obs[n] = psum.tile([P, blocks, P], F32, name="ob", tag="tx", bufs=3)
             for a in range(blocks):
                 nc.tensor.transpose(obs[n][:, a, :], r2s[n][:, a * P : (a + 1) * P], ident[:])
 
         def z_out(n):
             i, r0, width = z_tasks[n]
-            o = stage.tile([P, width // P, P], F32, name="o", bufs=6)
+            o = stage.tile([P, width // P, P], F32, name="o", align_bytes=64, bufs=8)
             nc.scalar.activation(out=o[:], in_=obs[n][:], func=ACT.Sin, scale=TWO_PI)
             nc.sync.dma_start(
                 out=out[r0 : r0 + width, P * i : P * i + P].rearrange("(a q) n -> q a n", q=P),
@@ -300,18 +328,19 @@ def tile_siren_anchor_field_f4_kernel(tc, x_bytes, x_scale, w, b, freq1, amp, p,
         x_mult(0)
         w_weave(0)
         w_weave(1)
+        w_weave(2)
         x_turn(0)
         x_copy(0)
         x_mult(1)
-        w_weave(2)
+        w_weave(3)
         x_turn(1)
         x_copy(1)
         x_mult(2)
-        w_weave(3)
+        w_weave(4)
         x_turn(2)
         x_copy(2)
         x_mult(3)
-        w_weave(4)
+        w_weave(5)
         x_turn(3)
         x_copy(3)
         w_quant(0)
@@ -319,24 +348,25 @@ def tile_siren_anchor_field_f4_kernel(tc, x_bytes, x_scale, w, b, freq1, amp, p,
         w_quant(2)
         w_quant(3)
         x_mult(4)
-        w_weave(5)
+        channel_constants_a()
+        w_weave(6)
         x_turn(4)
         x_copy(4)
         x_mult(5)
+        x_turn(5)
         x_quant(0)
+        channel_constants_b()
         x_quant(1)
-        channel_constants()
+        phase_constants()
+        x_copy(5)
         w_quant(4)
         w_quant(5)
-        w_weave(6)
-        phase_constants()
-        x_mult(6)
         z_step = {step: n for n, step in enumerate([17 + n + n // 3 for n in range(12)])}
-        x_at = {0: (5, 6), **{s: (s + 6,) for s in range(1, 10)}}
+        x_at = {1: (6, 7), **{s: (s + 6,) for s in range(2, 10)}}
         xq_at = {2: (2,), 3: (3,), 6: (4,), 7: (5,), 10: (6,), 11: (7,)}
-        p_at = {s: (s,) for s in range(16)}
-        pq_at = {5: (0,), 7: (1,), 9: (2,), 11: (3,), 13: (4,), 14: (5,), 17: (6,), 18: (7,)}
-        w_at = {s: (s + 7,) for s in range(-1, 9)}
+        p_at = {0: (0,), 1: (1,), 2: (2,), 3: (3, 4), 4: (5,), 5: (6,), 6: (7, 8), 7: (9,), 8: (10,), 9: (11,), 10: (12,), 11: (13,), 12: (14,), 13: (15,)}
+        pq_at = {9: (0,), 12: (1, 2), 13: (3, 4), 14: (5,), 15: (6,), 16: (7,), 17: (8,), 18: (9,), 20: (10,), 21: (11,)}
+        w_at = {0: (7,), 1: (8,), 2: (9,), 14: (10,), 15: (11,), 16: (12,), 20: (13,), 24: (14,), 25: (15,)}
         for s in range(0, 32):
             y_mm(s)
             at(z_mm, z_step.get(s), 14)
@@ -349,7 +379,7 @@ def tile_siren_anchor_field_f4_kernel(tc, x_bytes, x_scale, w, b, freq1, amp, p,
             if s - 1 in z_step:
                 two_port.append((z_round, z_step[s - 1]))
             if s >= 4:
-                two_port.extend((w_quant, n) for n in w_at.get(s - 1, ()))
+                two_port.extend((w_quant, n) for n in w_at.get(s - 2, ()) if n >= 10)
             two_port.extend((x_quant, n) for n in xq_at.get(s, ()))
             two_port.extend((p_quant, n) for n in pq_at.get(s, ()))
             if s - 2 in z_step:
@@ -368,10 +398,12 @@ def tile_siren_anchor_field_f4_kernel(tc, x_bytes, x_scale, w, b, freq1, amp, p,
             at(y_sin, s - 2, 32)
             at(h_amp, s - 3, 32)
             at(y_rest, s - 1, 32)
+            at(z_turns, z_step.get(s), 14)
+            for turn_fn, copy_fn, n in turned[:1]:
+                copy_fn(n)
             for n in w_at.get(s, ()):
                 w_weave(n)
-            at(z_turns, z_step.get(s), 14)
-            for turn_fn, copy_fn, n in turned[:3]:
+            for turn_fn, copy_fn, n in turned[1:]:
                 copy_fn(n)
             for turn_fn, copy_fn, n in turned[3:]:
                 turn_fn(n)
@@ -380,6 +412,7 @@ def tile_siren_anchor_field_f4_kernel(tc, x_bytes, x_scale, w, b, freq1, amp, p,
         h_turn(29)
         z_turn(9)
         z_mm(12)
+        z_mm(13)
         y_sin(30)
         y_rest(31)
         h_amp(29)
@@ -389,49 +422,52 @@ def tile_siren_anchor_field_f4_kernel(tc, x_bytes, x_scale, w, b, freq1, amp, p,
         y_sin(31)
         z_out(9)
         z_turns(12)
+        z_rest(11)
         h_turn(30)
         h_turn(31)
         z_turn(10)
-        z_mm(13)
+        z_turn(11)
+        z_turns(13)
         h_amp(30)
         h_quant(29)
         h_amp(31)
         h_quant(30)
-        z_rest(11)
-        h_quant(31)
         z_round(12)
+        h_quant(31)
         z_out(10)
-        z_turns(13)
-        last_open(0)
-        last_close(0)
-        last_open(1)
-        last_close(1)
-        z_rest(12)
+        z_out(11)
+        last_pass(0, 0)
+        last_pass(0, 1)
+        last_pass(1, 0)
+        last_pass(1, 1)
+        last_pass(0, 2)
+        last_pass(0, 3)
+        last_pass(1, 2)
+        last_pass(1, 3)
         z_round(13)
-        z_turn(11)
+        z_rest(12)
+        z_rest(13)
         z_turn(12)
+        z_turn(13)
         z_turns(14)
         z_turns(15)
         z_turns(16)
         z_turns(17)
-        z_out(11)
         z_out(12)
-        z_rest(13)
         z_round(14)
         z_round(15)
+        z_round(16)
         z_rest(14)
-        z_turn(13)
-        z_out(13)
+        z_round(17)
         z_rest(15)
         z_turn(14)
-        z_out(14)
-        z_round(16)
-        z_round(17)
-        z_rest(16)
         z_turn(15)
-        z_out(15)
+        z_out(13)
+        z_rest(16)
         z_rest(17)
         z_turn(16)
-        z_out(16)
         z_turn(17)
+        z_out(14)
+        z_out(15)
+        z_out(16)
         z_out(17)

@@ -19,7 +19,18 @@ OP = mybir.AluOpType
 
 P = 128
 PACK = 4
+BANK = 512
 TWO_PI = 2.0 * math.pi
+
+UNITS = 32
+FIRST_TILES = 4
+ROUND_ON_VECTOR = 3
+HEAD_X_ROWS = 6
+HEAD_W_PIECES = 7
+P_QUANT_START = 9
+Z_START = 17
+Z_EVERY_STEP = 6
+Z_IN_LOOP = 12
 
 
 def tile_siren_anchor_field_f4_kernel(tc, x_bytes, x_scale, w, b, freq1, amp, p, c, freq2, out):
@@ -30,25 +41,26 @@ def tile_siren_anchor_field_f4_kernel(tc, x_bytes, x_scale, w, b, freq1, amp, p,
         psum = ctx.enter_context(tc.psum_pool(name="psum", bufs=1))
         ctx.enter_context(tc.manual_schedule())
 
-        xs_col = keep.tile([P, 2, PACK], F32, name="xs_col")
-        nc.sync.dma_start(out=xs_col[:], in_=x_scale.rearrange("o (g q t) -> q (o g) t", q=P, t=PACK))
         x_view = x_bytes.rearrange("(j q t) k -> j q t k", q=P, t=PACK)
         w_view = w.rearrange("(g q t) n -> g q t n", q=P, t=PACK)
         xb, wraw, praw = {}, {}, {}
 
-        def load_x(j, hf):
-            xb[j, hf] = keep.tile([P, 2, K], U8, name=f"xb{j}_{hf}", align_bytes=64)
-            nc.sync.dma_start(out=xb[j, hf][:], in_=x_view[j][:, 2 * hf : 2 * hf + 2, :])
+        def load_x(j, pair):
+            xb[j, pair] = keep.tile([P, 2, K], U8, name=f"xb{j}_{pair}", align_bytes=64)
+            nc.sync.dma_start(out=xb[j, pair][:], in_=x_view[j][:, 2 * pair : 2 * pair + 2, :])
 
-        def load_w(q):
+        def load_w(quarter):
             for g in range(2):
-                wraw[q, g] = keep.tile([P, PACK, 256], BF16, name=f"wraw{q}_{g}", align_bytes=64)
-                nc.sync.dma_start(out=wraw[q, g][:], in_=w_view[g][:, :, 256 * q : 256 * q + 256])
+                wraw[quarter, g] = keep.tile([P, PACK, 2 * P], BF16, name=f"wraw{quarter}_{g}", align_bytes=64)
+                nc.sync.dma_start(out=wraw[quarter, g][:], in_=w_view[g][:, :, 2 * P * quarter : 2 * P * (quarter + 1)])
 
-        def load_p(rt):
-            praw[rt] = keep.tile([P, M], BF16, name=f"praw{rt}", align_bytes=64)
-            nc.sync.dma_start(out=praw[rt][:], in_=p[rt * P : (rt + 1) * P, :])
+        def load_p(half):
+            for rt in range(4 * half, 4 * half + 4):
+                praw[rt] = keep.tile([P, M], BF16, name=f"praw{rt}", align_bytes=64)
+                nc.sync.dma_start(out=praw[rt][:], in_=p[rt * P : (rt + 1) * P, :])
 
+        scale_cols = keep.tile([P, 2, PACK], F32, name="scale_cols")
+        nc.sync.dma_start(out=scale_cols[:], in_=x_scale.rearrange("o (g q t) -> q (o g) t", q=P, t=PACK))
         load_x(0, 0)
         load_w(0)
         load_x(0, 1)
@@ -56,18 +68,12 @@ def tile_siren_anchor_field_f4_kernel(tc, x_bytes, x_scale, w, b, freq1, amp, p,
         load_x(1, 0)
         load_x(1, 1)
         load_p(0)
-        load_p(1)
-        load_p(2)
-        load_p(3)
         load_x(2, 0)
         load_x(2, 1)
         load_w(2)
         load_x(3, 0)
         load_x(3, 1)
-        load_p(4)
-        load_p(5)
-        load_p(6)
-        load_p(7)
+        load_p(1)
         load_w(3)
 
         ident = keep.tile([P, P], F32, name="ident")
@@ -76,8 +82,8 @@ def tile_siren_anchor_field_f4_kernel(tc, x_bytes, x_scale, w, b, freq1, amp, p,
         nc.vector.tensor_copy(out=ident_b[:], in_=ident[:])
         vrows = keep.tile([P, 2, P], BF16, name="vrows")
         nc.gpsimd.memset(vrows[:], 0.0)
-        for layer, (fr, bias) in enumerate(((freq1, b), (freq2, c))):
-            nc.gpsimd.dma_start(out=vrows[8 * layer : 8 * layer + 8, 0, :], in_=fr.rearrange("(i q) -> i q", q=P))
+        for layer, (freq, bias) in enumerate(((freq1, b), (freq2, c))):
+            nc.gpsimd.dma_start(out=vrows[8 * layer : 8 * layer + 8, 0, :], in_=freq.rearrange("(i q) -> i q", q=P))
             nc.gpsimd.dma_start(out=vrows[8 * layer : 8 * layer + 8, 1, :], in_=bias.rearrange("(i q) -> i q", q=P))
         amp_sb = keep.tile([P, 4, PACK], BF16, name="amp_sb")
         nc.gpsimd.dma_start(out=amp_sb[:], in_=amp.rearrange("(j q t) -> q j t", q=P, t=PACK))
@@ -86,121 +92,129 @@ def tile_siren_anchor_field_f4_kernel(tc, x_bytes, x_scale, w, b, freq1, amp, p,
         nc.vector.memset(warm[:], 0.0)
         nc.scalar.activation(out=warm[:], in_=warm[:], func=ACT.Sin)
 
-        xs_sc = keep.tile([P, 2, P, PACK], F32, name="xs_sc")
-        for g in range(2):
-            bank = psum.tile([P, PACK, P], F32, name="bank", tag="tx", bufs=3)
-            for t in range(PACK):
-                nc.tensor.transpose(bank[:, t, :], xs_col[:, g, t : t + 1].to_broadcast([P, P]), ident[:])
-            (nc.scalar.copy, nc.vector.tensor_copy)[g](out=xs_sc[:, g], in_=bank[:].rearrange("p t q -> p q t"))
-
+        scale_rows = keep.tile([P, 2, P, PACK], F32, name="scale_rows")
         turn = keep.tile([P, 2, 16], F32, name="turn")
         phase1 = keep.tile([P, 8], F32, name="phase1")
+        vcols = psum.tile([P, 2, P], BF16, name="vcols", tag="th", bufs=2)
+        banks = {}
 
-        vt = psum.tile([P, 2, P], BF16, name="vt", tag="th", bufs=2)
+        def spread_turn(g):
+            banks["s", g] = psum.tile([P, PACK, P], F32, name="bank", tag="tx", bufs=3)
+            for t in range(PACK):
+                nc.tensor.transpose(banks["s", g][:, t, :], scale_cols[:, g, t : t + 1].to_broadcast([P, P]), ident[:])
 
-        def channel_constants_a():
-            for a in range(2):
-                nc.tensor.transpose(vt[:, a, :], vrows[:, a, :], ident_b[:])
-            nc.scalar.activation(out=turn[:, 0, :], in_=vt[:, 0, 0:16], func=ACT.Copy, scale=1.0 / TWO_PI)
+        def spread_copy(g):
+            nc.scalar.copy(out=scale_rows[:, g], in_=banks["s", g][:].rearrange("p t q -> p q t"))
 
-        def channel_constants_b():
-            nc.vector.tensor_tensor(turn[:, 1, :], vt[:, 1, 0:16], turn[:, 0, :], OP.mult)
+        def freq_turns():
+            for slot in range(2):
+                nc.tensor.transpose(vcols[:, slot, :], vrows[:, slot, :], ident_b[:])
+            nc.scalar.activation(out=turn[:, 0, :], in_=vcols[:, 0, 0:16], func=ACT.Copy, scale=1.0 / TWO_PI)
 
-        def phase_constants():
+        def bias_turns():
+            nc.vector.tensor_tensor(turn[:, 1, :], vcols[:, 1, 0:16], turn[:, 0, :], OP.mult)
+
+        def bias_phase():
             nc.scalar.activation(out=phase1[:], in_=turn[:, 1, 0:8], func=ACT.Copy, scale=TWO_PI)
 
-        def planes(name, count, width):
+        def operand(name, count, width):
             codes = [keep.tile([P, width], U32, name=f"{name}c{a}", align_bytes=64) for a in range(count)]
             scales = [keep.tile([P, width], U8, name=f"{name}s{a}", align_bytes=64) for a in range(count)]
             return codes, scales
 
-        xq, xqs = planes("xq", 8, 512)
-        wq, wqs = planes("wq", 16, P)
-        pq, pqs = planes("pq", 8, 512)
-        hq, hqs = planes("hq", 32, P)
+        xq, xqs = operand("xq", 8, BANK)
+        wq, wqs = operand("wq", 16, P)
+        pq, pqs = operand("pq", 8, BANK)
+        hq, hqs = operand("hq", 32, P)
 
-        def quantize(codes, scales, src):
-            nc.vector.quantize_mx(out=codes[:].bitcast(FP8X4), scales=scales[:], in_=src)
+        def quantize(codes, scales, woven):
+            nc.vector.quantize_mx(out=codes.bitcast(FP8X4), scales=scales, in_=woven)
 
-        wi, xs, xi, pi, banks = {}, {}, {}, {}, {}
+        def shared(shape, dtype, name, slot):
+            return stage.tile(shape, dtype, name=name, tag=f"shared{slot % 3}", align_bytes=64, bufs=1)
+
+        w_woven, xs, x_woven, p_woven = {}, {}, {}, {}
+        w_before_round = 8
 
         def w_weave(n):
             i, g = divmod(n, 2)
-            if 6 <= n < 10:
-                wi[n] = stage.tile([P, P, PACK], BF16, name="wi", tag=f"kh{(n - 7) % 3}", align_bytes=64, bufs=1)
+            if n == w_before_round:
+                w_woven[n] = shared([P, P, PACK], BF16, "w_woven", ROUND_ON_VECTOR - 1)
             else:
-                wi[n] = stage.tile([P, P, PACK], BF16, name="wi", align_bytes=64, bufs=4)
+                w_woven[n] = stage.tile([P, P, PACK], BF16, name="w_woven", align_bytes=64, bufs=4)
             nc.scalar.copy(
-                out=wi[n][:].rearrange("p (a e) t -> p a t e", e=4),
+                out=w_woven[n][:].rearrange("p (a e) t -> p a t e", e=4),
                 in_=wraw[i // 2, g][:, :, P * (i % 2) : P * (i % 2) + P].rearrange("p t (a e) -> p a t e", e=4),
             )
 
         def w_quant(n):
-            quantize(wq[n], wqs[n], wi[n][:].rearrange("p n t -> p (n t)"))
+            quantize(wq[n][:], wqs[n][:], w_woven[n][:].rearrange("p n t -> p (n t)"))
 
-        def x_mult(n):
+        def x_mult(n, cols=slice(0, K)):
             j, t = divmod(n, 4)
-            xs[n] = stage.tile([P, K], BF16, name="xs", align_bytes=64, bufs=3)
+            if n not in xs:
+                xs[n] = stage.tile([P, K], BF16, name="xs", align_bytes=64, bufs=3)
             nc.vector.tensor_tensor(
-                xs[n][:], xb[j, t // 2][:, t % 2, :].bitcast(FP8), xs_sc[:].rearrange("p g q t -> p (g q t)"), OP.mult
+                xs[n][:, cols],
+                xb[j, t // 2][:, t % 2, cols].bitcast(FP8),
+                scale_rows[:].rearrange("p g q t -> p (g q t)")[:, cols],
+                OP.mult,
             )
 
-        def turn_words(key, words):
-            banks[key] = psum.tile([P, 2, 2, P], F32, name="bank", tag="tx", bufs=3)
-            for g in range(2):
-                for u in range(2):
-                    nc.tensor.transpose(banks[key][:, g, u, :], words[:, 256 * g + u : 256 * (g + 1) : 2], ident[:])
-
-        def copy_words(key, woven, slot):
-            dst = woven[:].bitcast(F32)[:, :, slot * P : (slot + 1) * P, :]
-            nc.scalar.copy(out=dst, in_=banks[key][:].rearrange("q g u r -> q g r u"))
+        def turn_pass(dst, words, g):
+            for u in range(2):
+                nc.tensor.transpose(dst[:, u, :], words[:, 256 * g + u : 256 * (g + 1) : 2], ident[:])
 
         def x_turn(n):
-            turn_words(("x", n), xs[n][:].bitcast(F32))
+            banks["x", n] = psum.tile([P, 2, 2, P], F32, name="bank", tag="tx", bufs=3)
+            for g in range(2):
+                turn_pass(banks["x", n][:, g], xs[n][:].bitcast(F32), g)
 
         def x_copy(n):
             j, t = divmod(n, 4)
             if t == 0:
-                xi[j] = stage.tile([P, 2, 512, PACK], BF16, name="xi", align_bytes=64, bufs=2)
-            copy_words(("x", n), xi[j], t)
+                x_woven[j] = stage.tile([P, 2, BANK, PACK], BF16, name="x_woven", align_bytes=64, bufs=2)
+            nc.scalar.copy(
+                out=x_woven[j][:].bitcast(F32)[:, :, t * P : (t + 1) * P, :],
+                in_=banks["x", n][:].rearrange("q g u r -> q g r u"),
+            )
 
         def x_quant(n):
-            quantize(xq[n], xqs[n], xi[n // 2][:, n % 2].rearrange("q m t -> q (m t)"))
+            quantize(xq[n][:], xqs[n][:], x_woven[n // 2][:, n % 2].rearrange("q m t -> q (m t)"))
 
         def p_turn(n):
             half, j, pair = n // 8, n // 2 % 4, n % 2
             banks["p", n] = psum.tile([P, 2, 2, P], F32, name="bank", tag="tx", bufs=3)
             for a in range(2):
-                words = praw[4 * half + 2 * pair + a][:].bitcast(F32)
-                for u in range(2):
-                    nc.tensor.transpose(banks["p", n][:, a, u, :], words[:, 256 * j + u : 256 * (j + 1) : 2], ident[:])
+                turn_pass(banks["p", n][:, a], praw[4 * half + 2 * pair + a][:].bitcast(F32), j)
 
         def p_copy(n):
             m, pair = divmod(n, 2)
             if m < 4:
-                pi[n] = stage.tile([P, 1024], BF16, name="pi", tag="o", align_bytes=64, bufs=8)[:]
+                p_woven[n] = stage.tile([P, 1024], BF16, name="p_woven", tag="o", align_bytes=64, bufs=8)[:]
             else:
                 if pair == 0:
-                    pi[m, "both"] = keep.tile([P, M], BF16, name=f"praw{m - 4}", align_bytes=64)
-                pi[n] = pi[m, "both"][:, 1024 * pair : 1024 * pair + 1024]
+                    p_woven[m, "both"] = keep.tile([P, M], BF16, name=f"praw{m - 4}", align_bytes=64)
+                p_woven[n] = p_woven[m, "both"][:, 1024 * pair : 1024 * pair + 1024]
             nc.scalar.copy(
-                out=pi[n].bitcast(F32).rearrange("q (a r u) -> q a r u", a=2, u=2),
+                out=p_woven[n].bitcast(F32).rearrange("q (a r u) -> q a r u", a=2, u=2),
                 in_=banks["p", n][:].rearrange("q a u r -> q a r u"),
             )
 
         def p_quant(n):
-            if n >= 8:
-                quantize(pq[n - 4], pqs[n - 4], pi[n - 4, "both"][:])
-            else:
+            if n < 8:
                 cols = slice(256 * (n % 2), 256 * (n % 2) + 256)
-                nc.vector.quantize_mx(out=pq[n // 2][:, cols].bitcast(FP8X4), scales=pqs[n // 2][:, cols], in_=pi[n])
+                quantize(pq[n // 2][:, cols], pqs[n // 2][:, cols], p_woven[n])
+            else:
+                quantize(pq[n - 4][:], pqs[n - 4][:], p_woven[n - 4, "both"][:])
 
-        units = [(i, j) for j in range(4) for i in range(4)] + [(i, j) for i in range(4, 8) for j in range(4)]
-        ys, us, ks, rs, ss, ths, his = {}, {}, {}, {}, {}, {}, {}
+        units = [(i, j) for j in range(4) for i in range(FIRST_TILES)]
+        units.extend((i, j) for i in range(FIRST_TILES, 8) for j in range(4))
+        ys, ks, rs, sines, turned_h, h_woven = {}, {}, {}, {}, {}, {}
 
         def y_mm(s):
             i, j = units[s]
-            ys[s] = psum.tile([P, 512], F32, name="y", tag="y", bufs=3)
+            ys[s] = psum.tile([P, BANK], F32, name="y", tag="y", bufs=3)
             for g in range(2):
                 nc.tensor.matmul_mx(
                     out=ys[s][:],
@@ -212,87 +226,87 @@ def tile_siren_anchor_field_f4_kernel(tc, x_bytes, x_scale, w, b, freq1, amp, p,
                     stop=(g == 1),
                 )
 
-        def y_turns(s):
-            i = units[s][0]
-            us[s] = stage.tile([P, 512], F32, name="u", bufs=3)
-            nc.scalar.activation(
-                out=us[s][:], in_=ys[s][:], func=ACT.Identity, scale=turn[:, 0, i : i + 1], bias=turn[:, 1, i : i + 1]
-            )
-
         def y_round(s):
-            ks[s] = stage.tile([P, 512], I32, name="k", tag=f"kh{(s - 1) % 3}", align_bytes=64, bufs=1)
-            nc.gpsimd.tensor_scalar(ks[s][:], us[s][:], 1.0, 0.0, OP.mult, OP.add)
-
-        def y_round_direct(s):
             i = units[s][0]
-            ks[s] = stage.tile([P, 512], I32, name="k", tag=f"kh{(s - 1) % 3}", align_bytes=64, bufs=1)
-            nc.vector.tensor_scalar(ks[s][:], ys[s][:], turn[:, 0, i : i + 1], turn[:, 1, i : i + 1], OP.mult, OP.add)
+            freq, bias = turn[:, 0, i : i + 1], turn[:, 1, i : i + 1]
+            if s < ROUND_ON_VECTOR:
+                ks[s] = shared([P, BANK], I32, "k", s - 1)
+                nc.vector.tensor_scalar(ks[s][:], ys[s][:], freq, bias, OP.mult, OP.add)
+            else:
+                u = stage.tile([P, BANK], F32, name="u", bufs=3)
+                nc.scalar.activation(out=u[:], in_=ys[s][:], func=ACT.Identity, scale=freq, bias=bias)
+                ks[s] = shared([P, BANK], I32, "k", s - 1)
+                nc.gpsimd.tensor_scalar(ks[s][:], u[:], 1.0, 0.0, OP.mult, OP.add)
 
         def y_rest(s):
             i = units[s][0]
-            rs[s] = stage.tile([P, 512], F32, name="r", bufs=3)
+            rs[s] = stage.tile([P, BANK], F32, name="r", bufs=3)
             nc.vector.scalar_tensor_tensor(rs[s][:], ys[s][:], turn[:, 0, i : i + 1], ks[s][:], OP.mult, OP.subtract)
 
         def y_sin(s):
             i = units[s][0]
-            ss[s] = stage.tile([P, 512], F32, name="s", bufs=3)
-            nc.scalar.activation(out=ss[s][:], in_=rs[s][:], func=ACT.Sin, scale=TWO_PI, bias=phase1[:, i : i + 1])
+            sines[s] = stage.tile([P, BANK], F32, name="sine", bufs=3)
+            nc.scalar.activation(out=sines[s][:], in_=rs[s][:], func=ACT.Sin, scale=TWO_PI, bias=phase1[:, i : i + 1])
 
         def h_turn(s):
-            ths[s] = psum.tile([P, PACK, P], F32, name="th", tag="th", bufs=2)
+            turned_h[s] = psum.tile([P, PACK, P], F32, name="th", tag="th", bufs=2)
             for t in range(PACK):
-                nc.tensor.transpose(ths[s][:, t, :], ss[s][:, t * P : (t + 1) * P], ident[:])
+                nc.tensor.transpose(turned_h[s][:, t, :], sines[s][:, t * P : (t + 1) * P], ident[:])
 
         def h_amp(s):
             j = units[s][1]
-            his[s] = stage.tile([P, P, PACK], BF16, name="hi", tag=f"kh{s % 3}", align_bytes=64, bufs=1)
+            h_woven[s] = shared([P, P, PACK], BF16, "h_woven", s)
             nc.vector.tensor_tensor(
-                his[s][:],
-                ths[s][:].rearrange("q t n -> q n t"),
+                h_woven[s][:],
+                turned_h[s][:].rearrange("q t n -> q n t"),
                 amp_sb[:, j, :].unsqueeze(1).to_broadcast([P, P, PACK]),
                 OP.mult,
             )
 
         def h_quant(s):
             i, j = units[s]
-            quantize(hq[4 * i + j], hqs[4 * i + j], his[s][:].rearrange("q n t -> q (n t)"))
+            quantize(hq[4 * i + j][:], hqs[4 * i + j][:], h_woven[s][:].rearrange("q n t -> q (n t)"))
 
-        z_tasks = [(i, r0, 512) for r0 in (0, 512) for i in range(4)]
-        z_tasks.extend((i, r0, 512) for i in range(4, 7) for r0 in (0, 512))
+        z_tasks = [(i, r0, BANK) for r0 in (0, BANK) for i in range(FIRST_TILES)]
+        z_tasks.extend((i, r0, BANK) for i in range(FIRST_TILES, 7) for r0 in (0, BANK))
+        quarters = range(len(z_tasks), len(z_tasks) + 4)
         z_tasks.extend((7, r0, 256) for r0 in range(0, R, 256))
-        zs, u2s, k2s, r2s, obs = {}, {}, {}, {}, {}
+        zs, u2s, k2s, r2s, turned_z, last_z = {}, {}, {}, {}, {}, {}
 
-        def z_passes(i, half, dst, chunks):
-            for j in chunks:
-                nc.tensor.matmul_mx(
-                    out=dst[:],
-                    lhsT=hq[4 * i + j][:].bitcast(FP8X4),
-                    lhsT_scale=hqs[4 * i + j][:],
-                    rhs=pq[4 * half + j][:].bitcast(FP8X4),
-                    rhs_scale=pqs[4 * half + j][:],
-                    start=(j == 0),
-                    stop=(j == 3),
-                )
+        def z_pass(i, half, dst, j):
+            nc.tensor.matmul_mx(
+                out=dst[:],
+                lhsT=hq[4 * i + j][:].bitcast(FP8X4),
+                lhsT_scale=hqs[4 * i + j][:],
+                rhs=pq[4 * half + j][:].bitcast(FP8X4),
+                rhs_scale=pqs[4 * half + j][:],
+                start=(j == 0),
+                stop=(j == 3),
+            )
 
         def z_mm(n):
             i, r0, width = z_tasks[n]
             zs[n] = psum.tile([P, width], F32, name="z", tag="tx", bufs=3)
-            z_passes(i, r0 // 512, zs[n], range(4))
+            for j in range(4):
+                z_pass(i, r0 // BANK, zs[n], j)
 
-        last = {}
-
-        def last_pass(half, j):
-            if j == 0:
-                last[half] = psum.tile([P, 512], F32, name="z", tag="y", bufs=3)
-            z_passes(7, half, last[half], range(j, j + 1))
-            for a in range(2):
-                zs[14 + 2 * half + a] = last[half][:, 256 * a : 256 * a + 256]
+        def last_passes(half, chunks):
+            if half not in last_z:
+                last_z[half] = psum.tile([P, BANK], F32, name="z", tag="y", bufs=3)
+                for a in range(2):
+                    zs[quarters[2 * half + a]] = last_z[half][:, 256 * a : 256 * a + 256]
+            for j in chunks:
+                z_pass(7, half, last_z[half], j)
 
         def z_turns(n):
-            i = 8 + z_tasks[n][0]
+            col = 8 + z_tasks[n][0]
             u2s[n] = stage.tile([P, z_tasks[n][2]], F32, name="u2", bufs=4)
             nc.scalar.activation(
-                out=u2s[n][:], in_=zs[n][:], func=ACT.Identity, scale=turn[:, 0, i : i + 1], bias=turn[:, 1, i : i + 1]
+                out=u2s[n][:],
+                in_=zs[n][:],
+                func=ACT.Identity,
+                scale=turn[:, 0, col : col + 1],
+                bias=turn[:, 1, col : col + 1],
             )
 
         def z_round(n):
@@ -305,110 +319,115 @@ def tile_siren_anchor_field_f4_kernel(tc, x_bytes, x_scale, w, b, freq1, amp, p,
 
         def z_turn(n):
             blocks = z_tasks[n][2] // P
-            if n in (14, 15):
-                obs[n] = psum.tile([P, blocks, P], F32, name="ob", tag="th", bufs=2)
+            if n in quarters[:2]:
+                turned_z[n] = psum.tile([P, blocks, P], F32, name="turned_z", tag="th", bufs=2)
             else:
-                obs[n] = psum.tile([P, blocks, P], F32, name="ob", tag="tx", bufs=3)
+                turned_z[n] = psum.tile([P, blocks, P], F32, name="turned_z", tag="tx", bufs=3)
             for a in range(blocks):
-                nc.tensor.transpose(obs[n][:, a, :], r2s[n][:, a * P : (a + 1) * P], ident[:])
+                nc.tensor.transpose(turned_z[n][:, a, :], r2s[n][:, a * P : (a + 1) * P], ident[:])
 
         def z_out(n):
             i, r0, width = z_tasks[n]
             o = stage.tile([P, width // P, P], F32, name="o", align_bytes=64, bufs=8)
-            nc.scalar.activation(out=o[:], in_=obs[n][:], func=ACT.Sin, scale=TWO_PI)
+            nc.scalar.activation(out=o[:], in_=turned_z[n][:], func=ACT.Sin, scale=TWO_PI)
             nc.sync.dma_start(
                 out=out[r0 : r0 + width, P * i : P * i + P].rearrange("(a q) n -> q a n", q=P),
                 in_=o[:],
             )
 
-        def at(fn, n, count):
-            if n is not None and 0 <= n < count:
-                fn(n)
-
-        x_mult(0)
-        w_weave(0)
-        w_weave(1)
-        w_weave(2)
+        for g in range(2):
+            spread_turn(g)
+        for g in range(2):
+            spread_copy(g)
+        for g in range(2):
+            x_mult(0, slice(BANK * g, BANK * g + BANK))
+        for n in range(3):
+            w_weave(n)
         x_turn(0)
         x_copy(0)
-        x_mult(1)
-        w_weave(3)
-        x_turn(1)
-        x_copy(1)
-        x_mult(2)
-        w_weave(4)
-        x_turn(2)
-        x_copy(2)
-        x_mult(3)
-        w_weave(5)
-        x_turn(3)
-        x_copy(3)
-        w_quant(0)
-        w_quant(1)
-        w_quant(2)
-        w_quant(3)
+        for n in range(1, 4):
+            x_mult(n)
+            w_weave(n + 2)
+            x_turn(n)
+            x_copy(n)
+        for n in range(4):
+            w_quant(n)
         x_mult(4)
-        channel_constants_a()
+        freq_turns()
         w_weave(6)
         x_turn(4)
         x_copy(4)
         x_mult(5)
         x_turn(5)
         x_quant(0)
-        channel_constants_b()
+        bias_turns()
         x_quant(1)
-        phase_constants()
+        bias_phase()
         x_copy(5)
         w_quant(4)
         w_quant(5)
-        z_step = {step: n for n, step in enumerate([17 + n + n // 3 for n in range(12)])}
-        x_at = {1: (6, 7), **{s: (s + 6,) for s in range(2, 10)}}
-        xq_at = {2: (2,), 3: (3,), 6: (4,), 7: (5,), 10: (6,), 11: (7,)}
-        p_at = {0: (0,), 1: (1,), 2: (2,), 3: (3, 4), 4: (5,), 5: (6,), 6: (7, 8), 7: (9,), 8: (10,), 9: (11,), 10: (12,), 11: (13,), 12: (14,), 13: (15,)}
-        pq_at = {9: (0,), 12: (1, 2), 13: (3, 4), 14: (5,), 15: (6,), 16: (7,), 17: (8,), 18: (9,), 20: (10,), 21: (11,)}
-        w_at = {0: (7,), 1: (8,), 2: (9,), 14: (10,), 15: (11,), 16: (12,), 20: (13,), 24: (14,), 25: (15,)}
-        for s in range(0, 32):
+
+        def by_step(step_of, tasks):
+            table = {}
+            for n in tasks:
+                table.setdefault(step_of(n), []).append(n)
+            return table
+
+        x_at = by_step(lambda n: max(1, n - HEAD_X_ROWS), range(HEAD_X_ROWS, 16))
+        xq_at = by_step(lambda n: FIRST_TILES * (n // 2) - 2 + n % 2, range(2, 8))
+        p_at = by_step(lambda n: 2 * (n // 3) + n % 3 // 2 if n < 8 else n - 3, range(16))
+        pq_at = by_step(lambda n: P_QUANT_START + n, range(12))
+        w_at = by_step(lambda n: 4 * (n // 2) - 5 + n % 2, range(w_before_round + 1, 16))
+        w_at[0] = [HEAD_W_PIECES]
+        w_at[ROUND_ON_VECTOR - 1] = [w_before_round]
+        late = [Z_START + Z_EVERY_STEP + 1 + 3 * (a // 2) + a % 2 for a in range(Z_IN_LOOP - Z_EVERY_STEP)]
+        z_at = by_step(lambda n: Z_START + n if n < Z_EVERY_STEP else late[n - Z_EVERY_STEP], range(Z_IN_LOOP))
+
+        def each(fn, tasks):
+            for n in tasks:
+                fn(n)
+
+        def unit(lag):
+            return [s - lag] if s >= lag else []
+
+        for s in range(UNITS):
+            turns = [(x_turn, x_copy, n) for n in x_at.get(s, [])] + [(p_turn, p_copy, n) for n in p_at.get(s, [])]
             y_mm(s)
-            at(z_mm, z_step.get(s), 14)
-            at(h_turn, s - 3, 32)
-            at(z_turn, z_step.get(s - 3), 14)
-            turned = [(x_turn, x_copy, n) for n in x_at.get(s, ())] + [(p_turn, p_copy, n) for n in p_at.get(s, ())]
-            for turn_fn, copy_fn, n in turned[:3]:
+            each(z_mm, z_at.get(s, []))
+            each(h_turn, unit(3))
+            each(z_turn, z_at.get(s - 4, []))
+            for turn_fn, copy_fn, n in turns:
                 turn_fn(n)
-            two_port = []
-            if s - 1 in z_step:
-                two_port.append((z_round, z_step[s - 1]))
+
+            ported = [(z_round, n) for n in z_at.get(s - 2, [])]
+            ported.extend((w_quant, n) for n in w_at.get(s - 2, []) if n > w_before_round)
+            ported.extend((x_quant, n) for n in xq_at.get(s, []))
+            ported.extend((p_quant, n) for n in pq_at.get(s, []))
+            ported.extend((z_rest, n) for n in z_at.get(s - 3, []))
+            ported.extend((x_mult, n) for n in x_at.get(s + 1, []))
             if s >= 4:
-                two_port.extend((w_quant, n) for n in w_at.get(s - 2, ()) if n >= 10)
-            two_port.extend((x_quant, n) for n in xq_at.get(s, ()))
-            two_port.extend((p_quant, n) for n in pq_at.get(s, ()))
-            if s - 2 in z_step:
-                two_port.append((z_rest, z_step[s - 2]))
-            two_port.extend((x_mult, n) for n in x_at.get(s + 1, ()))
-            for fn, n in two_port[:-1]:
-                fn(n)
-            if s >= 4:
-                h_quant(s - 4)
+                frees_round = [(h_quant, s - 4)]
+            elif s == ROUND_ON_VECTOR:
+                frees_round = [(w_quant, w_before_round)]
             else:
-                w_quant(s + 6)
-            for fn, n in two_port[-1:]:
+                frees_round = [(w_quant, n) for n in range(HEAD_W_PIECES - 1, HEAD_W_PIECES + 1) if n == s + 6]
+            place = len(ported) - 1 if len(ported) > 1 or s < 4 else len(ported)
+            for fn, n in ported[:place] + frees_round + ported[place:]:
                 fn(n)
-            y_turns(s)
+
             y_round(s)
-            at(y_sin, s - 2, 32)
-            at(h_amp, s - 3, 32)
-            at(y_rest, s - 1, 32)
-            at(z_turns, z_step.get(s), 14)
-            for turn_fn, copy_fn, n in turned[:1]:
+            each(y_sin, unit(2))
+            each(y_rest, unit(1))
+            each(h_amp, unit(3))
+            each(z_turns, z_at.get(s, []))
+            for turn_fn, copy_fn, n in turns[:1]:
                 copy_fn(n)
-            for n in w_at.get(s, ()):
-                w_weave(n)
-            for turn_fn, copy_fn, n in turned[1:]:
+            each(w_weave, w_at.get(s, []))
+            for turn_fn, copy_fn, n in turns[1:]:
                 copy_fn(n)
-            for turn_fn, copy_fn, n in turned[3:]:
-                turn_fn(n)
-                copy_fn(n)
-            at(z_out, z_step.get(s - 3), 14)
+            each(z_out, z_at.get(s - 4, []))
+
+        z_round(10)
         h_turn(29)
         z_turn(9)
         z_mm(12)
@@ -423,10 +442,8 @@ def tile_siren_anchor_field_f4_kernel(tc, x_bytes, x_scale, w, b, freq1, amp, p,
         z_out(9)
         z_turns(12)
         z_rest(11)
-        h_turn(30)
-        h_turn(31)
-        z_turn(10)
-        z_turn(11)
+        each(h_turn, (30, 31))
+        each(z_turn, (10, 11))
         z_turns(13)
         h_amp(30)
         h_quant(29)
@@ -434,40 +451,21 @@ def tile_siren_anchor_field_f4_kernel(tc, x_bytes, x_scale, w, b, freq1, amp, p,
         h_quant(30)
         z_round(12)
         h_quant(31)
-        z_out(10)
-        z_out(11)
-        last_pass(0, 0)
-        last_pass(0, 1)
-        last_pass(1, 0)
-        last_pass(1, 1)
-        last_pass(0, 2)
-        last_pass(0, 3)
-        last_pass(1, 2)
-        last_pass(1, 3)
+        each(z_out, (10, 11))
+        for chunks in ((0, 1), (2, 3)):
+            for half in range(2):
+                last_passes(half, chunks)
         z_round(13)
-        z_rest(12)
-        z_rest(13)
-        z_turn(12)
-        z_turn(13)
-        z_turns(14)
-        z_turns(15)
-        z_turns(16)
-        z_turns(17)
+        each(z_rest, (12, 13))
+        each(z_turn, (12, 13))
+        each(z_turns, quarters)
         z_out(12)
-        z_round(14)
-        z_round(15)
-        z_round(16)
-        z_rest(14)
-        z_round(17)
-        z_rest(15)
-        z_turn(14)
-        z_turn(15)
+        each(z_round, quarters[:3])
+        z_rest(quarters[0])
+        z_round(quarters[3])
+        z_rest(quarters[1])
+        each(z_turn, quarters[:2])
         z_out(13)
-        z_rest(16)
-        z_rest(17)
-        z_turn(16)
-        z_turn(17)
-        z_out(14)
-        z_out(15)
-        z_out(16)
-        z_out(17)
+        each(z_rest, quarters[2:])
+        each(z_turn, quarters[2:])
+        each(z_out, quarters)

@@ -59,12 +59,28 @@ def tile_siren_anchor_field_f4_kernel(tc, x_bytes, x_scale, w, b, freq1, amp, p,
                 praw[rt] = keep.tile([P, M], BF16, name=f"praw{rt}", align_bytes=64)
                 nc.sync.dma_start(out=praw[rt][:], in_=p[rt * P : (rt + 1) * P, :])
 
-        scale_cols = keep.tile([P, 2, PACK], F32, name="scale_cols")
-        nc.sync.dma_start(out=scale_cols[:], in_=x_scale.rearrange("o (g q t) -> q (o g) t", q=P, t=PACK))
+
+        warm = keep.tile([P, 1], F32, name="warm")
+        nc.vector.memset(warm[:], 0.0)
+        nc.scalar.activation(out=warm[:], in_=warm[:], func=ACT.Sin)
+
+        ident = keep.tile([P, P], F32, name="ident")
+        nc.vector.memset(ident[:], 0.0)
+        make_identity(nc, ident[:], nomemset=True)
+
+        scale_cols = keep.tile([P, 2, 2 * PACK], F32, name="scale_cols")
+        nc.sync.dma_start(out=scale_cols[:, :, 0:PACK], in_=x_scale.rearrange("o (g q t) -> q (o g) t", q=P, t=PACK))
         load_x(0, 0)
         load_w(0)
         load_x(0, 1)
         load_w(1)
+        vrows = keep.tile([P, 2, P], BF16, name="vrows")
+        nc.vector.memset(vrows[:], 0.0)
+        for layer, (freq, bias) in enumerate(((freq1, b), (freq2, c))):
+            nc.sync.dma_start(out=vrows[8 * layer : 8 * layer + 8, 0, :], in_=freq.rearrange("(i q) -> i q", q=P))
+            nc.sync.dma_start(out=vrows[8 * layer : 8 * layer + 8, 1, :], in_=bias.rearrange("(i q) -> i q", q=P))
+        amp_sb = keep.tile([P, 4, PACK], BF16, name="amp_sb")
+        nc.sync.dma_start(out=amp_sb[:], in_=amp.rearrange("(j q t) -> q j t", q=P, t=PACK))
         load_x(1, 0)
         load_x(1, 1)
         load_p(0)
@@ -76,22 +92,8 @@ def tile_siren_anchor_field_f4_kernel(tc, x_bytes, x_scale, w, b, freq1, amp, p,
         load_p(1)
         load_w(3)
 
-        ident = keep.tile([P, P], F32, name="ident")
-        make_identity(nc, ident[:])
         ident_b = keep.tile([P, P], BF16, name="ident_b")
         nc.vector.tensor_copy(out=ident_b[:], in_=ident[:])
-        vrows = keep.tile([P, 2, P], BF16, name="vrows")
-        nc.gpsimd.memset(vrows[:], 0.0)
-        for layer, (freq, bias) in enumerate(((freq1, b), (freq2, c))):
-            nc.gpsimd.dma_start(out=vrows[8 * layer : 8 * layer + 8, 0, :], in_=freq.rearrange("(i q) -> i q", q=P))
-            nc.gpsimd.dma_start(out=vrows[8 * layer : 8 * layer + 8, 1, :], in_=bias.rearrange("(i q) -> i q", q=P))
-        amp_sb = keep.tile([P, 4, PACK], BF16, name="amp_sb")
-        nc.gpsimd.dma_start(out=amp_sb[:], in_=amp.rearrange("(j q t) -> q j t", q=P, t=PACK))
-
-        warm = keep.tile([P, 1], F32, name="warm")
-        nc.vector.memset(warm[:], 0.0)
-        nc.scalar.activation(out=warm[:], in_=warm[:], func=ACT.Sin)
-
         scale_rows = keep.tile([P, 2, P, PACK], F32, name="scale_rows")
         turn = keep.tile([P, 2, 16], F32, name="turn")
         phase1 = keep.tile([P, 8], F32, name="phase1")

@@ -22,43 +22,41 @@ PACK = 4
 BANK = 512
 TWO_PI = 2.0 * math.pi
 
-UNITS = 32
-FIRST_TILES = 4
-ROUND_ON_VECTOR = 3
-HEAD_X_ROWS = 6
-HEAD_W_PIECES = 7
-P_QUANT_START = 9
-Z_START = 17
-Z_EVERY_STEP = 6
-Z_IN_LOOP = 12
-
 
 def tile_siren_anchor_field_f4_kernel(tc, x_bytes, x_scale, w, b, freq1, amp, p, c, freq2, out):
     nc = tc.nc
     with ExitStack() as ctx:
         keep = ctx.enter_context(tc.tile_pool(name="keep", bufs=1))
-        stage = ctx.enter_context(tc.tile_pool(name="stage", bufs=2))
         psum = ctx.enter_context(tc.psum_pool(name="psum", bufs=1))
         ctx.enter_context(tc.manual_schedule())
+
+        def buf(tag, shape, dtype):
+            return keep.tile(shape, dtype, name=tag, tag=tag, align_bytes=64)
+
+        def bank(number, shape, dtype=F32):
+            return psum.tile(shape, dtype, name=f"bank{number}", tag=f"bank{number}")
 
         x_view = x_bytes.rearrange("(j q t) k -> j q t k", q=P, t=PACK)
         w_view = w.rearrange("(g q t) n -> g q t n", q=P, t=PACK)
         xb, wraw, praw = {}, {}, {}
 
-        def load_x(j, pair):
-            xb[j, pair] = keep.tile([P, 2, K], U8, name=f"xb{j}_{pair}", align_bytes=64)
-            nc.sync.dma_start(out=xb[j, pair][:], in_=x_view[j][:, 2 * pair : 2 * pair + 2, :])
+        def load_x(j, rows):
+            part = buf(f"xb{j}_{rows.start}", [P, len(rows), K], U8)
+            nc.sync.dma_start(out=part[:], in_=x_view[j][:, rows.start : rows.stop, :])
+            for t in rows:
+                xb[PACK * j + t] = part[:, t - rows.start, :]
 
-        def load_w(quarter):
+        def load_w(tiles):
+            part = buf(f"wraw{tiles.start}", [P, 2, PACK, P * len(tiles)], BF16)
             for g in range(2):
-                wraw[quarter, g] = keep.tile([P, PACK, 2 * P], BF16, name=f"wraw{quarter}_{g}", align_bytes=64)
-                nc.sync.dma_start(out=wraw[quarter, g][:], in_=w_view[g][:, :, 2 * P * quarter : 2 * P * (quarter + 1)])
+                nc.sync.dma_start(out=part[:, g], in_=w_view[g][:, :, P * tiles.start : P * tiles.stop])
+            for i in tiles:
+                wraw[i] = part[:, :, :, P * (i - tiles.start) : P * (i - tiles.start + 1)]
 
-        def load_p(half):
-            for rt in range(4 * half, 4 * half + 4):
-                praw[rt] = keep.tile([P, M], BF16, name=f"praw{rt}", align_bytes=64)
+        def load_p(row_tiles):
+            for rt in row_tiles:
+                praw[rt] = buf(f"praw{rt}", [P, M], BF16)
                 nc.sync.dma_start(out=praw[rt][:], in_=p[rt * P : (rt + 1) * P, :])
-
 
         warm = keep.tile([P, 1], F32, name="warm")
         nc.vector.memset(warm[:], 0.0)
@@ -70,10 +68,10 @@ def tile_siren_anchor_field_f4_kernel(tc, x_bytes, x_scale, w, b, freq1, amp, p,
 
         scale_cols = keep.tile([P, 2, 2 * PACK], F32, name="scale_cols")
         nc.sync.dma_start(out=scale_cols[:, :, 0:PACK], in_=x_scale.rearrange("o (g q t) -> q (o g) t", q=P, t=PACK))
-        load_x(0, 0)
-        load_w(0)
-        load_x(0, 1)
-        load_w(1)
+        load_x(0, range(0, 2))
+        load_w(range(0, 3))
+        load_x(0, range(2, 4))
+        load_x(1, range(0, 4))
         vrows = keep.tile([P, 2, P], BF16, name="vrows")
         nc.vector.memset(vrows[:], 0.0)
         for layer, (freq, bias) in enumerate(((freq1, b), (freq2, c))):
@@ -81,393 +79,473 @@ def tile_siren_anchor_field_f4_kernel(tc, x_bytes, x_scale, w, b, freq1, amp, p,
             nc.sync.dma_start(out=vrows[8 * layer : 8 * layer + 8, 1, :], in_=bias.rearrange("(i q) -> i q", q=P))
         amp_sb = keep.tile([P, 4, PACK], BF16, name="amp_sb")
         nc.sync.dma_start(out=amp_sb[:], in_=amp.rearrange("(j q t) -> q j t", q=P, t=PACK))
-        load_x(1, 0)
-        load_x(1, 1)
-        load_p(0)
-        load_x(2, 0)
-        load_x(2, 1)
-        load_w(2)
-        load_x(3, 0)
-        load_x(3, 1)
-        load_p(1)
-        load_w(3)
+        load_p(range(0, 2))
+        load_x(2, range(0, 4))
+        load_p(range(2, 4))
+        load_w(range(3, 8))
+        load_x(3, range(0, 4))
+        load_p(range(4, 8))
 
         ident_b = keep.tile([P, P], BF16, name="ident_b")
         nc.vector.tensor_copy(out=ident_b[:], in_=ident[:])
-        scale_rows = keep.tile([P, 2, P, PACK], F32, name="scale_rows")
+
         turn = keep.tile([P, 2, 16], F32, name="turn")
         phase1 = keep.tile([P, 8], F32, name="phase1")
-        vcols = psum.tile([P, 2, P], BF16, name="vcols", tag="th", bufs=2)
-        banks = {}
+        scale_rows = buf("scale_rows", [P, 2, P, PACK], F32)
 
-        def spread_turn(g):
-            banks["s", g] = psum.tile([P, PACK, P], F32, name="bank", tag="tx", bufs=3)
+        def spread_scales(g):
+            spread = bank(2 + g, [P, PACK, P])
             for t in range(PACK):
-                nc.tensor.transpose(banks["s", g][:, t, :], scale_cols[:, g, t : t + 1].to_broadcast([P, P]), ident[:])
+                nc.tensor.transpose(spread[:, t, :], scale_cols[:, g, t : t + 1].to_broadcast([P, P]), ident[:])
+            nc.scalar.copy(out=scale_rows[:, g], in_=spread[:].rearrange("p t q -> p q t"))
 
-        def spread_copy(g):
-            nc.scalar.copy(out=scale_rows[:, g], in_=banks["s", g][:].rearrange("p t q -> p q t"))
+        vcols = bank(0, [P, 2, P], BF16)
 
-        def freq_turns():
-            for slot in range(2):
-                nc.tensor.transpose(vcols[:, slot, :], vrows[:, slot, :], ident_b[:])
-            nc.scalar.activation(out=turn[:, 0, :], in_=vcols[:, 0, 0:16], func=ACT.Copy, scale=1.0 / TWO_PI)
-
-        def bias_turns():
-            nc.vector.tensor_tensor(turn[:, 1, :], vcols[:, 1, 0:16], turn[:, 0, :], OP.mult)
-
-        def bias_phase():
-            nc.scalar.activation(out=phase1[:], in_=turn[:, 1, 0:8], func=ACT.Copy, scale=TWO_PI)
+        def channel_constants(part):
+            if part == 0:
+                for slot in range(2):
+                    nc.tensor.transpose(vcols[:, slot, :], vrows[:, slot, :], ident_b[:])
+                nc.scalar.activation(out=turn[:, 0, :], in_=vcols[:, 0, 0:16], func=ACT.Copy, scale=1.0 / TWO_PI)
+            else:
+                nc.vector.tensor_tensor(turn[:, 1, :], vcols[:, 1, 0:16], turn[:, 0, :], OP.mult)
+                nc.scalar.activation(out=phase1[:], in_=turn[:, 1, 0:8], func=ACT.Copy, scale=TWO_PI)
 
         def operand(name, count, width):
-            codes = [keep.tile([P, width], U32, name=f"{name}c{a}", align_bytes=64) for a in range(count)]
-            scales = [keep.tile([P, width], U8, name=f"{name}s{a}", align_bytes=64) for a in range(count)]
+            codes = [buf(f"{name}c{a}", [P, width], U32) for a in range(count)]
+            scales = [buf(f"{name}s{a}", [P, width], U8) for a in range(count)]
             return codes, scales
 
         xq, xqs = operand("xq", 8, BANK)
-        wq, wqs = operand("wq", 16, P)
+        wq, wqs = operand("wq", 8, 2 * P)
         pq, pqs = operand("pq", 8, BANK)
-        hq, hqs = operand("hq", 32, P)
+        hq, hqs = operand("hq", 16, 2 * P)
 
         def quantize(codes, scales, woven):
             nc.vector.quantize_mx(out=codes.bitcast(FP8X4), scales=scales, in_=woven)
 
-        def shared(shape, dtype, name, slot):
-            return stage.tile(shape, dtype, name=name, tag=f"shared{slot % 3}", align_bytes=64, bufs=1)
+        def product(dst, lhs, lhs_scale, rhs, rhs_scale, first, last):
+            nc.tensor.matmul_mx(
+                out=dst, lhsT=lhs.bitcast(FP8X4), lhsT_scale=lhs_scale, rhs=rhs.bitcast(FP8X4), rhs_scale=rhs_scale,
+                start=first, stop=last,
+            )
 
-        w_woven, xs, x_woven, p_woven = {}, {}, {}, {}
-        w_before_round = 8
+        w_woven = {}
+        w_slot = {0: "ww0", 1: "ww1", 2: "k1", 3: "ww0", 4: "ww1", 5: "ww2", 6: "ww3", 7: "ww4"}
 
-        def w_weave(n):
-            i, g = divmod(n, 2)
-            if n == w_before_round:
-                w_woven[n] = shared([P, P, PACK], BF16, "w_woven", ROUND_ON_VECTOR - 1)
-            else:
-                w_woven[n] = stage.tile([P, P, PACK], BF16, name="w_woven", align_bytes=64, bufs=4)
+        def woven_w(n):
+            if n not in w_woven:
+                w_woven[n] = buf(w_slot[n], [P, 2, P, PACK], BF16)
+            return w_woven[n]
+
+        def w_weave(n, g):
             nc.scalar.copy(
-                out=w_woven[n][:].rearrange("p (a e) t -> p a t e", e=4),
-                in_=wraw[i // 2, g][:, :, P * (i % 2) : P * (i % 2) + P].rearrange("p t (a e) -> p a t e", e=4),
+                out=woven_w(n)[:, g].rearrange("p (a e) t -> p a t e", e=4),
+                in_=wraw[n][:, g].rearrange("p t (a e) -> p a t e", e=4),
+            )
+
+        def w_weave_late(n, g):
+            nc.gpsimd.tensor_scalar(woven_w(n)[:, g], wraw[n][:, g].rearrange("p t n -> p n t"), 1.0, 0.0, OP.mult, OP.add)
+
+        def w_weave_last(n, g):
+            nc.vector.tensor_copy(
+                out=woven_w(n)[:, g].rearrange("p (a e) t -> p a t e", e=4),
+                in_=wraw[n][:, g].rearrange("p t (a e) -> p a t e", e=4),
             )
 
         def w_quant(n):
-            quantize(wq[n][:], wqs[n][:], w_woven[n][:].rearrange("p n t -> p (n t)"))
+            quantize(wq[n][:], wqs[n][:], w_woven[n][:].rearrange("p g n t -> p (g n t)"))
+
+        xs, x_woven, p_woven, turned = {}, {}, {}, {}
 
         def x_mult(n, cols=slice(0, K)):
-            j, t = divmod(n, 4)
             if n not in xs:
-                xs[n] = stage.tile([P, K], BF16, name="xs", align_bytes=64, bufs=3)
+                xs[n] = buf(f"xs{n % 3}", [P, K], BF16)
             nc.vector.tensor_tensor(
-                xs[n][:, cols],
-                xb[j, t // 2][:, t % 2, cols].bitcast(FP8),
-                scale_rows[:].rearrange("p g q t -> p (g q t)")[:, cols],
-                OP.mult,
+                xs[n][:, cols], xb[n][:, cols].bitcast(FP8), scale_rows[:].rearrange("p g q t -> p (g q t)")[:, cols], OP.mult
             )
 
         def turn_pass(dst, words, g):
             for u in range(2):
                 nc.tensor.transpose(dst[:, u, :], words[:, 256 * g + u : 256 * (g + 1) : 2], ident[:])
 
-        def x_turn(n):
-            banks["x", n] = psum.tile([P, 2, 2, P], F32, name="bank", tag="tx", bufs=3)
+        def x_turn(n, number):
+            turned["x", n] = bank(number, [P, 2, 2, P])
             for g in range(2):
-                turn_pass(banks["x", n][:, g], xs[n][:].bitcast(F32), g)
+                turn_pass(turned["x", n][:, g], xs[n][:].bitcast(F32), g)
 
         def x_copy(n):
             j, t = divmod(n, 4)
             if t == 0:
-                x_woven[j] = stage.tile([P, 2, BANK, PACK], BF16, name="x_woven", align_bytes=64, bufs=2)
+                x_woven[j] = buf(f"xw{j % 2}", [P, 2, BANK, PACK], BF16)
             nc.scalar.copy(
                 out=x_woven[j][:].bitcast(F32)[:, :, t * P : (t + 1) * P, :],
-                in_=banks["x", n][:].rearrange("q g u r -> q g r u"),
+                in_=turned["x", n][:].rearrange("q g u r -> q g r u"),
             )
 
         def x_quant(n):
             quantize(xq[n][:], xqs[n][:], x_woven[n // 2][:, n % 2].rearrange("q m t -> q (m t)"))
 
-        def p_turn(n):
-            half, j, pair = n // 8, n // 2 % 4, n % 2
-            banks["p", n] = psum.tile([P, 2, 2, P], F32, name="bank", tag="tx", bufs=3)
+        p_slot = ["pw0", "pw1", "pw2", "pw3", "praw0", "praw1", "praw2", "praw3"]
+
+        def p_turn(n, number):
+            m, pair = divmod(n, 2)
+            turned["p", n] = bank(number, [P, 2, 2, P])
             for a in range(2):
-                turn_pass(banks["p", n][:, a], praw[4 * half + 2 * pair + a][:].bitcast(F32), j)
+                turn_pass(turned["p", n][:, a], praw[4 * (m // 4) + 2 * pair + a][:].bitcast(F32), m % 4)
 
         def p_copy(n):
             m, pair = divmod(n, 2)
-            if m < 4:
-                p_woven[n] = stage.tile([P, 1024], BF16, name="p_woven", tag="o", align_bytes=64, bufs=8)[:]
-            else:
-                if pair == 0:
-                    p_woven[m, "both"] = keep.tile([P, M], BF16, name=f"praw{m - 4}", align_bytes=64)
-                p_woven[n] = p_woven[m, "both"][:, 1024 * pair : 1024 * pair + 1024]
+            if pair == 0:
+                p_woven[m] = buf(p_slot[m], [P, M], BF16)
             nc.scalar.copy(
-                out=p_woven[n].bitcast(F32).rearrange("q (a r u) -> q a r u", a=2, u=2),
-                in_=banks["p", n][:].rearrange("q a u r -> q a r u"),
+                out=p_woven[m][:, 1024 * pair : 1024 * pair + 1024].bitcast(F32).rearrange("q (a r u) -> q a r u", a=2, u=2),
+                in_=turned["p", n][:].rearrange("q a u r -> q a r u"),
             )
 
-        def p_quant(n):
-            if n < 8:
-                cols = slice(256 * (n % 2), 256 * (n % 2) + 256)
-                quantize(pq[n // 2][:, cols], pqs[n // 2][:, cols], p_woven[n])
-            else:
-                quantize(pq[n - 4][:], pqs[n - 4][:], p_woven[n - 4, "both"][:])
+        def p_quant(m):
+            quantize(pq[m][:], pqs[m][:], p_woven[m][:])
 
-        units = [(i, j) for j in range(4) for i in range(FIRST_TILES)]
-        units.extend((i, j) for i in range(FIRST_TILES, 8) for j in range(4))
-        ys, ks, rs, sines, turned_h, h_woven = {}, {}, {}, {}, {}, {}
+        pairs = [(i, cp) for cp in range(2) for i in range(3)]
+        pairs.extend((i, cp) for i in range(3, 8) for cp in range(2))
+        ys, us, ks, turned_h, h_woven = {}, {}, {}, {}, {}
 
-        def y_mm(s):
-            i, j = units[s]
-            ys[s] = psum.tile([P, BANK], F32, name="y", tag="y", bufs=3)
-            for g in range(2):
-                nc.tensor.matmul_mx(
-                    out=ys[s][:],
-                    lhsT=wq[2 * i + g][:].bitcast(FP8X4),
-                    lhsT_scale=wqs[2 * i + g][:],
-                    rhs=xq[2 * j + g][:].bitcast(FP8X4),
-                    rhs_scale=xqs[2 * j + g][:],
-                    start=(g == 0),
-                    stop=(g == 1),
+        def turns_tile(s):
+            if s not in us:
+                us[s] = buf("u4" if s == 2 else f"u{s % 4}", [P, 2, BANK], F32)
+            return us[s]
+
+        def y_mm(s, units=range(2)):
+            i, cp = pairs[s]
+            for a in units:
+                ys[s, a] = bank(2 * ((s + 1) % 2) + a, [P, BANK])
+                for g in range(2):
+                    cols = slice(P * g, P * g + P)
+                    n = 2 * (2 * cp + a) + g
+                    product(ys[s, a][:], wq[i][:, cols], wqs[i][:, cols], xq[n][:], xqs[n][:], g == 0, g == 1)
+
+        def y_turns(s, units=range(2)):
+            i = pairs[s][0]
+            for a in units:
+                nc.scalar.activation(
+                    out=turns_tile(s)[:, a, :], in_=ys[s, a][:], func=ACT.Identity,
+                    scale=turn[:, 0, i : i + 1], bias=turn[:, 1, i : i + 1],
                 )
 
-        def y_round(s):
-            i = units[s][0]
-            freq, bias = turn[:, 0, i : i + 1], turn[:, 1, i : i + 1]
-            if s < ROUND_ON_VECTOR:
-                ks[s] = shared([P, BANK], I32, "k", s - 1)
-                nc.vector.tensor_scalar(ks[s][:], ys[s][:], freq, bias, OP.mult, OP.add)
-            else:
-                u = stage.tile([P, BANK], F32, name="u", bufs=3)
-                nc.scalar.activation(out=u[:], in_=ys[s][:], func=ACT.Identity, scale=freq, bias=bias)
-                ks[s] = shared([P, BANK], I32, "k", s - 1)
-                nc.gpsimd.tensor_scalar(ks[s][:], u[:], 1.0, 0.0, OP.mult, OP.add)
+        def rounding(s, tag):
+            ks[s] = buf(tag, [P, 2, BANK], I32)
+            nc.gpsimd.tensor_scalar(ks[s][:], us[s][:], 1.0, 0.0, OP.mult, OP.add)
 
-        def y_rest(s):
-            i = units[s][0]
-            rs[s] = stage.tile([P, BANK], F32, name="r", bufs=3)
-            nc.vector.scalar_tensor_tensor(rs[s][:], ys[s][:], turn[:, 0, i : i + 1], ks[s][:], OP.mult, OP.subtract)
+        def y_round(s, tag):
+            i = pairs[s][0]
+            ks[s] = buf(tag, [P, 2, BANK], I32)
+            for a in range(2):
+                nc.vector.tensor_scalar(
+                    ks[s][:, a, :], ys[s, a][:], turn[:, 0, i : i + 1], turn[:, 1, i : i + 1], OP.mult, OP.add
+                )
 
-        def y_sin(s):
-            i = units[s][0]
-            sines[s] = stage.tile([P, BANK], F32, name="sine", bufs=3)
-            nc.scalar.activation(out=sines[s][:], in_=rs[s][:], func=ACT.Sin, scale=TWO_PI, bias=phase1[:, i : i + 1])
+        def y_rest(s, units=range(2)):
+            i = pairs[s][0]
+            for a in units:
+                nc.vector.scalar_tensor_tensor(
+                    turns_tile(s)[:, a, :], ys[s, a][:], turn[:, 0, i : i + 1], ks[s][:, a, :], OP.mult, OP.subtract
+                )
 
-        def h_turn(s):
-            turned_h[s] = psum.tile([P, PACK, P], F32, name="th", tag="th", bufs=2)
-            for t in range(PACK):
-                nc.tensor.transpose(turned_h[s][:, t, :], sines[s][:, t * P : (t + 1) * P], ident[:])
+        def y_sin(s, units=range(2)):
+            i = pairs[s][0]
+            for a in units:
+                nc.scalar.activation(
+                    out=us[s][:, a, :], in_=us[s][:, a, :], func=ACT.Sin, scale=TWO_PI, bias=phase1[:, i : i + 1]
+                )
+
+        def h_turn(s, first=4):
+            for a in range(2):
+                turned_h[s, a] = bank(first + a, [P, PACK, P])
+                for t in range(PACK):
+                    nc.tensor.transpose(turned_h[s, a][:, t, :], us[s][:, a, t * P : (t + 1) * P], ident[:])
 
         def h_amp(s):
-            j = units[s][1]
-            h_woven[s] = shared([P, P, PACK], BF16, "h_woven", s)
-            nc.vector.tensor_tensor(
-                h_woven[s][:],
-                turned_h[s][:].rearrange("q t n -> q n t"),
-                amp_sb[:, j, :].unsqueeze(1).to_broadcast([P, P, PACK]),
-                OP.mult,
-            )
+            h_woven[s] = buf(f"hw{s % 2}", [P, 2, P, PACK], BF16)
+            for a in range(2):
+                j = 2 * pairs[s][1] + a
+                nc.vector.tensor_tensor(
+                    h_woven[s][:, a],
+                    turned_h[s, a][:].rearrange("q t n -> q n t"),
+                    amp_sb[:, j, :].unsqueeze(1).to_broadcast([P, P, PACK]),
+                    OP.mult,
+                )
 
         def h_quant(s):
-            i, j = units[s]
-            quantize(hq[4 * i + j][:], hqs[4 * i + j][:], h_woven[s][:].rearrange("q n t -> q (n t)"))
+            i, cp = pairs[s]
+            quantize(hq[2 * i + cp][:], hqs[2 * i + cp][:], h_woven[s][:].rearrange("q a n t -> q (a n t)"))
 
-        z_tasks = [(i, r0, BANK) for r0 in (0, BANK) for i in range(FIRST_TILES)]
-        z_tasks.extend((i, r0, BANK) for i in range(FIRST_TILES, 7) for r0 in (0, BANK))
-        quarters = range(len(z_tasks), len(z_tasks) + 4)
-        z_tasks.extend((7, r0, 256) for r0 in range(0, R, 256))
-        zs, u2s, k2s, r2s, turned_z, last_z = {}, {}, {}, {}, {}, {}
+        tasks = [(i, half) for half in range(2) for i in range(2)]
+        tasks.extend((i, half) for i in range(2, 8) for half in range(2))
+        zs, u2s, k2s, turned_z = {}, {}, {}, {}
 
-        def z_pass(i, half, dst, j):
-            nc.tensor.matmul_mx(
-                out=dst[:],
-                lhsT=hq[4 * i + j][:].bitcast(FP8X4),
-                lhsT_scale=hqs[4 * i + j][:],
-                rhs=pq[4 * half + j][:].bitcast(FP8X4),
-                rhs_scale=pqs[4 * half + j][:],
-                start=(j == 0),
-                stop=(j == 3),
-            )
-
-        def z_mm(n):
-            i, r0, width = z_tasks[n]
-            zs[n] = psum.tile([P, width], F32, name="z", tag="tx", bufs=3)
-            for j in range(4):
-                z_pass(i, r0 // BANK, zs[n], j)
-
-        def last_passes(half, chunks):
-            if half not in last_z:
-                last_z[half] = psum.tile([P, BANK], F32, name="z", tag="y", bufs=3)
-                for a in range(2):
-                    zs[quarters[2 * half + a]] = last_z[half][:, 256 * a : 256 * a + 256]
+        def z_mm(n, number, chunks=range(4)):
+            i, half = tasks[n]
+            if n not in zs:
+                zs[n] = bank(number, [P, BANK])
             for j in chunks:
-                z_pass(7, half, last_z[half], j)
+                cols = slice(P * (j % 2), P * (j % 2) + P)
+                m = 2 * i + j // 2
+                product(zs[n][:], hq[m][:, cols], hqs[m][:, cols], pq[4 * half + j][:], pqs[4 * half + j][:], j == 0, j == 3)
 
-        def z_turns(n):
-            col = 8 + z_tasks[n][0]
-            u2s[n] = stage.tile([P, z_tasks[n][2]], F32, name="u2", bufs=4)
+        def z_turns(n, cols=slice(0, BANK)):
+            col = 8 + tasks[n][0]
+            if n not in u2s:
+                u2s[n] = buf(f"u2{n % 4}" if n < 12 else f"pw{n - 12}", [P, BANK], F32)
             nc.scalar.activation(
-                out=u2s[n][:],
-                in_=zs[n][:],
-                func=ACT.Identity,
-                scale=turn[:, 0, col : col + 1],
-                bias=turn[:, 1, col : col + 1],
+                out=u2s[n][:, cols], in_=zs[n][:, cols], func=ACT.Identity,
+                scale=turn[:, 0, col : col + 1], bias=turn[:, 1, col : col + 1],
             )
 
-        def z_round(n):
-            k2s[n] = stage.tile([P, z_tasks[n][2]], I32, name="k2", bufs=3)
-            nc.vector.tensor_copy(out=k2s[n][:], in_=u2s[n][:])
+        def z_round_late(n, tag):
+            k2s[n] = buf(tag, [P, BANK], I32)
+            nc.gpsimd.tensor_scalar(k2s[n][:], u2s[n][:], 1.0, 0.0, OP.mult, OP.add)
 
-        def z_rest(n):
-            r2s[n] = stage.tile([P, z_tasks[n][2]], F32, name="r2", bufs=3)
-            nc.vector.tensor_tensor(r2s[n][:], u2s[n][:], k2s[n][:], OP.subtract)
+        def z_round(n, cols=slice(0, BANK)):
+            if n not in k2s:
+                k2s[n] = buf(f"xs{n % 3}", [P, BANK], I32)
+            nc.vector.tensor_copy(out=k2s[n][:, cols], in_=u2s[n][:, cols])
 
-        def z_turn(n):
-            blocks = z_tasks[n][2] // P
-            if n in quarters[:2]:
-                turned_z[n] = psum.tile([P, blocks, P], F32, name="turned_z", tag="th", bufs=2)
-            else:
-                turned_z[n] = psum.tile([P, blocks, P], F32, name="turned_z", tag="tx", bufs=3)
-            for a in range(blocks):
-                nc.tensor.transpose(turned_z[n][:, a, :], r2s[n][:, a * P : (a + 1) * P], ident[:])
+        def z_rest(n, cols=slice(0, BANK)):
+            nc.vector.tensor_tensor(u2s[n][:, cols], u2s[n][:, cols], k2s[n][:, cols], OP.subtract)
 
-        def z_out(n):
-            i, r0, width = z_tasks[n]
-            o = stage.tile([P, width // P, P], F32, name="o", align_bytes=64, bufs=8)
-            nc.scalar.activation(out=o[:], in_=turned_z[n][:], func=ACT.Sin, scale=TWO_PI)
-            nc.sync.dma_start(
-                out=out[r0 : r0 + width, P * i : P * i + P].rearrange("(a q) n -> q a n", q=P),
-                in_=o[:],
-            )
+        def z_turn(n, number, blocks=range(PACK)):
+            turned_z[n, blocks.start] = bank(number, [P, len(blocks), P])
+            for a in blocks:
+                nc.tensor.transpose(turned_z[n, blocks.start][:, a - blocks.start, :], u2s[n][:, a * P : (a + 1) * P], ident[:])
+
+        out_slots = ["xw0", "xw1", "praw4", "praw5", "praw6", "praw7"]
+        stored = []
+
+        def z_out(n, blocks=range(PACK)):
+            i, half = tasks[n]
+            o = buf(out_slots[len(stored) % 6], [P, len(blocks), P], F32)
+            stored.append(n)
+            nc.scalar.activation(out=o[:], in_=turned_z[n, blocks.start][:], func=ACT.Sin, scale=TWO_PI)
+            rows = slice(BANK * half + P * blocks.start, BANK * half + P * blocks.stop)
+            nc.sync.dma_start(out=out[rows, P * i : P * i + P].rearrange("(a q) n -> q a n", q=P), in_=o[:])
+
+        count = [0]
+
+        def free_bank():
+            count[0] = count[0] + 1
+            return 4 + count[0] % 4
+
+        def x_row(n, number=None):
+            x_mult(n)
+            x_turn(n, number or free_bank())
+            x_copy(n)
+
+        def p_piece(n, number=None):
+            p_turn(n, number or free_bank())
+            p_copy(n)
 
         for g in range(2):
-            spread_turn(g)
-        for g in range(2):
-            spread_copy(g)
+            spread_scales(g)
         for g in range(2):
             x_mult(0, slice(BANK * g, BANK * g + BANK))
-        for n in range(3):
-            w_weave(n)
-        x_turn(0)
+        x_turn(0, free_bank())
+        w_weave(0, 0)
+        w_weave(0, 1)
         x_copy(0)
-        for n in range(1, 4):
-            x_mult(n)
-            w_weave(n + 2)
-            x_turn(n)
-            x_copy(n)
-        for n in range(4):
-            w_quant(n)
-        x_mult(4)
-        freq_turns()
-        w_weave(6)
-        x_turn(4)
-        x_copy(4)
-        x_mult(5)
-        x_turn(5)
+        w_weave(1, 0)
+        x_row(1)
+        w_weave(1, 1)
+        x_row(2)
+        w_weave(2, 0)
+        x_row(3)
+        channel_constants(0)
+        x_row(4)
+        p_piece(0)
+        x_row(5)
+        p_piece(2)
         x_quant(0)
-        bias_turns()
         x_quant(1)
-        bias_phase()
-        x_copy(5)
-        w_quant(4)
-        w_quant(5)
+        w_quant(0)
+        w_weave(2, 1)
+        y_mm(0, [0])
+        x_row(6)
+        channel_constants(1)
+        p_piece(4)
+        x_row(7)
+        w_quant(1)
+        p_piece(6)
+        w_weave(5, 0)
+        y_mm(1, [0])
+        x_row(8)
+        p_piece(1)
+        y_turns(1, [0])
+        x_row(9)
+        x_quant(2)
+        x_quant(3)
+        p_piece(3)
+        y_mm(1, [1])
+        x_row(10)
+        y_turns(1, [1])
+        x_row(11)
+        w_weave(5, 1)
+        y_mm(0, [1])
+        p_piece(5)
+        x_row(12, 4)
+        p_piece(7, 5)
+        w_quant(2)
+        rounding(1, "k1")
+        w_weave_late(3, 0)
+        x_row(13, 6)
+        y_round(0, "k0")
+        y_rest(0)
+        w_weave(6, 0)
+        y_mm(2)
+        y_sin(0)
+        y_turns(2)
+        x_row(14, 7)
+        x_row(15, 6)
+        w_weave(6, 1)
+        h_turn(0)
+        x_quant(4)
+        x_quant(5)
+        rounding(2, "xw0")
+        p_quant(0)
+        y_rest(1)
+        p_piece(8, 7)
+        y_mm(3, [0])
+        y_sin(1, [0])
+        y_turns(3, [0])
+        y_sin(1, [1])
+        p_turn(9, 6)
+        x_quant(6)
+        x_quant(7)
+        y_rest(2, [0])
+        y_mm(3, [1])
+        y_mm(4, [0])
+        y_turns(3, [1])
+        p_copy(9)
+        y_turns(4, [0])
+        p_piece(10, 7)
+        w_weave(7, 0)
+        p_quant(1)
+        p_quant(2)
+        rounding(3, "pw2")
+        p_quant(3)
 
-        def by_step(step_of, tasks):
-            table = {}
-            for n in tasks:
-                table.setdefault(step_of(n), []).append(n)
-            return table
-
-        x_at = by_step(lambda n: max(1, n - HEAD_X_ROWS), range(HEAD_X_ROWS, 16))
-        xq_at = by_step(lambda n: FIRST_TILES * (n // 2) - 2 + n % 2, range(2, 8))
-        p_at = by_step(lambda n: 2 * (n // 3) + n % 3 // 2 if n < 8 else n - 3, range(16))
-        pq_at = by_step(lambda n: P_QUANT_START + n, range(12))
-        w_at = by_step(lambda n: 4 * (n // 2) - 5 + n % 2, range(w_before_round + 1, 16))
-        w_at[0] = [HEAD_W_PIECES]
-        w_at[ROUND_ON_VECTOR - 1] = [w_before_round]
-        late = [Z_START + Z_EVERY_STEP + 1 + 3 * (a // 2) + a % 2 for a in range(Z_IN_LOOP - Z_EVERY_STEP)]
-        z_at = by_step(lambda n: Z_START + n if n < Z_EVERY_STEP else late[n - Z_EVERY_STEP], range(Z_IN_LOOP))
-
-        def each(fn, tasks):
-            for n in tasks:
-                fn(n)
-
-        def unit(lag):
-            return [s - lag] if s >= lag else []
-
-        for s in range(UNITS):
-            turns = [(x_turn, x_copy, n) for n in x_at.get(s, [])] + [(p_turn, p_copy, n) for n in p_at.get(s, [])]
-            y_mm(s)
-            each(z_mm, z_at.get(s, []))
-            each(h_turn, unit(3))
-            each(z_turn, z_at.get(s - 4, []))
-            for turn_fn, copy_fn, n in turns:
-                turn_fn(n)
-
-            ported = [(z_round, n) for n in z_at.get(s - 2, [])]
-            ported.extend((w_quant, n) for n in w_at.get(s - 2, []) if n > w_before_round)
-            ported.extend((x_quant, n) for n in xq_at.get(s, []))
-            ported.extend((p_quant, n) for n in pq_at.get(s, []))
-            ported.extend((z_rest, n) for n in z_at.get(s - 3, []))
-            ported.extend((x_mult, n) for n in x_at.get(s + 1, []))
-            if s >= 4:
-                frees_round = [(h_quant, s - 4)]
-            elif s == ROUND_ON_VECTOR:
-                frees_round = [(w_quant, w_before_round)]
+        amp_order = [0, 1, 3, 4, 2] + list(range(5, 16))
+        first_z = 3
+        for s in range(12):
+            n = s - first_z
+            y_rest(s + 2, [1])
+            if n >= 1:
+                z_round_late(n - 1, f"k{s % 3}")
+            elif s >= 1:
+                w_weave_late(*divmod(s + 6, 2))
+            y_mm(s + 4, [1])
+            if n >= 0:
+                z_mm(n, 6)
             else:
-                frees_round = [(w_quant, n) for n in range(HEAD_W_PIECES - 1, HEAD_W_PIECES + 1) if n == s + 6]
-            place = len(ported) - 1 if len(ported) > 1 or s < 4 else len(ported)
-            for fn, n in ported[:place] + frees_round + ported[place:]:
-                fn(n)
+                p_turn(2 * s + 11, (6, 6, 7)[s])
+            if s in (1, 2):
+                y_sin(s + 2, [1])
+            y_turns(s + 4, [1])
+            if s in (1, 2):
+                p_copy(2 * s + 10)
+            if n < 0:
+                p_copy(2 * s + 11)
+            else:
+                y_sin(s + 2, [0])
+                z_turns(n)
+                y_sin(s + 2, [1])
+            h_amp(amp_order[s])
+            y_rest(s + 3, [0])
+            if n < 1:
+                p_quant(s + 4)
+            if n >= 1:
+                z_rest(n - 1)
+            if s == 4:
+                w_weave_last(7, 1)
+            if s in (1, 3, 5, 7, 9):
+                w_quant(s // 2 + 3)
+            h_quant(amp_order[s])
+            h_turn(amp_order[s + 1])
+            if s in (0, 1):
+                y_sin(s + 3, [0])
+            if s == 2:
+                y_sin(2)
+            if n >= 1:
+                z_turn(n - 1, 7)
+                z_out(n - 1)
+            if s < 11:
+                y_mm(s + 5, [0])
+                y_turns(s + 5, [0])
+            if s < 2:
+                p_turn(2 * s + 12, 7 - s)
+            rounding(s + 4, f"k{s % 3}" if n >= 1 else p_slot[s + 4])
 
-            y_round(s)
-            each(y_sin, unit(2))
-            each(y_rest, unit(1))
-            each(h_amp, unit(3))
-            each(z_turns, z_at.get(s, []))
-            for turn_fn, copy_fn, n in turns[:1]:
-                copy_fn(n)
-            each(w_weave, w_at.get(s, []))
-            for turn_fn, copy_fn, n in turns[1:]:
-                copy_fn(n)
-            each(z_out, z_at.get(s - 4, []))
-
+        lo, hi = slice(0, 256), slice(256, 512)
+        y_rest(14, [1])
+        z_round_late(8, "k0")
+        z_mm(9, 6)
+        h_turn(13, 2)
+        h_amp(12)
+        y_rest(15)
+        y_sin(14)
+        z_turns(9)
+        y_sin(15)
+        z_mm(10, 0)
+        z_mm(11, 1)
+        h_quant(12)
+        z_rest(8)
+        z_round_late(9, "k0")
+        h_amp(13)
+        h_turn(14)
+        h_turn(15, 2)
+        z_turn(8, 7)
+        z_turns(10)
+        z_turns(11)
+        z_out(8)
+        z_rest(9)
+        h_quant(13)
         z_round(10)
-        h_turn(29)
-        z_turn(9)
-        z_mm(12)
-        z_mm(13)
-        y_sin(30)
-        y_rest(31)
-        h_amp(29)
-        z_round(11)
-        h_quant(28)
+        z_round_late(11, "k1")
+        z_mm(12, 6)
+        z_mm(13, 0)
+        h_amp(14)
+        h_amp(15)
         z_rest(10)
-        y_sin(31)
-        z_out(9)
-        z_turns(12)
+        h_quant(14)
         z_rest(11)
-        each(h_turn, (30, 31))
-        each(z_turn, (10, 11))
+        h_quant(15)
+        z_turn(9, 7)
+        z_turn(10, 1)
+        z_turn(11, 2)
+        z_turns(12)
         z_turns(13)
-        h_amp(30)
-        h_quant(29)
-        h_amp(31)
-        h_quant(30)
+        z_mm(14, 4)
+        z_mm(15, 5)
+        z_out(9)
+        z_out(10)
+        z_out(11)
         z_round(12)
-        h_quant(31)
-        each(z_out, (10, 11))
-        for chunks in ((0, 1), (2, 3)):
-            for half in range(2):
-                last_passes(half, chunks)
         z_round(13)
-        each(z_rest, (12, 13))
-        each(z_turn, (12, 13))
-        each(z_turns, quarters)
+        z_rest(12)
+        z_rest(13)
+        z_turn(12, 3)
+        z_turn(13, 6)
+        z_turns(14)
+        z_turns(15, lo)
+        z_turns(15, hi)
         z_out(12)
-        each(z_round, quarters[:3])
-        z_rest(quarters[0])
-        z_round(quarters[3])
-        z_rest(quarters[1])
-        each(z_turn, quarters[:2])
         z_out(13)
-        each(z_rest, quarters[2:])
-        each(z_turn, quarters[2:])
-        each(z_out, quarters)
+        z_round(14)
+        z_rest(14)
+        z_round(15, lo)
+        z_round(15, hi)
+        z_rest(15, lo)
+        z_rest(15, hi)
+        z_turn(14, 7)
+        z_turn(15, 0, range(0, 2))
+        z_turn(15, 1, range(2, 4))
+        z_out(14)
+        z_out(15, range(0, 2))
+        z_out(15, range(2, 4))

@@ -278,55 +278,53 @@ def tile_siren_anchor_field_f4_kernel(tc, x_bytes, x_scale, w, b, freq1, amp, p,
             i, cp = pairs[s]
             quantize(hq[2 * i + cp][:], hqs[2 * i + cp][:], h_woven[s][:].rearrange("q a n t -> q (a n t)"))
 
-        tasks = [(i, half) for half in range(2) for i in range(2)]
-        tasks.extend((i, half) for i in range(2, 8) for half in range(2))
+        tasks = [(i, r0, BANK) for r0 in (0, BANK) for i in range(2)]
+        tasks.extend((i, r0, BANK) for i in range(2, 8) for r0 in (0, BANK))
+        tasks[14:] = [(7, 0, 256), (7, 256, 256), (7, 512, 256), (7, 768, 128), (7, 896, 128)]
         zs, u2s, k2s, turned_z = {}, {}, {}, {}
 
-        def z_mm(n, number, chunks=range(4)):
-            i, half = tasks[n]
-            if n not in zs:
-                zs[n] = bank(number, [P, BANK])
-            for j in chunks:
+        def z_mm(n, number):
+            i, r0, width = tasks[n]
+            zs[n] = bank(number, [P, width])
+            queries = slice(r0 % BANK, r0 % BANK + width)
+            for j in range(4):
                 cols = slice(P * (j % 2), P * (j % 2) + P)
                 m = 2 * i + j // 2
-                product(zs[n][:], hq[m][:, cols], hqs[m][:, cols], pq[4 * half + j][:], pqs[4 * half + j][:], j == 0, j == 3)
+                part = 4 * (r0 // BANK) + j
+                product(zs[n][:], hq[m][:, cols], hqs[m][:, cols], pq[part][:, queries], pqs[part][:, queries], j == 0, j == 3)
 
-        def z_turns(n, cols=slice(0, BANK)):
-            col = 8 + tasks[n][0]
-            if n not in u2s:
-                u2s[n] = buf(f"u2{n % 4}" if n < 12 else f"pw{n - 12}", [P, BANK], F32)
+        def z_turns(n):
+            i, r0, width = tasks[n]
+            u2s[n] = buf(f"u2{n % 4}" if n < 12 else f"praw{(n - 12) % 4}" if n >= 16 else f"pw{n - 12}", [P, width], F32)
             nc.scalar.activation(
-                out=u2s[n][:, cols], in_=zs[n][:, cols], func=ACT.Identity,
-                scale=turn[:, 0, col : col + 1], bias=turn[:, 1, col : col + 1],
+                out=u2s[n][:], in_=zs[n][:], func=ACT.Identity,
+                scale=turn[:, 0, 8 + i : 9 + i], bias=turn[:, 1, 8 + i : 9 + i],
             )
 
         def z_round_late(n, tag):
             k2s[n] = buf(tag, [P, BANK], I32)
             nc.gpsimd.tensor_scalar(k2s[n][:], u2s[n][:], 1.0, 0.0, OP.mult, OP.add)
 
-        def z_round(n, cols=slice(0, BANK)):
-            if n not in k2s:
-                k2s[n] = buf(f"xs{n % 3}", [P, BANK], I32)
-            nc.vector.tensor_copy(out=k2s[n][:, cols], in_=u2s[n][:, cols])
+        def z_round(n):
+            k2s[n] = buf(f"xs{n % 3}", [P, tasks[n][2]], I32)
+            nc.vector.tensor_copy(out=k2s[n][:], in_=u2s[n][:])
 
-        def z_rest(n, cols=slice(0, BANK)):
-            nc.vector.tensor_tensor(u2s[n][:, cols], u2s[n][:, cols], k2s[n][:, cols], OP.subtract)
+        def z_rest(n):
+            nc.vector.tensor_tensor(u2s[n][:], u2s[n][:], k2s[n][:], OP.subtract)
 
-        def z_turn(n, number, blocks=range(PACK)):
-            turned_z[n, blocks.start] = bank(number, [P, len(blocks), P])
-            for a in blocks:
-                nc.tensor.transpose(turned_z[n, blocks.start][:, a - blocks.start, :], u2s[n][:, a * P : (a + 1) * P], ident[:])
+        def z_turn(n, number):
+            blocks = tasks[n][2] // P
+            turned_z[n] = bank(number, [P, blocks, P])
+            for a in range(blocks):
+                nc.tensor.transpose(turned_z[n][:, a, :], u2s[n][:, a * P : (a + 1) * P], ident[:])
 
         out_slots = ["xw0", "xw1", "praw4", "praw5", "praw6", "praw7"]
-        stored = []
 
-        def z_out(n, blocks=range(PACK)):
-            i, half = tasks[n]
-            o = buf(out_slots[len(stored) % 6], [P, len(blocks), P], F32)
-            stored.append(n)
-            nc.scalar.activation(out=o[:], in_=turned_z[n, blocks.start][:], func=ACT.Sin, scale=TWO_PI)
-            rows = slice(BANK * half + P * blocks.start, BANK * half + P * blocks.stop)
-            nc.sync.dma_start(out=out[rows, P * i : P * i + P].rearrange("(a q) n -> q a n", q=P), in_=o[:])
+        def z_out(n):
+            i, r0, width = tasks[n]
+            o = buf(out_slots[n % 6], [P, width // P, P], F32)
+            nc.scalar.activation(out=o[:], in_=turned_z[n][:], func=ACT.Sin, scale=TWO_PI)
+            nc.sync.dma_start(out=out[r0 : r0 + width, P * i : P * i + P].rearrange("(a q) n -> q a n", q=P), in_=o[:])
 
         count = [0]
 
@@ -482,7 +480,6 @@ def tile_siren_anchor_field_f4_kernel(tc, x_bytes, x_scale, w, b, freq1, amp, p,
                 p_turn(2 * s + 12, 7 - s)
             rounding(s + 4, f"k{s % 3}" if n >= 1 else p_slot[s + 4])
 
-        lo, hi = slice(0, 256), slice(256, 512)
         y_rest(14, [1])
         z_round_late(8, "k0")
         z_mm(9, 6)
@@ -498,54 +495,64 @@ def tile_siren_anchor_field_f4_kernel(tc, x_bytes, x_scale, w, b, freq1, amp, p,
         z_rest(8)
         z_round_late(9, "k0")
         h_amp(13)
+        z_rest(9)
         h_turn(14)
         h_turn(15, 2)
         z_turn(8, 7)
         z_turns(10)
         z_turns(11)
+        z_turn(9, 0)
         z_out(8)
-        z_rest(9)
+        z_out(9)
         h_quant(13)
         z_round(10)
         z_round_late(11, "k1")
         z_mm(12, 6)
-        z_mm(13, 0)
+        z_mm(13, 1)
         h_amp(14)
         h_amp(15)
-        z_rest(10)
         h_quant(14)
-        z_rest(11)
+        z_rest(10)
         h_quant(15)
-        z_turn(9, 7)
-        z_turn(10, 1)
-        z_turn(11, 2)
+        z_rest(11)
+        z_turn(10, 7)
+        z_turn(11, 0)
         z_turns(12)
         z_turns(13)
         z_mm(14, 4)
         z_mm(15, 5)
-        z_out(9)
         z_out(10)
+        z_turns(14)
         z_out(11)
+        z_turns(15)
         z_round(12)
         z_round(13)
         z_rest(12)
         z_rest(13)
         z_turn(12, 3)
         z_turn(13, 6)
-        z_turns(14)
-        z_turns(15, lo)
-        z_turns(15, hi)
+        z_mm(16, 2)
+        z_mm(17, 1)
+        z_mm(18, 7)
+        z_round(14)
+        z_round(15)
+        z_rest(14)
+        z_rest(15)
         z_out(12)
         z_out(13)
-        z_round(14)
-        z_rest(14)
-        z_round(15, lo)
-        z_round(15, hi)
-        z_rest(15, lo)
-        z_rest(15, hi)
-        z_turn(14, 7)
-        z_turn(15, 0, range(0, 2))
-        z_turn(15, 1, range(2, 4))
-        z_out(14)
-        z_out(15, range(0, 2))
-        z_out(15, range(2, 4))
+        z_turns(16)
+        z_turns(17)
+        z_turns(18)
+        z_turn(14, 0)
+        z_turn(15, 4)
+        z_round(16)
+        z_round(17)
+        z_rest(16)
+        z_round(18)
+        z_rest(17)
+        z_rest(18)
+        z_turn(16, 5)
+        z_turn(17, 3)
+        z_turn(18, 6)
+        for n in range(14, 19):
+            z_out(n)

@@ -21,6 +21,7 @@ P = 128
 PACK = 4
 BANK = 512
 TWO_PI = 2.0 * math.pi
+ON_VECTOR = (3, 5, 8)
 
 
 def tile_siren_anchor_field_f4_kernel(tc, x_bytes, x_scale, w, b, freq1, amp, p, c, freq2, out):
@@ -129,7 +130,7 @@ def tile_siren_anchor_field_f4_kernel(tc, x_bytes, x_scale, w, b, freq1, amp, p,
                 start=first, stop=last,
             )
 
-        w_woven = {}
+        w_woven, turned = {}, {}
         w_slot = {0: "ww0", 1: "ww1", 2: "k1", 3: "ww0", 4: "ww1", 5: "ww2", 6: "ww3", 7: "ww4"}
 
         def woven_w(n):
@@ -146,16 +147,20 @@ def tile_siren_anchor_field_f4_kernel(tc, x_bytes, x_scale, w, b, freq1, amp, p,
         def w_weave_late(n, g):
             nc.gpsimd.tensor_scalar(woven_w(n)[:, g], wraw[n][:, g].rearrange("p t n -> p n t"), 1.0, 0.0, OP.mult, OP.add)
 
-        def w_weave_last(n, g):
-            nc.vector.tensor_copy(
-                out=woven_w(n)[:, g].rearrange("p (a e) t -> p a t e", e=4),
-                in_=wraw[n][:, g].rearrange("p t (a e) -> p a t e", e=4),
-            )
+        def w_pass_through(n, number):
+            turned["w", n] = bank(number, [P, 2, BANK], BF16)
+            for g in range(2):
+                nc.tensor.matmul(
+                    turned["w", n][:, g, :], ident_b[:], wraw[n][:, g].rearrange("p t n -> p n t"), start=True, stop=True
+                )
+
+        def w_copy(n):
+            nc.scalar.copy(out=woven_w(n)[:].rearrange("p g n t -> p (g n t)"), in_=turned["w", n][:].rearrange("p g c -> p (g c)"))
 
         def w_quant(n):
             quantize(wq[n][:], wqs[n][:], w_woven[n][:].rearrange("p g n t -> p (g n t)"))
 
-        xs, x_woven, p_woven, turned = {}, {}, {}, {}
+        xs, x_woven, p_woven = {}, {}, {}
 
         def x_mult(n, cols=slice(0, K)):
             if n not in xs:
@@ -252,10 +257,8 @@ def tile_siren_anchor_field_f4_kernel(tc, x_bytes, x_scale, w, b, freq1, amp, p,
 
         def y_sin(s, units=range(2)):
             i = pairs[s][0]
-            for a in units:
-                nc.scalar.activation(
-                    out=us[s][:, a, :], in_=us[s][:, a, :], func=ACT.Sin, scale=TWO_PI, bias=phase1[:, i : i + 1]
-                )
+            rest = us[s][:, units[0] : units[-1] + 1, :]
+            nc.scalar.activation(out=rest, in_=rest, func=ACT.Sin, scale=TWO_PI, bias=phase1[:, i : i + 1])
 
         def h_turn(s, first=4):
             for a in range(2):
@@ -263,8 +266,8 @@ def tile_siren_anchor_field_f4_kernel(tc, x_bytes, x_scale, w, b, freq1, amp, p,
                 for t in range(PACK):
                     nc.tensor.transpose(turned_h[s, a][:, t, :], us[s][:, a, t * P : (t + 1) * P], ident[:])
 
-        def h_amp(s):
-            h_woven[s] = buf(f"hw{s % 2}", [P, 2, P, PACK], BF16)
+        def h_amp(s, tag=None):
+            h_woven[s] = buf(tag or f"hw{s % 2}", [P, 2, P, PACK], BF16)
             for a in range(2):
                 j = 2 * pairs[s][1] + a
                 nc.vector.tensor_tensor(
@@ -280,7 +283,7 @@ def tile_siren_anchor_field_f4_kernel(tc, x_bytes, x_scale, w, b, freq1, amp, p,
 
         tasks = [(i, r0, BANK) for r0 in (0, BANK) for i in range(2)]
         tasks.extend((i, r0, BANK) for i in range(2, 8) for r0 in (0, BANK))
-        tasks[14:] = [(7, 0, 256), (7, 256, 256), (7, 512, 256), (7, 768, 128), (7, 896, 128)]
+        tasks[15:] = [(7, 512, 256), (7, 768, 256)]
         zs, u2s, k2s, turned_z = {}, {}, {}, {}
 
         def z_mm(n, number):
@@ -301,6 +304,11 @@ def tile_siren_anchor_field_f4_kernel(tc, x_bytes, x_scale, w, b, freq1, amp, p,
                 scale=turn[:, 0, 8 + i : 9 + i], bias=turn[:, 1, 8 + i : 9 + i],
             )
 
+        def z_turns_vector(n):
+            i, r0, width = tasks[n]
+            u2s[n] = buf(f"u2{n % 4}" if n < 12 else f"praw{(n - 12) % 4}" if n >= 16 else f"pw{n - 12}", [P, width], F32)
+            nc.vector.tensor_scalar(u2s[n][:], zs[n][:], turn[:, 0, 8 + i : 9 + i], turn[:, 1, 8 + i : 9 + i], OP.mult, OP.add)
+
         def z_round_late(n, tag):
             k2s[n] = buf(tag, [P, BANK], I32)
             nc.gpsimd.tensor_scalar(k2s[n][:], u2s[n][:], 1.0, 0.0, OP.mult, OP.add)
@@ -318,11 +326,11 @@ def tile_siren_anchor_field_f4_kernel(tc, x_bytes, x_scale, w, b, freq1, amp, p,
             for a in range(blocks):
                 nc.tensor.transpose(turned_z[n][:, a, :], u2s[n][:, a * P : (a + 1) * P], ident[:])
 
-        out_slots = ["xw0", "xw1", "praw4", "praw5", "praw6", "praw7"]
+        out_slots = ["xw0", "xw1", "praw4", "praw5", "praw6", "praw7", "wraw0", "wraw3"]
 
         def z_out(n):
             i, r0, width = tasks[n]
-            o = buf(out_slots[n % 6], [P, width // P, P], F32)
+            o = buf(out_slots[n % 8], [P, width // P, P], F32)
             nc.scalar.activation(out=o[:], in_=turned_z[n][:], func=ACT.Sin, scale=TWO_PI)
             nc.sync.dma_start(out=out[r0 : r0 + width, P * i : P * i + P].rearrange("(a q) n -> q a n", q=P), in_=o[:])
 
@@ -393,22 +401,23 @@ def tile_siren_anchor_field_f4_kernel(tc, x_bytes, x_scale, w, b, freq1, amp, p,
         rounding(1, "k1")
         w_weave_late(3, 0)
         x_row(13, 6)
+        w_pass_through(6, 7)
+        w_copy(6)
         y_round(0, "k0")
         y_rest(0)
-        w_weave(6, 0)
         y_mm(2)
+        w_pass_through(7, 4)
         y_sin(0)
         y_turns(2)
         x_row(14, 7)
         x_row(15, 6)
-        w_weave(6, 1)
-        h_turn(0)
+        w_copy(7)
         x_quant(4)
         x_quant(5)
         rounding(2, "xw0")
         p_quant(0)
         y_rest(1)
-        p_piece(8, 7)
+        p_piece(8, 5)
         y_mm(3, [0])
         y_sin(1, [0])
         y_turns(3, [0])
@@ -419,11 +428,11 @@ def tile_siren_anchor_field_f4_kernel(tc, x_bytes, x_scale, w, b, freq1, amp, p,
         y_rest(2, [0])
         y_mm(3, [1])
         y_mm(4, [0])
+        h_turn(0)
         y_turns(3, [1])
         p_copy(9)
         y_turns(4, [0])
         p_piece(10, 7)
-        w_weave(7, 0)
         p_quant(1)
         p_quant(2)
         rounding(3, "pw2")
@@ -434,6 +443,8 @@ def tile_siren_anchor_field_f4_kernel(tc, x_bytes, x_scale, w, b, freq1, amp, p,
         for s in range(12):
             n = s - first_z
             y_rest(s + 2, [1])
+            if n - 1 in ON_VECTOR:
+                z_turns_vector(n - 1)
             if n >= 1:
                 z_round_late(n - 1, f"k{s % 3}")
             elif s >= 1:
@@ -451,17 +462,15 @@ def tile_siren_anchor_field_f4_kernel(tc, x_bytes, x_scale, w, b, freq1, amp, p,
             if n < 0:
                 p_copy(2 * s + 11)
             else:
-                y_sin(s + 2, [0])
-                z_turns(n)
-                y_sin(s + 2, [1])
+                if n not in ON_VECTOR:
+                    z_turns(n)
+                y_sin(s + 2)
             h_amp(amp_order[s])
             y_rest(s + 3, [0])
             if n < 1:
                 p_quant(s + 4)
             if n >= 1:
                 z_rest(n - 1)
-            if s == 4:
-                w_weave_last(7, 1)
             if s in (1, 3, 5, 7, 9):
                 w_quant(s // 2 + 3)
             h_quant(amp_order[s])
@@ -481,78 +490,69 @@ def tile_siren_anchor_field_f4_kernel(tc, x_bytes, x_scale, w, b, freq1, amp, p,
             rounding(s + 4, f"k{s % 3}" if n >= 1 else p_slot[s + 4])
 
         y_rest(14, [1])
+        z_turns_vector(8)
+        y_sin(14)
         z_round_late(8, "k0")
-        z_mm(9, 6)
-        h_turn(13, 2)
+        z_mm(9, 2)
+        h_turn(13, 6)
         h_amp(12)
         y_rest(15)
-        y_sin(14)
         z_turns(9)
         y_sin(15)
-        z_mm(10, 0)
-        z_mm(11, 1)
+        z_mm(10, 3)
+        z_mm(11, 0)
         h_quant(12)
         z_rest(8)
         z_round_late(9, "k0")
         h_amp(13)
         z_rest(9)
         h_turn(14)
-        h_turn(15, 2)
+        h_turn(15, 1)
         z_turn(8, 7)
         z_turns(10)
         z_turns(11)
-        z_turn(9, 0)
+        z_turn(9, 6)
         z_out(8)
         z_out(9)
         h_quant(13)
-        z_round(10)
+        z_round_late(10, "hw1")
         z_round_late(11, "k1")
-        z_mm(12, 6)
-        z_mm(13, 1)
+        z_mm(12, 3)
+        z_mm(13, 0)
         h_amp(14)
-        h_amp(15)
+        h_amp(15, "k2")
         h_quant(14)
-        z_rest(10)
         h_quant(15)
+        z_rest(10)
         z_rest(11)
-        z_turn(10, 7)
-        z_turn(11, 0)
         z_turns(12)
         z_turns(13)
         z_mm(14, 4)
+        z_turn(10, 7)
+        z_turn(11, 6)
         z_mm(15, 5)
-        z_out(10)
-        z_turns(14)
-        z_out(11)
-        z_turns(15)
+        z_mm(16, 1)
         z_round(12)
         z_round(13)
         z_rest(12)
         z_rest(13)
-        z_turn(12, 3)
-        z_turn(13, 6)
-        z_mm(16, 2)
-        z_mm(17, 1)
-        z_mm(18, 7)
-        z_round(14)
-        z_round(15)
-        z_rest(14)
-        z_rest(15)
+        z_turn(12, 2)
+        z_turn(13, 3)
+        z_turns(14)
+        z_out(10)
+        z_out(11)
         z_out(12)
         z_out(13)
-        z_turns(16)
-        z_turns(17)
-        z_turns(18)
+        z_round(14)
+        z_turns_vector(15)
+        z_rest(14)
+        z_turns_vector(16)
+        z_round(15)
+        z_round(16)
+        z_rest(15)
+        z_rest(16)
         z_turn(14, 0)
         z_turn(15, 4)
-        z_round(16)
-        z_round(17)
-        z_rest(16)
-        z_round(18)
-        z_rest(17)
-        z_rest(18)
         z_turn(16, 5)
-        z_turn(17, 3)
-        z_turn(18, 6)
-        for n in range(14, 19):
+        for n in range(14, 17):
             z_out(n)

@@ -21,7 +21,7 @@ P = 128
 PACK = 4
 BANK = 512
 TWO_PI = 2.0 * math.pi
-ON_VECTOR = (3, 5, 8)
+ON_VECTOR = ()
 
 
 def tile_siren_anchor_field_f4_kernel(tc, x_bytes, x_scale, w, b, freq1, amp, p, c, freq2, out):
@@ -98,7 +98,9 @@ def tile_siren_anchor_field_f4_kernel(tc, x_bytes, x_scale, w, b, freq1, amp, p,
             spread = bank(2 + g, [P, PACK, P])
             for t in range(PACK):
                 nc.tensor.transpose(spread[:, t, :], scale_cols[:, g, t : t + 1].to_broadcast([P, P]), ident[:])
-            nc.scalar.copy(out=scale_rows[:, g], in_=spread[:].rearrange("p t q -> p q t"))
+            for half in range(2):
+                rows = slice(64 * half, 64 * half + 64)
+                nc.scalar.copy(out=scale_rows[:, g, rows], in_=spread[:, :, rows].rearrange("p t q -> p q t"))
 
         vcols = bank(0, [P, 2, P], BF16)
 
@@ -146,16 +148,6 @@ def tile_siren_anchor_field_f4_kernel(tc, x_bytes, x_scale, w, b, freq1, amp, p,
 
         def w_weave_late(n, g):
             nc.gpsimd.tensor_scalar(woven_w(n)[:, g], wraw[n][:, g].rearrange("p t n -> p n t"), 1.0, 0.0, OP.mult, OP.add)
-
-        def w_pass_through(n, number):
-            turned["w", n] = bank(number, [P, 2, BANK], BF16)
-            for g in range(2):
-                nc.tensor.matmul(
-                    turned["w", n][:, g, :], ident_b[:], wraw[n][:, g].rearrange("p t n -> p n t"), start=True, stop=True
-                )
-
-        def w_copy(n):
-            nc.scalar.copy(out=woven_w(n)[:].rearrange("p g n t -> p (g n t)"), in_=turned["w", n][:].rearrange("p g c -> p (g c)"))
 
         def w_quant(n):
             quantize(wq[n][:], wqs[n][:], w_woven[n][:].rearrange("p g n t -> p (g n t)"))
@@ -351,8 +343,8 @@ def tile_siren_anchor_field_f4_kernel(tc, x_bytes, x_scale, w, b, freq1, amp, p,
 
         for g in range(2):
             spread_scales(g)
-        for g in range(2):
-            x_mult(0, slice(BANK * g, BANK * g + BANK))
+        for quarter in range(4):
+            x_mult(0, slice(256 * quarter, 256 * quarter + 256))
         x_turn(0, free_bank())
         w_weave(0, 0)
         w_weave(0, 1)
@@ -401,17 +393,15 @@ def tile_siren_anchor_field_f4_kernel(tc, x_bytes, x_scale, w, b, freq1, amp, p,
         rounding(1, "k1")
         w_weave_late(3, 0)
         x_row(13, 6)
-        w_pass_through(6, 7)
-        w_copy(6)
         y_round(0, "k0")
         y_rest(0)
+        w_weave(6, 0)
         y_mm(2)
-        w_pass_through(7, 4)
         y_sin(0)
         y_turns(2)
         x_row(14, 7)
         x_row(15, 6)
-        w_copy(7)
+        w_weave(6, 1)
         x_quant(4)
         x_quant(5)
         rounding(2, "xw0")
@@ -433,6 +423,7 @@ def tile_siren_anchor_field_f4_kernel(tc, x_bytes, x_scale, w, b, freq1, amp, p,
         p_copy(9)
         y_turns(4, [0])
         p_piece(10, 7)
+        w_weave(7, 0)
         p_quant(1)
         p_quant(2)
         rounding(3, "pw2")
@@ -477,6 +468,8 @@ def tile_siren_anchor_field_f4_kernel(tc, x_bytes, x_scale, w, b, freq1, amp, p,
             h_turn(amp_order[s + 1])
             if s in (0, 1):
                 y_sin(s + 3, [0])
+            if s == 3:
+                w_weave(7, 1)
             if s == 2:
                 y_sin(2)
             if n >= 1:
@@ -490,7 +483,6 @@ def tile_siren_anchor_field_f4_kernel(tc, x_bytes, x_scale, w, b, freq1, amp, p,
             rounding(s + 4, f"k{s % 3}" if n >= 1 else p_slot[s + 4])
 
         y_rest(14, [1])
-        z_turns_vector(8)
         y_sin(14)
         z_round_late(8, "k0")
         z_mm(9, 2)

@@ -39,7 +39,7 @@ def tile_siren_anchor_field_f4_kernel(tc, x_bytes, x_scale, w, b, freq1, amp, p,
 
         x_view = x_bytes.rearrange("(j q t) k -> j q t k", q=P, t=PACK)
         w_view = w.rearrange("(g q t) n -> g q t n", q=P, t=PACK)
-        xb, wraw, praw = {}, {}, {}
+        xb, wraw, wparts, praw = {}, {}, {}, {}
 
         def load_x(j, rows):
             part = buf(f"xb{j}_{rows.start}", [P, len(rows), K], U8)
@@ -47,12 +47,13 @@ def tile_siren_anchor_field_f4_kernel(tc, x_bytes, x_scale, w, b, freq1, amp, p,
             for t in rows:
                 xb[PACK * j + t] = part[:, t - rows.start, :]
 
-        def load_w(tiles):
-            part = buf(f"wraw{tiles.start}", [P, 2, PACK, P * len(tiles)], BF16)
-            for g in range(2):
-                nc.sync.dma_start(out=part[:, g], in_=w_view[g][:, :, P * tiles.start : P * tiles.stop])
-            for i in tiles:
-                wraw[i] = part[:, :, :, P * (i - tiles.start) : P * (i - tiles.start + 1)]
+        def load_w(tiles, g):
+            if g == 0:
+                part = buf(f"wraw{tiles.start}", [P, 2, PACK, P * len(tiles)], BF16)
+                wparts[tiles.start] = part
+                for i in tiles:
+                    wraw[i] = part[:, :, :, P * (i - tiles.start) : P * (i - tiles.start + 1)]
+            nc.sync.dma_start(out=wparts[tiles.start][:, g], in_=w_view[g][:, :, P * tiles.start : P * tiles.stop])
 
         def load_p(row_tiles):
             for rt in row_tiles:
@@ -70,8 +71,9 @@ def tile_siren_anchor_field_f4_kernel(tc, x_bytes, x_scale, w, b, freq1, amp, p,
         scale_cols = keep.tile([P, 2, 2 * PACK], F32, name="scale_cols")
         nc.sync.dma_start(out=scale_cols[:, :, 0:PACK], in_=x_scale.rearrange("o (g q t) -> q (o g) t", q=P, t=PACK))
         load_x(0, range(0, 2))
-        load_w(range(0, 3))
+        load_w(range(0, 4), 0)
         load_x(0, range(2, 4))
+        load_w(range(0, 4), 1)
         load_x(1, range(0, 4))
         vrows = keep.tile([P, 2, P], BF16, name="vrows")
         nc.vector.memset(vrows[:], 0.0)
@@ -83,7 +85,8 @@ def tile_siren_anchor_field_f4_kernel(tc, x_bytes, x_scale, w, b, freq1, amp, p,
         load_p(range(0, 2))
         load_x(2, range(0, 4))
         load_p(range(2, 4))
-        load_w(range(3, 8))
+        load_w(range(4, 8), 0)
+        load_w(range(4, 8), 1)
         load_x(3, range(0, 4))
         load_p(range(4, 8))
 
@@ -133,7 +136,7 @@ def tile_siren_anchor_field_f4_kernel(tc, x_bytes, x_scale, w, b, freq1, amp, p,
             )
 
         w_woven, turned = {}, {}
-        w_slot = {0: "ww0", 1: "ww1", 2: "k1", 3: "ww0", 4: "ww1", 5: "ww2", 6: "ww3", 7: "ww4"}
+        w_slot = {0: "ww0", 1: "ww1", 2: "k1", 3: "ww2", 4: "ww0", 5: "ww1", 6: "ww3", 7: "ww4"}
 
         def woven_w(n):
             if n not in w_woven:
@@ -318,7 +321,7 @@ def tile_siren_anchor_field_f4_kernel(tc, x_bytes, x_scale, w, b, freq1, amp, p,
             for a in range(blocks):
                 nc.tensor.transpose(turned_z[n][:, a, :], u2s[n][:, a * P : (a + 1) * P], ident[:])
 
-        out_slots = ["xw0", "xw1", "praw4", "praw5", "praw6", "praw7", "wraw0", "wraw3"]
+        out_slots = ["xw0", "xw1", "praw4", "praw5", "praw6", "praw7", "wraw0", "wraw4"]
 
         def z_out(n):
             i, r0, width = tasks[n]
@@ -347,15 +350,16 @@ def tile_siren_anchor_field_f4_kernel(tc, x_bytes, x_scale, w, b, freq1, amp, p,
             x_mult(0, slice(256 * quarter, 256 * quarter + 256))
         x_turn(0, free_bank())
         w_weave(0, 0)
-        w_weave(0, 1)
-        x_copy(0)
         w_weave(1, 0)
+        x_copy(0)
+        w_weave(0, 1)
         x_row(1)
         w_weave(1, 1)
         x_row(2)
         w_weave(2, 0)
         x_row(3)
         channel_constants(0)
+        w_weave(2, 1)
         x_row(4)
         p_piece(0)
         x_row(5)
@@ -363,7 +367,8 @@ def tile_siren_anchor_field_f4_kernel(tc, x_bytes, x_scale, w, b, freq1, amp, p,
         x_quant(0)
         x_quant(1)
         w_quant(0)
-        w_weave(2, 1)
+        w_weave(3, 0)
+        w_weave(3, 1)
         y_mm(0, [0])
         x_row(6)
         channel_constants(1)
@@ -371,7 +376,7 @@ def tile_siren_anchor_field_f4_kernel(tc, x_bytes, x_scale, w, b, freq1, amp, p,
         x_row(7)
         w_quant(1)
         p_piece(6)
-        w_weave(5, 0)
+        w_weave(6, 0)
         y_mm(1, [0])
         x_row(8)
         p_piece(1)
@@ -384,24 +389,24 @@ def tile_siren_anchor_field_f4_kernel(tc, x_bytes, x_scale, w, b, freq1, amp, p,
         x_row(10)
         y_turns(1, [1])
         x_row(11)
-        w_weave(5, 1)
+        w_weave(6, 1)
         y_mm(0, [1])
         p_piece(5)
         x_row(12, 4)
         p_piece(7, 5)
         w_quant(2)
         rounding(1, "k1")
-        w_weave_late(3, 0)
+        w_weave_late(4, 0)
         x_row(13, 6)
         y_round(0, "k0")
         y_rest(0)
-        w_weave(6, 0)
+        w_weave(7, 0)
         y_mm(2)
         y_sin(0)
         y_turns(2)
         x_row(14, 7)
         x_row(15, 6)
-        w_weave(6, 1)
+        w_weave(7, 1)
         x_quant(4)
         x_quant(5)
         rounding(2, "xw0")
@@ -423,7 +428,6 @@ def tile_siren_anchor_field_f4_kernel(tc, x_bytes, x_scale, w, b, freq1, amp, p,
         p_copy(9)
         y_turns(4, [0])
         p_piece(10, 7)
-        w_weave(7, 0)
         p_quant(1)
         p_quant(2)
         rounding(3, "pw2")
@@ -439,7 +443,7 @@ def tile_siren_anchor_field_f4_kernel(tc, x_bytes, x_scale, w, b, freq1, amp, p,
             if n >= 1:
                 z_round_late(n - 1, f"k{s % 3}")
             elif s >= 1:
-                w_weave_late(*divmod(s + 6, 2))
+                w_weave_late(*divmod(s + 8, 2))
             y_mm(s + 4, [1])
             if n >= 0:
                 z_mm(n, 6)
@@ -462,14 +466,12 @@ def tile_siren_anchor_field_f4_kernel(tc, x_bytes, x_scale, w, b, freq1, amp, p,
                 p_quant(s + 4)
             if n >= 1:
                 z_rest(n - 1)
-            if s in (1, 3, 5, 7, 9):
+            if s in (0, 2, 4, 6, 8):
                 w_quant(s // 2 + 3)
             h_quant(amp_order[s])
             h_turn(amp_order[s + 1])
             if s in (0, 1):
                 y_sin(s + 3, [0])
-            if s == 3:
-                w_weave(7, 1)
             if s == 2:
                 y_sin(2)
             if n >= 1:

@@ -236,12 +236,8 @@ def tile_siren_anchor_field_f4_kernel(tc, x_bytes, x_scale, w, b, freq1, amp, p,
             nc.gpsimd.tensor_scalar(ks[s][:], us[s][:], 1.0, 0.0, OP.mult, OP.add)
 
         def y_round(s, tag):
-            i = pairs[s][0]
             ks[s] = buf(tag, [P, 2, BANK], I32)
-            for a in range(2):
-                nc.vector.tensor_scalar(
-                    ks[s][:, a, :], ys[s, a][:], turn[:, 0, i : i + 1], turn[:, 1, i : i + 1], OP.mult, OP.add
-                )
+            nc.vector.tensor_copy(out=ks[s][:], in_=us[s][:])
 
         def y_rest(s, units=range(2)):
             i = pairs[s][0]
@@ -372,11 +368,11 @@ def tile_siren_anchor_field_f4_kernel(tc, x_bytes, x_scale, w, b, freq1, amp, p,
         y_mm(0, [0])
         x_row(6)
         channel_constants(1)
-        p_piece(4)
         x_row(7)
+        y_turns(0, [0])
+        p_piece(4)
         w_quant(1)
         p_piece(6)
-        w_weave(6, 0)
         y_mm(1, [0])
         x_row(8)
         p_piece(1)
@@ -384,29 +380,28 @@ def tile_siren_anchor_field_f4_kernel(tc, x_bytes, x_scale, w, b, freq1, amp, p,
         x_row(9)
         x_quant(2)
         x_quant(3)
+        y_mm(0, [1])
+        y_turns(0, [1])
         p_piece(3)
-        y_mm(1, [1])
         x_row(10)
+        y_mm(1, [1])
         y_turns(1, [1])
         x_row(11)
-        w_weave(6, 1)
-        y_mm(0, [1])
         p_piece(5)
         x_row(12, 4)
         p_piece(7, 5)
+        y_round(0, "k0")
         w_quant(2)
         rounding(1, "k1")
-        w_weave_late(4, 0)
         x_row(13, 6)
-        y_round(0, "k0")
         y_rest(0)
-        w_weave(7, 0)
         y_mm(2)
-        y_sin(0)
+        w_weave(6, 0)
         y_turns(2)
         x_row(14, 7)
         x_row(15, 6)
-        w_weave(7, 1)
+        y_sin(0)
+        w_weave(6, 1)
         x_quant(4)
         x_quant(5)
         rounding(2, "xw0")
@@ -428,9 +423,11 @@ def tile_siren_anchor_field_f4_kernel(tc, x_bytes, x_scale, w, b, freq1, amp, p,
         p_copy(9)
         y_turns(4, [0])
         p_piece(10, 7)
+        w_weave(7, 0)
         p_quant(1)
         p_quant(2)
         rounding(3, "pw2")
+        w_weave_late(4, 0)
         p_quant(3)
 
         amp_order = [0, 1, 3, 4, 2] + list(range(5, 16))
@@ -472,6 +469,8 @@ def tile_siren_anchor_field_f4_kernel(tc, x_bytes, x_scale, w, b, freq1, amp, p,
             h_turn(amp_order[s + 1])
             if s in (0, 1):
                 y_sin(s + 3, [0])
+            if s == 3:
+                w_weave(7, 1)
             if s == 2:
                 y_sin(2)
             if n >= 1:

@@ -21,7 +21,11 @@ P = 128
 PACK = 4
 BANK = 512
 TWO_PI = 2.0 * math.pi
-ON_VECTOR = ()
+Y_BANKS = 4
+H_BANK = 4
+Z_BANK = 6
+STEPS = 12
+FIRST_Z = 3
 
 
 def tile_siren_anchor_field_f4_kernel(tc, x_bytes, x_scale, w, b, freq1, amp, p, c, freq2, out):
@@ -121,7 +125,7 @@ def tile_siren_anchor_field_f4_kernel(tc, x_bytes, x_scale, w, b, freq1, amp, p,
             scales = [buf(f"{name}s{a}", [P, width], U8) for a in range(count)]
             return codes, scales
 
-        xq, xqs = operand("xq", 8, BANK)
+        xq, xqs = operand("xq", 4, 2 * BANK)
         wq, wqs = operand("wq", 8, 2 * P)
         pq, pqs = operand("pq", 8, BANK)
         hq, hqs = operand("hq", 16, 2 * P)
@@ -136,7 +140,7 @@ def tile_siren_anchor_field_f4_kernel(tc, x_bytes, x_scale, w, b, freq1, amp, p,
             )
 
         w_woven, turned = {}, {}
-        w_slot = {0: "ww0", 1: "ww1", 2: "k1", 3: "ww2", 4: "ww0", 5: "ww1", 6: "ww3", 7: "ww4"}
+        w_slot = ["ww0", "ww1", "k1", "ww2", "ww0", "ww1", "ww3", "ww4"]
 
         def woven_w(n):
             if n not in w_woven:
@@ -149,7 +153,7 @@ def tile_siren_anchor_field_f4_kernel(tc, x_bytes, x_scale, w, b, freq1, amp, p,
                 in_=wraw[n][:, g].rearrange("p t (a e) -> p a t e", e=4),
             )
 
-        def w_weave_late(n, g):
+        def w_weave_gpsimd(n, g):
             nc.gpsimd.tensor_scalar(woven_w(n)[:, g], wraw[n][:, g].rearrange("p t n -> p n t"), 1.0, 0.0, OP.mult, OP.add)
 
         def w_quant(n):
@@ -182,10 +186,10 @@ def tile_siren_anchor_field_f4_kernel(tc, x_bytes, x_scale, w, b, freq1, amp, p,
                 in_=turned["x", n][:].rearrange("q g u r -> q g r u"),
             )
 
-        def x_quant(n):
-            quantize(xq[n][:], xqs[n][:], x_woven[n // 2][:, n % 2].rearrange("q m t -> q (m t)"))
+        def x_quant(j):
+            quantize(xq[j][:], xqs[j][:], x_woven[j][:].rearrange("q g m t -> q (g m t)"))
 
-        p_slot = ["pw0", "pw1", "pw2", "pw3", "praw0", "praw1", "praw2", "praw3"]
+        p_slot = [f"pw{j}" for j in range(4)] + [f"praw{j}" for j in range(4)]
 
         def p_turn(n, number):
             m, pair = divmod(n, 2)
@@ -208,20 +212,32 @@ def tile_siren_anchor_field_f4_kernel(tc, x_bytes, x_scale, w, b, freq1, amp, p,
         pairs = [(i, cp) for cp in range(2) for i in range(3)]
         pairs.extend((i, cp) for i in range(3, 8) for cp in range(2))
         ys, us, ks, turned_h, h_woven = {}, {}, {}, {}, {}
+        y_bank, h_bank, z_bank, turned_bank = {}, {}, {}, {}
+        released = []
+
+        def release(number):
+            if number in released:
+                released.remove(number)
+            released.append(number)
+
+        def oldest_bank():
+            return released.pop(0)
 
         def turns_tile(s):
             if s not in us:
-                us[s] = buf("u4" if s == 2 else f"u{s % 4}", [P, 2, BANK], F32)
+                us[s] = buf("u_waiting" if s == 2 else f"u{s % 4}", [P, 2, BANK], F32)
             return us[s]
 
         def y_mm(s, units=range(2)):
             i, cp = pairs[s]
             for a in units:
-                ys[s, a] = bank(2 * ((s + 1) % 2) + a, [P, BANK])
+                y_bank[s, a] = 2 * ((s + 1) % 2) + a
+                ys[s, a] = bank(y_bank[s, a], [P, BANK])
                 for g in range(2):
                     cols = slice(P * g, P * g + P)
-                    n = 2 * (2 * cp + a) + g
-                    product(ys[s, a][:], wq[i][:, cols], wqs[i][:, cols], xq[n][:], xqs[n][:], g == 0, g == 1)
+                    rows = slice(BANK * g, BANK * g + BANK)
+                    j = 2 * cp + a
+                    product(ys[s, a][:], wq[i][:, cols], wqs[i][:, cols], xq[j][:, rows], xqs[j][:, rows], g == 0, g == 1)
 
         def y_turns(s, units=range(2)):
             i = pairs[s][0]
@@ -245,15 +261,17 @@ def tile_siren_anchor_field_f4_kernel(tc, x_bytes, x_scale, w, b, freq1, amp, p,
                 nc.vector.scalar_tensor_tensor(
                     turns_tile(s)[:, a, :], ys[s, a][:], turn[:, 0, i : i + 1], ks[s][:, a, :], OP.mult, OP.subtract
                 )
+                release(y_bank[s, a])
 
         def y_sin(s, units=range(2)):
             i = pairs[s][0]
             rest = us[s][:, units[0] : units[-1] + 1, :]
             nc.scalar.activation(out=rest, in_=rest, func=ACT.Sin, scale=TWO_PI, bias=phase1[:, i : i + 1])
 
-        def h_turn(s, first=4):
+        def h_turn(s, banks=(H_BANK, H_BANK + 1)):
             for a in range(2):
-                turned_h[s, a] = bank(first + a, [P, PACK, P])
+                h_bank[s, a] = banks[a]
+                turned_h[s, a] = bank(banks[a], [P, PACK, P])
                 for t in range(PACK):
                     nc.tensor.transpose(turned_h[s, a][:, t, :], us[s][:, a, t * P : (t + 1) * P], ident[:])
 
@@ -267,6 +285,7 @@ def tile_siren_anchor_field_f4_kernel(tc, x_bytes, x_scale, w, b, freq1, amp, p,
                     amp_sb[:, j, :].unsqueeze(1).to_broadcast([P, P, PACK]),
                     OP.mult,
                 )
+                release(h_bank[s, a])
 
         def h_quant(s):
             i, cp = pairs[s]
@@ -279,6 +298,7 @@ def tile_siren_anchor_field_f4_kernel(tc, x_bytes, x_scale, w, b, freq1, amp, p,
 
         def z_mm(n, number):
             i, r0, width = tasks[n]
+            z_bank[n] = number
             zs[n] = bank(number, [P, width])
             queries = slice(r0 % BANK, r0 % BANK + width)
             for j in range(4):
@@ -287,20 +307,17 @@ def tile_siren_anchor_field_f4_kernel(tc, x_bytes, x_scale, w, b, freq1, amp, p,
                 part = 4 * (r0 // BANK) + j
                 product(zs[n][:], hq[m][:, cols], hqs[m][:, cols], pq[part][:, queries], pqs[part][:, queries], j == 0, j == 3)
 
-        def z_turns(n):
+        def z_turns(n, on_vector=False):
             i, r0, width = tasks[n]
-            u2s[n] = buf(f"u2{n % 4}" if n < 12 else f"praw{(n - 12) % 4}" if n >= 16 else f"pw{n - 12}", [P, width], F32)
-            nc.scalar.activation(
-                out=u2s[n][:], in_=zs[n][:], func=ACT.Identity,
-                scale=turn[:, 0, 8 + i : 9 + i], bias=turn[:, 1, 8 + i : 9 + i],
-            )
+            u2s[n] = buf(f"u2{n % 4}" if n < STEPS else p_slot[n - STEPS], [P, width], F32)
+            freq, shift = turn[:, 0, 8 + i : 9 + i], turn[:, 1, 8 + i : 9 + i]
+            if on_vector:
+                nc.vector.tensor_scalar(u2s[n][:], zs[n][:], freq, shift, OP.mult, OP.add)
+            else:
+                nc.scalar.activation(out=u2s[n][:], in_=zs[n][:], func=ACT.Identity, scale=freq, bias=shift)
+            release(z_bank[n])
 
-        def z_turns_vector(n):
-            i, r0, width = tasks[n]
-            u2s[n] = buf(f"u2{n % 4}" if n < 12 else f"praw{(n - 12) % 4}" if n >= 16 else f"pw{n - 12}", [P, width], F32)
-            nc.vector.tensor_scalar(u2s[n][:], zs[n][:], turn[:, 0, 8 + i : 9 + i], turn[:, 1, 8 + i : 9 + i], OP.mult, OP.add)
-
-        def z_round_late(n, tag):
+        def z_round_gpsimd(n, tag):
             k2s[n] = buf(tag, [P, BANK], I32)
             nc.gpsimd.tensor_scalar(k2s[n][:], u2s[n][:], 1.0, 0.0, OP.mult, OP.add)
 
@@ -313,38 +330,43 @@ def tile_siren_anchor_field_f4_kernel(tc, x_bytes, x_scale, w, b, freq1, amp, p,
 
         def z_turn(n, number):
             blocks = tasks[n][2] // P
+            turned_bank[n] = number
             turned_z[n] = bank(number, [P, blocks, P])
             for a in range(blocks):
                 nc.tensor.transpose(turned_z[n][:, a, :], u2s[n][:, a * P : (a + 1) * P], ident[:])
 
-        out_slots = ["xw0", "xw1", "praw4", "praw5", "praw6", "praw7", "wraw0", "wraw4"]
+        out_slots = ["xw0", "xw1"] + [f"praw{rt}" for rt in range(4, 8)] + ["wraw0", "wraw4"]
 
         def z_out(n):
             i, r0, width = tasks[n]
-            o = buf(out_slots[n % 8], [P, width // P, P], F32)
+            o = buf(out_slots[n % len(out_slots)], [P, width // P, P], F32)
             nc.scalar.activation(out=o[:], in_=turned_z[n][:], func=ACT.Sin, scale=TWO_PI)
+            release(turned_bank[n])
             nc.sync.dma_start(out=out[r0 : r0 + width, P * i : P * i + P].rearrange("(a q) n -> q a n", q=P), in_=o[:])
 
-        count = [0]
+        turns_done = []
 
-        def free_bank():
-            count[0] = count[0] + 1
-            return 4 + count[0] % 4
+        def turn_bank():
+            turns_done.append(0)
+            return Y_BANKS + len(turns_done) % 4
 
-        def x_row(n, number=None):
+        def x_row(n):
             x_mult(n)
-            x_turn(n, number or free_bank())
+            x_turn(n, turn_bank())
             x_copy(n)
 
-        def p_piece(n, number=None):
-            p_turn(n, number or free_bank())
+        def p_piece(n):
+            p_turn(n, turn_bank())
             p_copy(n)
+
+        def late_p_turn(n):
+            p_turn(n, Z_BANK + n % 2)
 
         for g in range(2):
             spread_scales(g)
         for quarter in range(4):
             x_mult(0, slice(256 * quarter, 256 * quarter + 256))
-        x_turn(0, free_bank())
+        x_turn(0, turn_bank())
         w_weave(0, 0)
         w_weave(1, 0)
         x_copy(0)
@@ -356,15 +378,14 @@ def tile_siren_anchor_field_f4_kernel(tc, x_bytes, x_scale, w, b, freq1, amp, p,
         x_row(3)
         channel_constants(0)
         w_weave(2, 1)
-        x_row(4)
-        p_piece(0)
-        x_row(5)
-        p_piece(2)
+        for n in (4, 5):
+            x_row(n)
+            p_piece(2 * (n - 4))
         x_quant(0)
-        x_quant(1)
         w_quant(0)
         w_weave(3, 0)
         w_weave(3, 1)
+
         y_mm(0, [0])
         x_row(6)
         channel_constants(1)
@@ -378,43 +399,42 @@ def tile_siren_anchor_field_f4_kernel(tc, x_bytes, x_scale, w, b, freq1, amp, p,
         p_piece(1)
         y_turns(1, [0])
         x_row(9)
-        x_quant(2)
-        x_quant(3)
+        x_quant(1)
         y_mm(0, [1])
         y_turns(0, [1])
         p_piece(3)
         x_row(10)
         y_mm(1, [1])
         y_turns(1, [1])
-        x_row(11)
-        p_piece(5)
-        x_row(12, 4)
-        p_piece(7, 5)
+        for n in (11, 12):
+            x_row(n)
+            p_piece(2 * n - 17)
+
         y_round(0, "k0")
         w_quant(2)
-        rounding(1, "k1")
-        x_row(13, 6)
+        rounding(1, w_slot[2])
+        x_row(13)
         y_rest(0)
         y_mm(2)
         w_weave(6, 0)
         y_turns(2)
-        x_row(14, 7)
-        x_row(15, 6)
+        x_row(14)
+        x_row(15)
         y_sin(0)
         w_weave(6, 1)
-        x_quant(4)
-        x_quant(5)
+
+        x_quant(2)
         rounding(2, "xw0")
         p_quant(0)
         y_rest(1)
-        p_piece(8, 5)
+        p_piece(8)
         y_mm(3, [0])
         y_sin(1, [0])
         y_turns(3, [0])
         y_sin(1, [1])
-        p_turn(9, 6)
-        x_quant(6)
-        x_quant(7)
+        late_p_turn(9)
+
+        x_quant(3)
         y_rest(2, [0])
         y_mm(3, [1])
         y_mm(4, [0])
@@ -422,130 +442,132 @@ def tile_siren_anchor_field_f4_kernel(tc, x_bytes, x_scale, w, b, freq1, amp, p,
         y_turns(3, [1])
         p_copy(9)
         y_turns(4, [0])
-        p_piece(10, 7)
+        late_p_turn(10)
+        p_copy(10)
         w_weave(7, 0)
         p_quant(1)
         p_quant(2)
-        rounding(3, "pw2")
-        w_weave_late(4, 0)
+        rounding(3, p_slot[2])
+        w_weave_gpsimd(4, 0)
         p_quant(3)
 
         amp_order = [0, 1, 3, 4, 2] + list(range(5, 16))
-        first_z = 3
-        for s in range(12):
-            n = s - first_z
+        for s in range(STEPS):
+            n = s - FIRST_Z
+            overtaking = s in (1, 2)
             y_rest(s + 2, [1])
-            if n - 1 in ON_VECTOR:
-                z_turns_vector(n - 1)
             if n >= 1:
-                z_round_late(n - 1, f"k{s % 3}")
+                z_round_gpsimd(n - 1, f"k{s % 3}")
             elif s >= 1:
-                w_weave_late(*divmod(s + 8, 2))
+                w_weave_gpsimd(*divmod(s + 8, 2))
             y_mm(s + 4, [1])
             if n >= 0:
-                z_mm(n, 6)
+                z_mm(n, Z_BANK)
             else:
-                p_turn(2 * s + 11, (6, 6, 7)[s])
-            if s in (1, 2):
+                late_p_turn(2 * s + 11)
+            if overtaking:
                 y_sin(s + 2, [1])
             y_turns(s + 4, [1])
-            if s in (1, 2):
+            if overtaking:
                 p_copy(2 * s + 10)
-            if n < 0:
-                p_copy(2 * s + 11)
-            else:
-                if n not in ON_VECTOR:
-                    z_turns(n)
-                y_sin(s + 2)
             h_amp(amp_order[s])
             y_rest(s + 3, [0])
-            if n < 1:
-                p_quant(s + 4)
+            if n >= 0:
+                z_turns(n)
+                y_sin(s + 2)
+            else:
+                p_copy(2 * s + 11)
             if n >= 1:
                 z_rest(n - 1)
-            if s in (0, 2, 4, 6, 8):
+            else:
+                p_quant(s + 4)
+            if s % 2 == 0 and s // 2 + 3 < 8:
                 w_quant(s // 2 + 3)
             h_quant(amp_order[s])
             h_turn(amp_order[s + 1])
-            if s in (0, 1):
+            if s < 2:
                 y_sin(s + 3, [0])
-            if s == 3:
-                w_weave(7, 1)
-            if s == 2:
+            elif s == 2:
                 y_sin(2)
+            elif s == FIRST_Z:
+                w_weave(7, 1)
             if n >= 1:
-                z_turn(n - 1, 7)
+                z_turn(n - 1, Z_BANK + 1)
                 z_out(n - 1)
-            if s < 11:
+            if s + 5 < len(pairs):
                 y_mm(s + 5, [0])
                 y_turns(s + 5, [0])
             if s < 2:
-                p_turn(2 * s + 12, 7 - s)
+                late_p_turn(2 * s + 12)
             rounding(s + 4, f"k{s % 3}" if n >= 1 else p_slot[s + 4])
+
+        held = [y_bank[14, 1], y_bank[15, 0], y_bank[15, 1], h_bank[12, 0], h_bank[12, 1]]
+        for number in held:
+            released.remove(number)
+
+        def two_banks():
+            return (oldest_bank(), oldest_bank())
 
         y_rest(14, [1])
         y_sin(14)
-        z_round_late(8, "k0")
-        z_mm(9, 2)
-        h_turn(13, 6)
+        z_round_gpsimd(8, "k0")
+        z_mm(9, oldest_bank())
+        h_turn(13, two_banks())
         h_amp(12)
         y_rest(15)
         z_turns(9)
         y_sin(15)
-        z_mm(10, 3)
-        z_mm(11, 0)
+        for n in (10, 11):
+            z_mm(n, oldest_bank())
         h_quant(12)
         z_rest(8)
-        z_round_late(9, "k0")
+        z_round_gpsimd(9, "k0")
         h_amp(13)
         z_rest(9)
-        h_turn(14)
-        h_turn(15, 1)
-        z_turn(8, 7)
-        z_turns(10)
-        z_turns(11)
-        z_turn(9, 6)
-        z_out(8)
-        z_out(9)
+        for s in (14, 15):
+            h_turn(s, two_banks())
+        z_turn(8, oldest_bank())
+        for n in (10, 11):
+            z_turns(n)
+        z_turn(9, oldest_bank())
+        for n in (8, 9):
+            z_out(n)
+
         h_quant(13)
-        z_round_late(10, "hw1")
-        z_round_late(11, "k1")
-        z_mm(12, 3)
-        z_mm(13, 0)
+        z_round_gpsimd(10, "hw1")
+        z_round_gpsimd(11, "k1")
+        for n in (12, 13):
+            z_mm(n, oldest_bank())
         h_amp(14)
         h_amp(15, "k2")
-        h_quant(14)
-        h_quant(15)
-        z_rest(10)
-        z_rest(11)
-        z_turns(12)
-        z_turns(13)
-        z_mm(14, 4)
-        z_turn(10, 7)
-        z_turn(11, 6)
-        z_mm(15, 5)
-        z_mm(16, 1)
-        z_round(12)
-        z_round(13)
-        z_rest(12)
-        z_rest(13)
-        z_turn(12, 2)
-        z_turn(13, 3)
+        for s in (14, 15):
+            h_quant(s)
+        for n in (10, 11):
+            z_rest(n)
+        for n in (12, 13):
+            z_turns(n)
+        z_mm(14, oldest_bank())
+        for n in (10, 11):
+            z_turn(n, oldest_bank())
+        for n in (15, 16):
+            z_mm(n, oldest_bank())
+        for stage in (z_round, z_rest):
+            for n in (12, 13):
+                stage(n)
+        for n in (12, 13):
+            z_turn(n, oldest_bank())
         z_turns(14)
-        z_out(10)
-        z_out(11)
-        z_out(12)
-        z_out(13)
+        for n in range(10, 14):
+            z_out(n)
+
         z_round(14)
-        z_turns_vector(15)
+        z_turns(15, on_vector=True)
         z_rest(14)
-        z_turns_vector(16)
-        z_round(15)
-        z_round(16)
-        z_rest(15)
-        z_rest(16)
-        z_turn(14, 0)
-        z_turn(15, 4)
-        z_turn(16, 5)
+        z_turns(16, on_vector=True)
+        for stage in (z_round, z_rest):
+            for n in (15, 16):
+                stage(n)
+        for n in range(14, 17):
+            z_turn(n, oldest_bank())
         for n in range(14, 17):
             z_out(n)

@@ -35,8 +35,8 @@ def tile_siren_anchor_field_f4_kernel(tc, x_bytes, x_scale, w, b, freq1, amp, p,
         psum = ctx.enter_context(tc.psum_pool(name="psum", bufs=1))
         ctx.enter_context(tc.manual_schedule())
 
-        def buf(tag, shape, dtype):
-            return keep.tile(shape, dtype, name=tag, tag=tag, align_bytes=64)
+        def buf(tag, shape, dtype, align=64):
+            return keep.tile(shape, dtype, name=tag, tag=tag, align_bytes=align)
 
         def bank(number, shape, dtype=F32):
             return psum.tile(shape, dtype, name=f"bank{number}", tag=f"bank{number}")
@@ -121,7 +121,7 @@ def tile_siren_anchor_field_f4_kernel(tc, x_bytes, x_scale, w, b, freq1, amp, p,
                 nc.scalar.activation(out=phase1[:], in_=turn[:, 1, 0:8], func=ACT.Copy, scale=TWO_PI)
 
         def operand(name, count, width):
-            codes = [buf(f"{name}c{a}", [P, width], U32) for a in range(count)]
+            codes = [buf(f"{name}c{a}", [P, width], U32, 256 if a == 0 else 64) for a in range(count)]
             scales = [buf(f"{name}s{a}", [P, width], U8) for a in range(count)]
             return codes, scales
 

from contextlib import ExitStack
import math

import concourse.mybir as mybir
from concourse.masks import make_identity

M, K, N, R = 2048, 1024, 1024, 1024
FLOPS = 2 * M * K * N + 2 * R * M * N

F32 = mybir.dt.float32
BF16 = mybir.dt.bfloat16
I32 = mybir.dt.int32
U32 = mybir.dt.uint32
U8 = mybir.dt.uint8
FP8 = mybir.dt.float8_e4m3fn
FP8X4 = mybir.dt.float8_e4m3fn_x4
ACT = mybir.ActivationFunctionType
OP = mybir.AluOpType

P = 128
PACK = 4
BANK = 512
TWO_PI = 2.0 * math.pi
Y_BANKS = 4
H_BANK = 4
Z_BANK = 6
STEPS = 12
FIRST_Z = 3


def tile_siren_anchor_field_f4_kernel(tc, x_bytes, x_scale, w, b, freq1, amp, p, c, freq2, out):
    nc = tc.nc
    with ExitStack() as ctx:
        keep = ctx.enter_context(tc.tile_pool(name="keep", bufs=1))
        psum = ctx.enter_context(tc.psum_pool(name="psum", bufs=1))
        ctx.enter_context(tc.manual_schedule())

        def buf(tag, shape, dtype, align=64):
            return keep.tile(shape, dtype, name=tag, tag=tag, align_bytes=align)

        def bank(number, shape, dtype=F32):
            return psum.tile(shape, dtype, name=f"bank{number}", tag=f"bank{number}")

        x_view = x_bytes.rearrange("(j q t) k -> j q t k", q=P, t=PACK)
        w_view = w.rearrange("(g q t) n -> g q t n", q=P, t=PACK)
        xb, wraw, wparts, praw = {}, {}, {}, {}

        def load_x(j, rows):
            part = buf(f"xb{j}_{rows.start}", [P, len(rows), K], U8)
            nc.sync.dma_start(out=part[:], in_=x_view[j][:, rows.start : rows.stop, :])
            for t in rows:
                xb[PACK * j + t] = part[:, t - rows.start, :]

        def load_w(tiles, g):
            if g == 0:
                part = buf(f"wraw{tiles.start}", [P, 2, PACK, P * len(tiles)], BF16)
                wparts[tiles.start] = part
                for i in tiles:
                    wraw[i] = part[:, :, :, P * (i - tiles.start) : P * (i - tiles.start + 1)]
            nc.sync.dma_start(out=wparts[tiles.start][:, g], in_=w_view[g][:, :, P * tiles.start : P * tiles.stop])

        def load_p(row_tiles):
            for rt in row_tiles:
                praw[rt] = buf(f"praw{rt}", [P, M], BF16)
                nc.sync.dma_start(out=praw[rt][:], in_=p[rt * P : (rt + 1) * P, :])

        warm = keep.tile([P, 1], F32, name="warm")
        nc.vector.memset(warm[:], 0.0)
        nc.scalar.activation(out=warm[:], in_=warm[:], func=ACT.Sin)

        ident = keep.tile([P, P], F32, name="ident")
        nc.vector.memset(ident[:], 0.0)
        make_identity(nc, ident[:], nomemset=True)

        scale_cols = keep.tile([P, 2, 2 * PACK], F32, name="scale_cols")
        nc.sync.dma_start(out=scale_cols[:, :, 0:PACK], in_=x_scale.rearrange("o (g q t) -> q (o g) t", q=P, t=PACK))
        load_x(0, range(0, 2))
        load_w(range(0, 4), 0)
        load_x(0, range(2, 4))
        load_w(range(0, 4), 1)
        load_x(1, range(0, 4))
        vrows = keep.tile([P, 2, P], BF16, name="vrows")
        nc.vector.memset(vrows[:], 0.0)
        for layer, (freq, bias) in enumerate(((freq1, b), (freq2, c))):
            nc.sync.dma_start(out=vrows[8 * layer : 8 * layer + 8, 0, :], in_=freq.rearrange("(i q) -> i q", q=P))
            nc.sync.dma_start(out=vrows[8 * layer : 8 * layer + 8, 1, :], in_=bias.rearrange("(i q) -> i q", q=P))
        amp_sb = keep.tile([P, 4, PACK], BF16, name="amp_sb")
        nc.sync.dma_start(out=amp_sb[:], in_=amp.rearrange("(j q t) -> q j t", q=P, t=PACK))
        load_p(range(0, 2))
        load_x(2, range(0, 4))
        load_p(range(2, 4))
        load_w(range(4, 8), 0)
        load_w(range(4, 8), 1)
        load_x(3, range(0, 4))
        load_p(range(4, 8))

        ident_b = keep.tile([P, P], BF16, name="ident_b")
        nc.vector.tensor_copy(out=ident_b[:], in_=ident[:])

        turn = keep.tile([P, 2, 16], F32, name="turn")
        phase1 = keep.tile([P, 8], F32, name="phase1")
        scale_rows = buf("scale_rows", [P, 2, P, PACK], F32)

        def spread_scales(g):
            spread = bank(2 + g, [P, PACK, P])
            for t in range(PACK):
                nc.tensor.transpose(spread[:, t, :], scale_cols[:, g, t : t + 1].to_broadcast([P, P]), ident[:])
            for half in range(2):
                rows = slice(64 * half, 64 * half + 64)
                nc.scalar.copy(out=scale_rows[:, g, rows], in_=spread[:, :, rows].rearrange("p t q -> p q t"))

        vcols = bank(0, [P, 2, P], BF16)

        def channel_constants(part):
            if part == 0:
                for slot in range(2):
                    nc.tensor.transpose(vcols[:, slot, :], vrows[:, slot, :], ident_b[:])
                nc.scalar.activation(out=turn[:, 0, :], in_=vcols[:, 0, 0:16], func=ACT.Copy, scale=1.0 / TWO_PI)
            else:
                nc.vector.tensor_tensor(turn[:, 1, :], vcols[:, 1, 0:16], turn[:, 0, :], OP.mult)
                nc.scalar.activation(out=phase1[:], in_=turn[:, 1, 0:8], func=ACT.Copy, scale=TWO_PI)

        def operand(name, count, width):
            codes = [buf(f"{name}c{a}", [P, width], U32, 256 if a == 0 else 64) for a in range(count)]
            scales = [buf(f"{name}s{a}", [P, width], U8) for a in range(count)]
            return codes, scales

        xq, xqs = operand("xq", 4, 2 * BANK)
        wq, wqs = operand("wq", 8, 2 * P)
        pq, pqs = operand("pq", 8, BANK)
        hq, hqs = operand("hq", 16, 2 * P)

        def quantize(codes, scales, woven):
            nc.vector.quantize_mx(out=codes.bitcast(FP8X4), scales=scales, in_=woven)

        def product(dst, lhs, lhs_scale, rhs, rhs_scale, first, last):
            nc.tensor.matmul_mx(
                out=dst, lhsT=lhs.bitcast(FP8X4), lhsT_scale=lhs_scale, rhs=rhs.bitcast(FP8X4), rhs_scale=rhs_scale,
                start=first, stop=last,
            )

        w_woven, turned = {}, {}
        w_slot = ["ww0", "ww1", "k1", "ww2", "ww0", "ww1", "ww3", "ww4"]

        def woven_w(n):
            if n not in w_woven:
                w_woven[n] = buf(w_slot[n], [P, 2, P, PACK], BF16)
            return w_woven[n]

        def w_weave(n, g):
            nc.scalar.copy(
                out=woven_w(n)[:, g].rearrange("p (a e) t -> p a t e", e=4),
                in_=wraw[n][:, g].rearrange("p t (a e) -> p a t e", e=4),
            )

        def w_weave_gpsimd(n, g):
            nc.gpsimd.tensor_scalar(woven_w(n)[:, g], wraw[n][:, g].rearrange("p t n -> p n t"), 1.0, 0.0, OP.mult, OP.add)

        def w_quant(n):
            quantize(wq[n][:], wqs[n][:], w_woven[n][:].rearrange("p g n t -> p (g n t)"))

        xs, x_woven, p_woven = {}, {}, {}

        def x_mult(n, cols=slice(0, K)):
            if n not in xs:
                xs[n] = buf(f"xs{n % 3}", [P, K], BF16)
            nc.vector.tensor_tensor(
                xs[n][:, cols], xb[n][:, cols].bitcast(FP8), scale_rows[:].rearrange("p g q t -> p (g q t)")[:, cols], OP.mult
            )

        def turn_pass(dst, words, g):
            for u in range(2):
                nc.tensor.transpose(dst[:, u, :], words[:, 256 * g + u : 256 * (g + 1) : 2], ident[:])

        def x_turn(n, number):
            turned["x", n] = bank(number, [P, 2, 2, P])
            for g in range(2):
                turn_pass(turned["x", n][:, g], xs[n][:].bitcast(F32), g)

        def x_copy(n):
            j, t = divmod(n, 4)
            if t == 0:
                x_woven[j] = buf(f"xw{j % 2}", [P, 2, BANK, PACK], BF16)
            nc.scalar.copy(
                out=x_woven[j][:].bitcast(F32)[:, :, t * P : (t + 1) * P, :],
                in_=turned["x", n][:].rearrange("q g u r -> q g r u"),
            )

        def x_quant(j):
            quantize(xq[j][:], xqs[j][:], x_woven[j][:].rearrange("q g m t -> q (g m t)"))

        p_slot = [f"pw{j}" for j in range(4)] + [f"praw{j}" for j in range(4)]

        def p_turn(n, number):
            m, pair = divmod(n, 2)
            turned["p", n] = bank(number, [P, 2, 2, P])
            for a in range(2):
                turn_pass(turned["p", n][:, a], praw[4 * (m // 4) + 2 * pair + a][:].bitcast(F32), m % 4)

        def p_copy(n):
            m, pair = divmod(n, 2)
            if pair == 0:
                p_woven[m] = buf(p_slot[m], [P, M], BF16)
            nc.scalar.copy(
                out=p_woven[m][:, 1024 * pair : 1024 * pair + 1024].bitcast(F32).rearrange("q (a r u) -> q a r u", a=2, u=2),
                in_=turned["p", n][:].rearrange("q a u r -> q a r u"),
            )

        def p_quant(m):
            quantize(pq[m][:], pqs[m][:], p_woven[m][:])

        pairs = [(i, cp) for cp in range(2) for i in range(3)]
        pairs.extend((i, cp) for i in range(3, 8) for cp in range(2))
        ys, us, ks, turned_h, h_woven = {}, {}, {}, {}, {}
        y_bank, h_bank, z_bank, turned_bank = {}, {}, {}, {}
        released = []

        def release(number):
            if number in released:
                released.remove(number)
            released.append(number)

        def oldest_bank():
            return released.pop(0)

        def turns_tile(s):
            if s not in us:
                us[s] = buf("u_waiting" if s == 2 else f"u{s % 4}", [P, 2, BANK], F32)
            return us[s]

        def y_mm(s, units=range(2)):
            i, cp = pairs[s]
            for a in units:
                y_bank[s, a] = 2 * ((s + 1) % 2) + a
                ys[s, a] = bank(y_bank[s, a], [P, BANK])
                for g in range(2):
                    cols = slice(P * g, P * g + P)
                    rows = slice(BANK * g, BANK * g + BANK)
                    j = 2 * cp + a
                    product(ys[s, a][:], wq[i][:, cols], wqs[i][:, cols], xq[j][:, rows], xqs[j][:, rows], g == 0, g == 1)

        def y_turns(s, units=range(2)):
            i = pairs[s][0]
            for a in units:
                nc.scalar.activation(
                    out=turns_tile(s)[:, a, :], in_=ys[s, a][:], func=ACT.Identity,
                    scale=turn[:, 0, i : i + 1], bias=turn[:, 1, i : i + 1],
                )

        def rounding(s, tag):
            ks[s] = buf(tag, [P, 2, BANK], I32)
            nc.gpsimd.tensor_scalar(ks[s][:], us[s][:], 1.0, 0.0, OP.mult, OP.add)

        def y_round(s, tag):
            ks[s] = buf(tag, [P, 2, BANK], I32)
            nc.vector.tensor_copy(out=ks[s][:], in_=us[s][:])

        def y_rest(s, units=range(2)):
            i = pairs[s][0]
            for a in units:
                nc.vector.scalar_tensor_tensor(
                    turns_tile(s)[:, a, :], ys[s, a][:], turn[:, 0, i : i + 1], ks[s][:, a, :], OP.mult, OP.subtract
                )
                release(y_bank[s, a])

        def y_sin(s, units=range(2)):
            i = pairs[s][0]
            rest = us[s][:, units[0] : units[-1] + 1, :]
            nc.scalar.activation(out=rest, in_=rest, func=ACT.Sin, scale=TWO_PI, bias=phase1[:, i : i + 1])

        def h_turn(s, banks=(H_BANK, H_BANK + 1)):
            for a in range(2):
                h_bank[s, a] = banks[a]
                turned_h[s, a] = bank(banks[a], [P, PACK, P])
                for t in range(PACK):
                    nc.tensor.transpose(turned_h[s, a][:, t, :], us[s][:, a, t * P : (t + 1) * P], ident[:])

        def h_amp(s, tag=None):
            h_woven[s] = buf(tag or f"hw{s % 2}", [P, 2, P, PACK], BF16)
            for a in range(2):
                j = 2 * pairs[s][1] + a
                nc.vector.tensor_tensor(
                    h_woven[s][:, a],
                    turned_h[s, a][:].rearrange("q t n -> q n t"),
                    amp_sb[:, j, :].unsqueeze(1).to_broadcast([P, P, PACK]),
                    OP.mult,
                )
                release(h_bank[s, a])

        def h_quant(s):
            i, cp = pairs[s]
            quantize(hq[2 * i + cp][:], hqs[2 * i + cp][:], h_woven[s][:].rearrange("q a n t -> q (a n t)"))

        tasks = [(i, r0, BANK) for r0 in (0, BANK) for i in range(2)]
        tasks.extend((i, r0, BANK) for i in range(2, 8) for r0 in (0, BANK))
        tasks[15:] = [(7, 512, 256), (7, 768, 256)]
        zs, u2s, k2s, turned_z = {}, {}, {}, {}

        def z_mm(n, number):
            i, r0, width = tasks[n]
            z_bank[n] = number
            zs[n] = bank(number, [P, width])
            queries = slice(r0 % BANK, r0 % BANK + width)
            for j in range(4):
                cols = slice(P * (j % 2), P * (j % 2) + P)
                m = 2 * i + j // 2
                part = 4 * (r0 // BANK) + j
                product(zs[n][:], hq[m][:, cols], hqs[m][:, cols], pq[part][:, queries], pqs[part][:, queries], j == 0, j == 3)

        def z_turns(n, on_vector=False):
            i, r0, width = tasks[n]
            u2s[n] = buf(f"u2{n % 4}" if n < STEPS else p_slot[n - STEPS], [P, width], F32)
            freq, shift = turn[:, 0, 8 + i : 9 + i], turn[:, 1, 8 + i : 9 + i]
            if on_vector:
                nc.vector.tensor_scalar(u2s[n][:], zs[n][:], freq, shift, OP.mult, OP.add)
            else:
                nc.scalar.activation(out=u2s[n][:], in_=zs[n][:], func=ACT.Identity, scale=freq, bias=shift)
            release(z_bank[n])

        def z_round_gpsimd(n, tag):
            k2s[n] = buf(tag, [P, BANK], I32)
            nc.gpsimd.tensor_scalar(k2s[n][:], u2s[n][:], 1.0, 0.0, OP.mult, OP.add)

        def z_round(n):
            k2s[n] = buf(f"xs{n % 3}", [P, tasks[n][2]], I32)
            nc.vector.tensor_copy(out=k2s[n][:], in_=u2s[n][:])

        def z_rest(n):
            nc.vector.tensor_tensor(u2s[n][:], u2s[n][:], k2s[n][:], OP.subtract)

        def z_turn(n, number):
            blocks = tasks[n][2] // P
            turned_bank[n] = number
            turned_z[n] = bank(number, [P, blocks, P])
            for a in range(blocks):
                nc.tensor.transpose(turned_z[n][:, a, :], u2s[n][:, a * P : (a + 1) * P], ident[:])

        out_slots = ["xw0", "xw1"] + [f"praw{rt}" for rt in range(4, 8)] + ["wraw0", "wraw4"]

        def z_out(n):
            i, r0, width = tasks[n]
            o = buf(out_slots[n % len(out_slots)], [P, width // P, P], F32)
            nc.scalar.activation(out=o[:], in_=turned_z[n][:], func=ACT.Sin, scale=TWO_PI)
            release(turned_bank[n])
            nc.sync.dma_start(out=out[r0 : r0 + width, P * i : P * i + P].rearrange("(a q) n -> q a n", q=P), in_=o[:])

        turns_done = []

        def turn_bank():
            turns_done.append(0)
            return Y_BANKS + len(turns_done) % 4

        def x_row(n):
            x_mult(n)
            x_turn(n, turn_bank())
            x_copy(n)

        def p_piece(n):
            p_turn(n, turn_bank())
            p_copy(n)

        def late_p_turn(n):
            p_turn(n, Z_BANK + n % 2)

        for g in range(2):
            spread_scales(g)
        for quarter in range(4):
            x_mult(0, slice(256 * quarter, 256 * quarter + 256))
        x_turn(0, turn_bank())
        w_weave(0, 0)
        w_weave(1, 0)
        x_copy(0)
        w_weave(0, 1)
        x_row(1)
        w_weave(1, 1)
        x_row(2)
        w_weave(2, 0)
        x_row(3)
        channel_constants(0)
        w_weave(2, 1)
        for n in (4, 5):
            x_row(n)
            p_piece(2 * (n - 4))
        x_quant(0)
        w_quant(0)
        w_weave(3, 0)
        w_weave(3, 1)

        y_mm(0, [0])
        x_row(6)
        channel_constants(1)
        x_row(7)
        y_turns(0, [0])
        p_piece(4)
        w_quant(1)
        p_piece(6)
        y_mm(1, [0])
        x_row(8)
        p_piece(1)
        y_turns(1, [0])
        x_row(9)
        x_quant(1)
        y_mm(0, [1])
        y_turns(0, [1])
        p_piece(3)
        x_row(10)
        y_mm(1, [1])
        y_turns(1, [1])
        for n in (11, 12):
            x_row(n)
            p_piece(2 * n - 17)

        y_round(0, "k0")
        w_quant(2)
        rounding(1, w_slot[2])
        x_row(13)
        y_rest(0)
        y_mm(2)
        w_weave(6, 0)
        y_turns(2)
        x_row(14)
        x_row(15)
        y_sin(0)
        w_weave(6, 1)

        x_quant(2)
        rounding(2, "xw0")
        p_quant(0)
        y_rest(1)
        p_piece(8)
        y_mm(3, [0])
        y_sin(1, [0])
        y_turns(3, [0])
        y_sin(1, [1])
        late_p_turn(9)

        x_quant(3)
        y_rest(2, [0])
        y_mm(3, [1])
        y_mm(4, [0])
        h_turn(0)
        y_turns(3, [1])
        p_copy(9)
        y_turns(4, [0])
        late_p_turn(10)
        p_copy(10)
        w_weave(7, 0)
        p_quant(1)
        p_quant(2)
        rounding(3, p_slot[2])
        w_weave_gpsimd(4, 0)
        p_quant(3)

        amp_order = [0, 1, 3, 4, 2] + list(range(5, 16))
        for s in range(STEPS):
            n = s - FIRST_Z
            overtaking = s in (1, 2)
            y_rest(s + 2, [1])
            if n >= 1:
                z_round_gpsimd(n - 1, f"k{s % 3}")
            elif s >= 1:
                w_weave_gpsimd(*divmod(s + 8, 2))
            y_mm(s + 4, [1])
            if n >= 0:
                z_mm(n, Z_BANK)
            else:
                late_p_turn(2 * s + 11)
            if overtaking:
                y_sin(s + 2, [1])
            y_turns(s + 4, [1])
            if overtaking:
                p_copy(2 * s + 10)
            h_amp(amp_order[s])
            y_rest(s + 3, [0])
            if n >= 0:
                z_turns(n)
                y_sin(s + 2)
            else:
                p_copy(2 * s + 11)
            if n >= 1:
                z_rest(n - 1)
            else:
                p_quant(s + 4)
            if s % 2 == 0 and s // 2 + 3 < 8:
                w_quant(s // 2 + 3)
            h_quant(amp_order[s])
            h_turn(amp_order[s + 1])
            if s < 2:
                y_sin(s + 3, [0])
            elif s == 2:
                y_sin(2)
            elif s == FIRST_Z:
                w_weave(7, 1)
            if n >= 1:
                z_turn(n - 1, Z_BANK + 1)
                z_out(n - 1)
            if s + 5 < len(pairs):
                y_mm(s + 5, [0])
                y_turns(s + 5, [0])
            if s < 2:
                late_p_turn(2 * s + 12)
            rounding(s + 4, f"k{s % 3}" if n >= 1 else p_slot[s + 4])

        held = [y_bank[14, 1], y_bank[15, 0], y_bank[15, 1], h_bank[12, 0], h_bank[12, 1]]
        for number in held:
            released.remove(number)

        def two_banks():
            return (oldest_bank(), oldest_bank())

        y_rest(14, [1])
        y_sin(14)
        z_round_gpsimd(8, "k0")
        z_mm(9, oldest_bank())
        h_turn(13, two_banks())
        h_amp(12)
        y_rest(15)
        z_turns(9)
        y_sin(15)
        for n in (10, 11):
            z_mm(n, oldest_bank())
        h_quant(12)
        z_rest(8)
        z_round_gpsimd(9, "k0")
        h_amp(13)
        z_rest(9)
        for s in (14, 15):
            h_turn(s, two_banks())
        z_turn(8, oldest_bank())
        for n in (10, 11):
            z_turns(n)
        z_turn(9, oldest_bank())
        for n in (8, 9):
            z_out(n)

        h_quant(13)
        z_round_gpsimd(10, "hw1")
        z_round_gpsimd(11, "k1")
        for n in (12, 13):
            z_mm(n, oldest_bank())
        h_amp(14)
        h_amp(15, "k2")
        for s in (14, 15):
            h_quant(s)
        for n in (10, 11):
            z_rest(n)
        for n in (12, 13):
            z_turns(n)
        z_mm(14, oldest_bank())
        for n in (10, 11):
            z_turn(n, oldest_bank())
        for n in (15, 16):
            z_mm(n, oldest_bank())
        for stage in (z_round, z_rest):
            for n in (12, 13):
                stage(n)
        for n in (12, 13):
            z_turn(n, oldest_bank())
        z_turns(14)
        for n in range(10, 14):
            z_out(n)

        z_round(14)
        z_turns(15, on_vector=True)
        z_rest(14)
        z_turns(16, on_vector=True)
        for stage in (z_round, z_rest):
            for n in (15, 16):
                stage(n)
        for n in range(14, 17):
            z_turn(n, oldest_bank())
        for n in range(14, 17):
            z_out(n)
